import numpy as np, ml_dtypes
CORES = [3,7,11,15,131,135,139,143]
N = 8
BF = ml_dtypes.bfloat16
def gentries(a):
    return np.ascontiguousarray(a.reshape(8, 16, -1).transpose(0, 2, 1)).reshape(8, -1)
def gtable(e):
    e = np.asarray(e); return np.ascontiguousarray(e.reshape(8, -1, 16).transpose(0, 2, 1)).reshape(128, -1).astype(np.int32)
V, R, M, RO, P, H, CAP, NEED = 4096, 1280, 2, 2, 4, 3, 96, 9
S, TOP = V // N, 2 ** 20 - 1
def parts(rng):
    base = rng.integers(0, 2 ** 20, (1, 8, 16, 1)); amp = np.exp2(10 + 7 * rng.random((N, 8, 1, R)))
    x = np.clip(base + amp * rng.standard_normal((N, 8, 16, R)), 0, TOP).astype(np.int64)
    t = (np.exp2(14 + 3.5 * rng.random((N, 8, 1, 1))) * (0.5 + rng.random((N, 8, 16, 1)))).astype(np.int64)
    lv = rng.integers(0, V, (N, 8, P, R)); lv = np.where(rng.random((N, 8, 1, R)) < 0.5, np.sort(lv, axis=2), lv)
    cd = rng.integers(0, R, (N, 8, RO, M, V))
    return x, t, lv, cd
def pack(x, t, lv, cd):
    return {"px": np.ascontiguousarray(x.reshape(N, 128, R)).astype(np.int32), "th": np.ascontiguousarray(t.reshape(N, 128, 1)).astype(np.int32),
            "ray": np.stack([gtable(a.reshape(8, -1)) for a in lv]), "cand": np.stack([gtable(a.reshape(8, -1)) for a in cd])}
def setup_inputs(rng):
    return pack(*parts(rng))
def setup_inputs_room(rng):
    x, t, lv, cd = parts(rng); h = R // 8
    t = rng.integers(2 ** 14, 2 ** 15, (N, 8, 16, 1)); x = rng.integers(2 ** 18, 2 ** 19, (1, 8, 16, 1)) + rng.integers(0, 2 ** 13, (N, 8, 16, R))
    inc = np.zeros((8, V), bool); own = np.arange(V) // S
    for o in range(N):
        for g in range(8):
            n = int(rng.choice(np.array([0, 1, CAP - 1, CAP, CAP + 1, S]))); last = o == N - 1 and g < 4
            if o == 0: n = (CAP, CAP + 1, S, CAP - 1, 1, 0, CAP, CAP + 1)[g]
            if last: n = (CAP, 1, CAP - 1, CAP)[g]
            s = rng.permutation(S)[:n]
            if last and not np.any(s == S - 1): s[0] = S - 1
            inc[g, o * S + s] = True
    for a in range(N):
        for g in range(8):
            o = rng.permutation(R); hot, watch, calm = o[:h], o[h:2 * h], o[h:]
            m = np.argsort(rng.random((16, h)), axis=0) < rng.integers(NEED, 17, h)
            x[a, g][:, hot] += m * (rng.choice(np.array([-1, 1]), h) * rng.integers(2 ** 16, 2 ** 17, h))
            lv[a, g, 0, o[:2 * h]] = V - 1; cd[a, g, 0] = rng.choice(calm, (M, V))
            for who, back in ((hot, 1), (watch, 2)):
                v = np.flatnonzero(inc[g] & ((own + back) % N == a))
                cd[a, g, 0, rng.integers(0, M, len(v)), v] = rng.choice(who, len(v))
    return pack(x, t, lv, cd)
def setup_inputs_ties(rng):
    x, t, lv, cd = parts(rng); n = min(R // 8, S)
    base = rng.choice(np.array([0, 2 ** 19, TOP]), 8); base[0] = 0; base[1] = TOP; base[2] = 2 ** 19; sg = np.where(base > 2 ** 19, -1, 1)
    t = rng.choice(np.array([0, 1, 1000, 2 ** 18, 2 ** 19 - 8]), (N, 8, 1, 1)) + rng.integers(0, 3, (N, 8, 16, 1))
    x = np.tile(base.reshape(1, 8, 1, 1), (N, 1, 16, R))
    for a in range(N):
        for g in range(8):
            o = rng.permutation(R); hot, watch, calm = o[:n], o[n:2 * n], o[n:]; b, e = (a - 1) % N, (a - 2) % N
            m = (np.argsort(rng.random((16, n)), axis=0) < rng.choice(np.array([NEED - 1, NEED, 16]), n)).astype(np.int64)
            x[a, g][:, hot] = base[g] + sg[g] * (t[b, g] + m)
            v = b * S + rng.permutation(S)[:n]
            lv[a, g, 0, hot] = np.where(rng.random(n) < 0.4, v, np.where(rng.random(n) < 0.5, V - 1, np.maximum(v - 1, 0)))
            lv[a, g, 0, watch] = V - 1
            cd[a, g, 0] = rng.choice(calm, (M, V)); cd[a, g, 0, 0, v] = hot
            cd[a, g, 0, M - 1, e * S:(e + 1) * S] = rng.choice(watch, S)
    return pack(x, t, lv, cd)
def setup_inputs_alike(rng):
    x, t, lv, cd = parts(rng)
    cd[:, ::4] = rng.choice(np.array([0, R - 1, R // 2, 5]), (N, 2, RO, M, V)); cd[:, 3] = cd[:, 3][:, :, :1]
    lv[:, 1::2] = lv[:, 1::2, :1]
    lv[:, 2] = rng.choice(np.array([0, V - 1]), (N, P, R)); lv[:, 6] = rng.integers(0, 16, (N, P, R))
    return pack(x, t, lv, cd)
def setup_inputs_dim(rng):
    x, t, lv, cd = parts(rng); q = rng.permutation(N); k = int(rng.integers(0, 7)); o = int(q[1])
    lv[:, k] = lv[:, k] // 2; lv[q[0], :7] = rng.integers(0, 4, (7, P, R)); t[o] = TOP; t[q[2]] = 0
    for a, pixel in ((int(q[0]), 0), (int(q[3]), TOP)):
        s = rng.permutation(R)[:R // 16]; x[a, 7][:, s] = pixel; lv[a, 7, 0, s] = V - 1
        cd[a, 7, 0, 0, o * S:(o + 1) * S] = rng.choice(s, S)
    return pack(x, t, lv, cd)
def setup_inputs_spread(rng):
    x, t, lv, cd = parts(rng)
    t = np.minimum(np.exp2(10 + 10 * rng.random((N, 8, 16, 1))).astype(np.int64), TOP)
    x = np.minimum((np.exp2(20 * rng.random((N, 8, 1, R))) * rng.random((N, 8, 16, R))).astype(np.int64), TOP)
    return pack(x, t, lv, cd)
def check_inputs(d):
    bad = []
    for k, lo, hi in (("px", 0, TOP), ("th", 0, TOP), ("ray", 0, V - 1), ("cand", 0, R - 1)):
        if np.min(d[k]) < lo or np.max(d[k]) > hi: bad.append("range of " + k)
    return bad
def reference(px, th, ray, cand):
    x = px.astype(np.int64).reshape(N, 8, 16, R); t = th.astype(np.int64).reshape(N, 8, 16, 1)
    lv = np.stack([gentries(a) for a in ray]).astype(np.int64).reshape(N, 8, P, R)
    cd = np.stack([gentries(a) for a in cand]).astype(np.int64).reshape(N, 8, RO, M, V)
    c = np.zeros((N, 8, R), np.int64); number = np.arange(V)
    for rnd in range(RO):
        w = np.take_along_axis(lv, c[:, :, None, :], 2)[:, :, 0]
        lo = np.full((8, 16, V), TOP + 1, np.int64); hi = np.full((8, 16, V), -1, np.int64)
        for a in range(N):
            for m in range(M):
                ix = cd[a, :, rnd, m]
                sees = (number <= np.take_along_axis(w[a], ix, 1))[:, None, :]
                v = np.take_along_axis(x[a], ix[:, None, :], 2)
                lo = np.minimum(lo, np.where(sees, v, TOP + 1)); hi = np.maximum(hi, np.where(sees, v, -1))
        carved = np.zeros((8, V), bool)
        for o in range(N):
            far = (hi[:, :, o * S:(o + 1) * S] - lo[:, :, o * S:(o + 1) * S] > t[o]).astype(np.int64)
            odd = np.add.reduce(far, axis=1) >= NEED
            carved[:, o * S:(o + 1) * S] = odd & (np.add.accumulate(odd.astype(np.int64), axis=1) <= CAP)
        for step in range(H):
            w = np.take_along_axis(lv, c[:, :, None, :], 2)[:, :, 0]
            nx, nc = [], []
            for a in range(N):
                gone = np.take_along_axis(carved, w[a], 1); e = np.take_along_axis(lo, w[a][:, None, :], 2)
                nx.append(np.where(gone[:, None, :], np.clip(x[a] + ((x[a] - e) >> 2), 0, TOP), x[a]))
                nc.append(np.minimum(c[a] + gone.astype(np.int64), P - 1))
            x = np.stack(nx); c = np.stack(nc)
    yc = np.stack([gtable(c[a]) for a in range(N)])
    return {"yx": x.reshape(N, 128, R).astype(np.float32), "yc": yc.astype(np.float32)}

@@ -1,0 +1,436 @@
+from concourse.bass import DstId, RemoteDMATransfer
+from concourse.mybir import AluOpType, ActivationFunctionType
+
+A = AluOpType
+AF = ActivationFunctionType
+V, R, RO, H, CAP, NEED = 4096, 1280, 2, 3, 96, 9
+TOP = 2 ** 20 - 1
+D = float(2 ** 21)
+XW = R + 8
+
+_S = {
+    "ones": ([128, V], "float32"),
+    "cio": ([128, V], "float32"),
+    "wg": ([128, 4 * 2048], "bfloat16"),
+    "lo": ([128, V], "float32"), "hi": ([128, V], "float32"),
+    "bl": ([128, V], "float32"), "bh": ([128, V], "float32"),
+    "xs": ([128, 4 * R], "int32"), "xl": ([128, XW], "float32"), "xh": ([128, XW], "float32"),
+    "wr": ([128, R], "float32"), "fl": ([128, 3 * R], "bfloat16"), "ft": ([128, V], "bfloat16"),
+    "yb": ([128, R], "float32"), "x5": ([128, R], "float32"), "xf": ([128, R], "float32"),
+    "s1": ([128, 1024], "float32"), "s2": ([128, 512], "float32"),
+    "lof": ([128, 512], "float32"), "lt": ([128, 512], "float32"), "odd": ([128, 512], "float32"),
+    "pre": ([128, 520], "float32"), "c96": ([128, 512], "float32"),
+    "far": ([128, 512], "bfloat16"), "cv": ([128, 512], "bfloat16"), "fb": ([128, 512], "float32"),
+    "ci0": ([128, 512], "int32"), "ci1": ([128, 512], "int32"),
+    "cf0": ([128, 512], "float32"), "cf1": ([128, 512], "float32"),
+    "cu0": ([128, 512], "uint16"), "cu1": ([128, 512], "uint16"),
+    "off": ([128, 512], "uint16"), "tm": ([128, 512], "float32"),
+    "ri": ([128, 320], "int32"), "rf": ([128, 320], "float32"), "ru": ([128, 320], "uint16"),
+    "rd": ([128, 240], "float32"), "lq": ([128, 240], "uint16"), "lf": ([128, 240], "float32"),
+    "ef": ([128, 240], "float32"), "eg": ([128, 240], "float32"), "t1": ([128, 80], "float32"),
+    "t2": ([128, 80], "float32"), "t3": ([128, 80], "float32"), "t4": ([128, 80], "float32"),
+    "kk": ([128, 80], "float32"), "k2": ([128, 80], "float32"), "so": ([128, 80], "uint16"),
+    "cu": ([128, 80], "float32"), "cn": ([128, 80], "float32"), "rc": ([128, 80], "float32"),
+    "dsel": ([128, 16 * 128], "bfloat16"), "selo": ([128, 8 * 128], "bfloat16"),
+    "bones": ([128, 128], "bfloat16"), "ni": ([128, 128], "bfloat16"), "nv": ([128, 128], "bfloat16"),
+    "eye": ([128, 128], "float32"), "mi": ([128, 128], "int32"), "mj": ([128, 128], "int32"),
+    "mf": ([128, 128], "float32"), "mg": ([128, 128], "float32"),
+    "pi": ([128, 8], "int32"), "pf": ([128, 8], "float32"), "cm": ([128, 16], "float32"), "sm": ([128, 8], "float32"),
+    "thi": ([128, 1], "int32"), "thf": ([128, 1], "float32"),
+}
+SCRATCH = {k: ("sbuf", s, d) for k, (s, d) in _S.items()}
+for _k, _w, _d in (("c0", 64, "int32"), ("r", 40, "int32"), ("p", 160, "int32"), ("c1", 64, "int32"),
+                   ("y0", 80, "float32"), ("y1", 80, "float32"), ("c", 10, "float32")):
+    SCRATCH["st" + _k] = ("dram", [8, 128, _w], _d)
+    SCRATCH["ld" + _k] = ("dram", [8, 128, _w], _d)
+SCRATCH["stt"] = ("dram", [128, 1], "int32")
+SCRATCH["ldt"] = ("dram", [8, 128, 1], "int32")
+SCRATCH["fd"] = ("dram", [16, V], "float32")
+SCRATCH["pp"] = ("psum", [128, 2048], "float32")
+for _k in range(4):
+    SCRATCH["z%d" % _k] = ("psum", [128, 512], "float32")
+PSUM = ("pp", "z0", "z1", "z2", "z3")
+
+CLASSES = ("c0", "r", "p", "t", "c1", "y0", "y1", "c")
+TWO_CALLS = ("c0", "p", "c1", "y0", "y1", "r")
+SEMAPHORES = (["q_v", "q_a", "q_t", "q_g", "sent"] + ["arr_" + k for k in CLASSES] + ["stg_" + k for k in CLASSES]
+              + ["own_" + k for k in CLASSES] + ["get_" + k for k in CLASSES]
+              + ["rl0", "rl1", "rh0", "rh1", "fs0", "fs1", "fg0", "fg1"])
+
+
+def plan(core, cores, topo, two):
+    r = cores.index(core)
+    order = [cores[(r + k) % len(cores)] for k in range(1, len(cores))]
+    near = [d for d in order if d in topo.cores_of(core)]
+    far = [d for d in order if d not in near]
+    fe = topo.engines(core, far[0])
+    ne = [e for e in topo.engines(core, near[0]) if e not in fe]
+    if two:
+        first = [(d, fe[2 * k:2 * k + 2]) for k, d in enumerate(far[:4])]
+        second = [(d, fe[4 * k:4 * k + 4]) for k, d in enumerate(far[4:])]
+        return [second + [(near[0], ne)], first]
+    return [[(d, fe[k:k + 1]) for k, d in enumerate(far)] + [(near[0], ne)]]
+
+
+def rank_program(g, core, T, topo):
+    q = T.rank_of(core)
+    if q is None:
+        return
+    cores = list(T.cores)
+    sem = T.sem
+    queues = {"v": g.vector, "a": g.scalar, "t": g.tensor, "s": g.sync, "g": g}
+    csem = {"v": "q_v", "a": "q_a", "t": "q_t", "g": "q_g"}
+    total = {}
+    known = {}
+    closed = {}
+    hist = {}
+
+    def need(qn, s, val):
+        if val is None:
+            val = total[s]
+            closed[s] = True
+        if known.get((qn, s), 0) < val:
+            queues[qn].wait_ge(sem[s], val)
+            known[(qn, s)] = val
+
+    def depend(qn, acc, own):
+        wants = {}
+        for name, lo, hi, w in acc:
+            ps = name in PSUM
+            if ps:
+                lo, hi = lo // 512 * 512, -(-hi // 512) * 512
+            for (l2, h2, w2, q2, s2, v2) in hist.get(name, []):
+                if l2 >= hi or h2 <= lo or s2 == own:
+                    continue
+                if not (w or w2 or (ps and q2 != qn)):
+                    continue
+                v = total[s2] if v2 is None else v2
+                if v2 is None:
+                    closed[s2] = True
+                wants[s2] = max(wants.get(s2, 0), v)
+        for s in wants:
+            need(qn, s, wants[s])
+
+    def record(qn, acc, s, val):
+        for name, lo, hi, w in acc:
+            if name in PSUM:
+                lo, hi = lo // 512 * 512, -(-hi // 512) * 512
+            h = hist.setdefault(name, [])
+            if w:
+                h[:] = [e for e in h if not (e[0] >= lo and e[1] <= hi and not (e[4] == s and e[5] is None))]
+            h.append((lo, hi, w, qn, s, val))
+
+    def accs(rd, wr):
+        return [(n, a, b, False) for n, a, b in rd] + [(n, a, b, True) for n, a, b in wr]
+
+    def ops(qn, rd, wr, fns):
+        s = csem[qn]
+        acc = accs(rd, wr)
+        depend(qn, acc, None)
+        for f in fns[:-1]:
+            f(queues[qn])
+        fns[-1](queues[qn]).then_inc(sem[s], 1)
+        total[s] = total.get(s, 0) + 1
+        record(qn, acc, s, total[s])
+
+    def op(qn, rd, wr, fn):
+        ops(qn, rd, wr, [fn])
+
+    def dma(qn, s, rd, wr, out, in_):
+        assert s not in closed, s
+        acc = accs(rd, wr)
+        depend(qn, acc, s)
+        queues[qn].dma_start(out=out, in_=in_).then_inc(sem[s], 16)
+        total[s] = total.get(s, 0) + 16
+        record(qn, acc, s, None)
+
+    def send(c, piece):
+        need("g", "stg_" + c, None)
+        for call in plan(core, cores, topo, c in TWO_CALLS):
+            tr = []
+            for d, eng in call:
+                rid, pid = topo.addr(d, core)
+                m = sum(1 << e for e in eng)
+                assert m & topo.mask(core, d) == m
+                tr.append(RemoteDMATransfer(dst_ids=[DstId(rid=rid, pnc=pid)], dma_engine_mask=m,
+                                            remote_sem=sem["arr_" + c], srcs=[piece(T.rank_of(d))], dsts=[T["ld" + c][q]]))
+                total["sent"] = total.get("sent", 0) + len(eng)
+            g.remote_dma_fused(tr, local_sem=sem.sent)
+        n = 0
+        for o in cores:
+            if o != core:
+                for call in plan(o, cores, topo, c in TWO_CALLS):
+                    n += sum(len(eng) for d, eng in call if d == core)
+        total["arr_" + c] = n
+        record("far", [("ld" + c, 0, q, True), ("ld" + c, q + 1, 8, True)], "arr_" + c, n)
+
+    dma("s", "stg_c0", [], [("stc0", 0, 8)], T.stc0[:], T.cand[:, 0:512])
+    dma("a", "stg_r", [], [("str", 0, 8)], T["str"][:], T.ray[:])
+    dma("s", "stg_p", [], [("stp", 0, 8)], T.stp[:], T.px[:])
+    dma("a", "own_c0", [], [("ldc0", q, q + 1)], T.ldc0[q], T.cand[16 * q:16 * q + 16, 0:512])
+    dma("a", "own_r", [], [("ldr", q, q + 1)], T.ldr[q], T.ray[16 * q:16 * q + 16, :])
+    dma("s", "own_p", [], [("ldp", q, q + 1)], T.ldp[q], T.px[16 * q:16 * q + 16, :])
+    op("g", [], [("pi", 0, 1)], lambda e: e.iota(T.pi[:, 0:1], [[0, 1]], 0, 1))
+    send("r", lambda d: T["str"][d])
+    send("c0", lambda d: T.stc0[d])
+    send("p", lambda d: T.stp[d])
+    dma("s", "get_r", [("ldr", 0, 8)], [("ri", 0, 320)], T.ri[:], T.ldr[:])
+    dma("s", "get_c0", [("ldc0", 0, 8)], [("ci0", 0, 512)], T.ci0[:], T.ldc0[:])
+    dma("s", "get_p", [("ldp", 0, 8)], [("xs", 0, R)], T.xs[:, 0:R], T.ldp[:])
+    dma("s", "stg_t", [], [("stt", 0, 8)], T.stt[:], T.th[:])
+    dma("s", "own_t", [], [("ldt", q, q + 1)], T.ldt[q], T.th[:])
+    dma("s", "stg_c1", [], [("stc1", 0, 8)], T.stc1[:], T.cand[:, 512:1024])
+    dma("s", "own_c1", [], [("ldc1", q, q + 1)], T.ldc1[q], T.cand[16 * q:16 * q + 16, 512:1024])
+    send("t", lambda d: T.stt[:])
+    send("c1", lambda d: T.stc1[d])
+
+    def ap(b):
+        return T[b[0]][:, b[1]:b[2]]
+
+    def ts(out, in0, s1, s2, o0, o1=None, extra=()):
+        if o1 is None:
+            op("v", [in0] + list(extra), [out], lambda e: e.tensor_scalar(ap(out), ap(in0), s1, None, o0))
+        else:
+            op("v", [in0] + list(extra), [out], lambda e: e.tensor_scalar(ap(out), ap(in0), s1, s2, o0, o1))
+
+    def tt(out, in0, in1, o):
+        op("v", [in0, in1], [out], lambda e: e.tensor_tensor(ap(out), ap(in0), ap(in1), o))
+
+    def copy(out, in_):
+        op("v", [in_], [out], lambda e: e.tensor_copy(ap(out), ap(in_)))
+
+    def fill(out, c):
+        op("v", [], [out], lambda e: e.memset(ap(out), c))
+
+    def act(out, in_, scale=1.0, bias=0.0, extra=()):
+        op("a", [in_] + list(extra), [out], lambda e: e.activation(ap(out), ap(in_), AF.Identity, bias=bias, scale=scale))
+
+    def act_gather(out, win, lst, bias=0.0, scale=1.0):
+        op("a", [win, lst], [out],
+           lambda e: e.activation(ap(out), ap(win).indirect(ap(lst)), AF.Identity, bias=bias, scale=scale))
+
+    def tt_gather(out, win, lst, in1, o):
+        op("v", [win, lst, in1], [out], lambda e: e.tensor_tensor(ap(out), ap(win).indirect(ap(lst)), ap(in1), o))
+
+    fill(("ones", 0, V), 1.0)
+    op("v", [("ones", 0, V)], [("cio", 0, V)],
+       lambda e: e.tensor_tensor_scan(T.cio[:], T.ones[:], T.ones[:], -1.0, A.add, A.mult))
+    ts(("pi", 1, 2), ("pi", 0, 1), 15, None, A.bitwise_and)
+    ts(("pi", 2, 3), ("pi", 0, 1), 4, None, A.arith_shift_right)
+    copy(("pf", 0, 3), ("pi", 0, 3))
+    ts(("pf", 3, 4), ("pf", 1, 2), -1.0, 255.0, A.mult, A.add)
+    pcol, c16, bcol, k255 = (T.pf[:, k:k + 1] for k in range(4))
+    pfr = [("pf", 0, 4)]
+    copy(("mi", 0, 128), ("cio", 0, 128))
+    ts(("eye", 0, 128), ("cio", 0, 128), pcol, None, A.is_equal, extra=pfr)
+    ts(("cm", 0, 16), ("cio", 0, 16), c16, -2048.0, A.is_equal, A.mult, extra=pfr)
+    ts(("sm", 0, 8), ("cio", 0, 8), 16.0, pcol, A.mult, A.is_equal, extra=pfr)
+    ts(("rc", 0, 80), ("cio", 0, 80), 16.0, c16, A.mult, A.add, extra=pfr)
+    ts(("mj", 0, 128), ("mi", 0, 128), 31, None, A.bitwise_and)
+    copy(("mf", 0, 128), ("mj", 0, 128))
+    ts(("nv", 0, 128), ("mf", 0, 128), -16.0, k255, A.mult, A.add, extra=pfr)
+    ts(("ni", 0, 128), ("eye", 0, 128), -2048.0, None, A.mult)
+    for i in range(16):
+        ts(("dsel", 128 * i, 128 * i + 128), ("eye", 0, 128), T.cm[:, i:i + 1], None, A.mult, extra=[("cm", 0, 16)])
+    fill(("xl", R, XW), D)
+    fill(("xh", R, XW), -1.0)
+    copy(("ru", 0, 320), ("ri", 0, 320))
+    ts(("mi", 0, 128), ("mi", 0, 128), 4, None, A.arith_shift_right)
+    copy(("mg", 0, 128), ("mi", 0, 128))
+    ts(("bones", 0, 128), ("mg", 0, 128), bcol, None, A.is_equal, extra=pfr)
+    fill(("c96", 0, 512), float(CAP))
+    fill(("pre", 7, 8), 0.0)
+    copy(("rf", 0, 320), ("ri", 0, 320))
+    tt(("rd", 0, 240), ("rf", 80, 320), ("rf", 0, 240), A.subtract)
+    copy(("cu0", 0, 512), ("ci0", 0, 512))
+    copy(("cf0", 0, 512), ("ci0", 0, 512))
+
+    def extract(bank, ncol, buf, base, with_v):
+        fns = []
+        for i in range(16):
+            fns.append(lambda e, i=i: e.matmul(T[bank][:, 0:ncol], T.dsel[:, 128 * i:128 * i + 128],
+                                               T[buf][:, base + i:base + 16 * ncol:16], i == 0, (not with_v) and i == 15))
+        rd = [("dsel", 0, 2048), (buf, base, base + 16 * ncol)]
+        if with_v:
+            fns.append(lambda e: e.matmul(T[bank][:, 0:ncol], T.ni[:], T.nv[:, 0:ncol], False, True))
+            rd += [("ni", 0, 128), ("nv", 0, 128)]
+        ops("t", rd, [(bank, 0, 512)], fns)
+
+    def reduce_ranks(b, o, last):
+        act(("pp", 0, 1024), (b, 0, 1024))
+        act(("pp", 1024, 2048), (b, 1024, 2048))
+        tt(("s1", 0, 1024), ("pp", 0, 1024), (b, 2048, 3072), o)
+        tt(("pp", 0, 1024), ("pp", 1024, 2048), (b, 3072, 4096), o)
+        tt(("s2", 0, 512), ("pp", 0, 512), ("s1", 0, 512), o)
+        tt(("pp", 1024, 1536), ("pp", 512, 1024), ("s1", 512, 1024), o)
+        tt(last, ("pp", 1024, 1536), ("s2", 0, 512), o)
+
+    def relayout(s, b, to, p, split):
+        for o in (2 * p, 2 * p + 1):
+            for a in range(8):
+                qn = "a" if split and o % 2 else "s"
+                dma(qn, s, [(b, 512 * o, 512 * o + 512)], [(to, 512 * a, 512 * a + 512)],
+                    T[to][16 * o:16 * o + 16, 512 * a:512 * a + 512], T[b][16 * a:16 * a + 16, 512 * o:512 * o + 512])
+
+    for t in range(RO):
+        cu, cf = "cu%d" % t, "cf%d" % t
+        lst = "ru" if t == 0 else "lq"
+
+        def see(qn, j, k):
+            b = 2048 * (j // 2) + 512 * k
+            c = 256 * (j % 2) + b // 16
+            out, win, off = ("wg", 2048 * j + 512 * k, 2048 * j + 512 * k + 512), ("wr", 0, R), (cu, c, c + 32)
+            if qn == "a":
+                act_gather(out, win, off, -(b + 255.0))
+            else:
+                op("v", [win, off], [out],
+                   lambda e: e.tensor_scalar(ap(out), ap(win).indirect(ap(off)), b + 255.0, None, A.subtract))
+
+        def lists(j):
+            h, m = j // 2, j % 2
+            tt(("tm", 128 * j, 128 * j + 128), ("z%d" % j, 0, 128), (cf, 256 * m + 128 * h, 256 * m + 128 * h + 128), A.max)
+            ts(("off", 128 * j, 128 * j + 128), ("tm", 128 * j, 128 * j + 128), float(R), None, A.min)
+
+        def first(b, x, p):
+            c = 256 * (p // 2) + 64 * (p % 2)
+            act_gather((b, 1024 * p, 1024 * p + 1024), (x, 0, XW), ("off", c, c + 64))
+
+        def second(b, x, p, o):
+            c = 256 * (p // 2) + 128 + 64 * (p % 2)
+            tt_gather((b, 1024 * p, 1024 * p + 1024), (x, 0, XW), ("off", c, c + 64), (b, 1024 * p, 1024 * p + 1024), o)
+
+        act_gather(("wr", 0, R), ("cio", 0, V), (lst, 0, 80))
+        for k in range(4):
+            see("a", 0, k)
+            see("v", 1, k)
+        extract("z0", 128, "wg", 0, True)
+        extract("z1", 128, "wg", 2048, True)
+        for k in range(4):
+            see("a", 2, k)
+        see("a", 3, 0)
+        extract("z2", 128, "wg", 4096, True)
+        if t == 0:
+            copy(("xl", 0, R), ("xs", 0, R))
+        see("v", 3, 1)
+        lists(0)
+        first("lo", "xl", 0)
+        see("v", 3, 2)
+        see("v", 3, 3)
+        extract("z3", 128, "wg", 6144, True)
+        first("lo", "xl", 1)
+        lists(1)
+
+        second("lo", "xl", 0, A.min)
+        relayout("rl%d" % t, "lo", "bl", 0, False)
+        lists(2)
+        second("lo", "xl", 1, A.min)
+        relayout("rl%d" % t, "lo", "bl", 1, False)
+        lists(3)
+        for p in (2, 3):
+            first("lo", "xl", p)
+            second("lo", "xl", p, A.min)
+            relayout("rl%d" % t, "lo", "bl", p, False)
+        act(("xh", 0, R), ("xl", 0, R))
+        for p in range(4):
+            first("hi", "xh", p)
+        for p in range(4):
+            second("hi", "xh", p, A.max)
+            if p < 3:
+                relayout("rh%d" % t, "hi", "bh", p, False)
+        reduce_ranks("bl", A.min, ("lof", 0, 512))
+        relayout("rh%d" % t, "hi", "bh", 3, True)
+        act(("x5", 0, R), ("xl", 0, R), scale=1.25)
+        if t == 0:
+            dma("s", "get_t", [("ldt", 0, 8)], [("thi", 0, 1)], T.thi[:], T.ldt[:, 16 * q:16 * q + 16, :])
+            copy(("thf", 0, 1), ("thi", 0, 1))
+            for o in range(8):
+                ts(("selo", 128 * o, 128 * o + 128), ("cio", 0, 128), 0.0, T.sm[:, o:o + 1], A.is_ge, A.mult,
+                   extra=[("sm", 0, 8)])
+        else:
+            copy(("xs", 0, R), ("xl", 0, R))
+        act(("fb", 0, 512), ("lof", 0, 512), scale=-0.25, bias=-0.375)
+        act(("lt", 0, 512), ("lof", 0, 512), bias=T.thf[:, 0:1], extra=[("thf", 0, 1)])
+        for o in range(8):
+            dma("s", "fs%d" % t, [("fb", 0, 512)], [("fd", 512 * o, 512 * o + 512)],
+                T.fd[:, 512 * o:512 * o + 512], T.fb[16 * o:16 * o + 16, :])
+        for a in range(8):
+            dma("s", "fg%d" % t, [("fd", 0, V)], [("ones", 0, V)], T.ones[16 * a:16 * a + 16, :], T.fd[:])
+        if t == 0:
+            dma("s", "get_c1", [("ldc1", 0, 8)], [("ci1", 0, 512)], T.ci1[:], T.ldc1[:])
+        reduce_ranks("bh", A.max, ("pp", 1536, 2048))
+
+        tt(("far", 0, 512), ("pp", 1536, 2048), ("lt", 0, 512), A.is_gt)
+        ops("t", [("bones", 0, 128), ("far", 0, 512)], [("z0", 0, 512)],
+            [lambda e: e.matmul(T.z0[:], T.bones[:], T.far[:], True, True)])
+        ts(("odd", 0, 512), ("z0", 0, 512), float(NEED), None, A.is_ge)
+        op("v", [("odd", 0, 512), ("c96", 0, 512)], [("pre", 8, 520)],
+           lambda e: e.tensor_tensor_scan(T.pre[:, 8:520], T.odd[:], T.c96[:], 0.0, A.add, A.min))
+        tt(("cv", 0, 512), ("pre", 8, 520), ("pre", 7, 519), A.subtract)
+        for o in range(8):
+            z = "z%d" % (o % 4)
+            ops("t", [("selo", 128 * o, 128 * o + 128), ("cv", 0, 512)], [(z, 0, 512)],
+                [lambda e, z=z, o=o: e.matmul(T[z][:], T.selo[:, 128 * o:128 * o + 128], T.cv[:], True, True)])
+            act(("ft", 512 * o, 512 * o + 512), (z, 0, 512))
+
+        for s in range(H):
+            act_gather(("fl", R * s, R * s + R), ("ft", 0, V), (lst, 80 * s, 80 * s + 80), scale=-1.0 / 2048.0)
+            extract("z%d" % s, 80, "fl", R * s, False)
+        for s in range(H):
+            tt_gather(("yb", 0, R), ("ones", 0, V), (lst, 80 * s, 80 * s + 80), ("x5", 0, R), A.add)
+            ts(("xs", R * s + R, R * s + 2 * R), ("yb", 0, R), 0.0, float(TOP), A.max, A.min)
+            if s < H - 1:
+                ts(("x5", 0, R), ("xs", R * s + R, R * s + 2 * R), 1.25, None, A.mult)
+            if t == 0 and s == 0:
+                copy(("cu1", 0, 512), ("ci1", 0, 512))
+                copy(("cf1", 0, 512), ("ci1", 0, 512))
+        e1, e2, e3 = ("ef", 0, 80), ("ef", 80, 160), ("ef", 160, 240)
+        copy(e1, ("z0", 0, 80))
+        tt(e2, ("z1", 0, 80), e1, A.mult)
+        tt(e3, ("z2", 0, 80), e2, A.mult)
+        if t == 0:
+            tt(("eg", 0, 240), ("ef", 0, 240), ("rd", 0, 240), A.mult)
+            tt(("t1", 0, 80), ("eg", 0, 80), ("rf", 0, 80), A.add)
+            tt(("t2", 0, 80), ("eg", 80, 160), ("eg", 160, 240), A.add)
+            tt(("lf", 0, 80), ("t1", 0, 80), ("t2", 0, 80), A.add)
+            copy(("lq", 0, 80), ("lf", 0, 80))
+        tt(("k2", 0, 80), e1, e2, A.add)
+        tt(("kk", 0, 80), ("k2", 0, 80), e3, A.add)
+        ts(("t4", 0, 80), ("kk", 0, 80), float(R), None, A.mult)
+        tt(("t4", 0, 80), ("t4", 0, 80), ("rc", 0, 80), A.add)
+        copy(("so", 0, 80), ("t4", 0, 80))
+
+        def pick(to, h):
+            op("v", [("xs", 0, 4 * R), ("so", 0, 80)], [(to, 640 * h, 640 * h + 640)],
+               lambda e: e.tensor_copy(T[to][:, 640 * h:640 * h + 640], T.xs[:].indirect(T.so[:, 40 * h:40 * h + 40])))
+
+        if t == 0:
+            pick("xl", 0)
+            pick("xl", 1)
+            tt(("t1", 0, 80), e1, ("rd", 80, 160), A.mult)
+            tt(("t2", 0, 80), e2, ("rd", 160, 240), A.mult)
+            tt(("t3", 0, 80), e1, ("rd", 160, 240), A.mult)
+            tt(("t1", 0, 80), ("t1", 0, 80), ("rf", 80, 160), A.add)
+            tt(("lf", 80, 160), ("t1", 0, 80), ("t2", 0, 80), A.add)
+            tt(("lf", 160, 240), ("t3", 0, 80), ("rf", 160, 240), A.add)
+            copy(("lq", 80, 240), ("lf", 80, 240))
+            copy(("cu", 0, 80), ("kk", 0, 80))
+        else:
+            pick("xf", 0)
+            dma("s", "stg_y0", [("xf", 0, 640)], [("sty0", 0, 8)], T.sty0[:], T.xf[:, 0:640])
+            pick("xf", 1)
+            dma("a", "stg_y1", [("xf", 640, R)], [("sty1", 0, 8)], T.sty1[:], T.xf[:, 640:R])
+            tt(("t1", 0, 80), ("cu", 0, 80), ("kk", 0, 80), A.add)
+            ts(("cn", 0, 80), ("t1", 0, 80), 3.0, None, A.min)
+
+    dma("s", "stg_c", [("cn", 0, 80)], [("stc", 0, 8)], T.stc[:], T.cn[:])
+    send("y0", lambda d: T.sty0[d])
+    send("y1", lambda d: T.sty1[d])
+    send("c", lambda d: T.stc[d])
+    dma("a", "own_y0", [("sty0", 0, 8)], [("ldy0", q, q + 1)], T.ldy0[q], T.sty0[q])
+    dma("a", "own_y1", [("sty1", 0, 8)], [("ldy1", q, q + 1)], T.ldy1[q], T.sty1[q])
+    dma("a", "own_c", [("stc", 0, 8)], [("ldc", q, q + 1)], T.ldc[q], T.stc[q])
+    dma("s", "get_y0", [("ldy0", 0, 8)], [], T.yx[:, 0:640], T.ldy0[:])
+    dma("s", "get_y1", [("ldy1", 0, 8)], [], T.yx[:, 640:R], T.ldy1[:])
+    dma("a", "get_c", [("ldc", 0, 8)], [], T.yc[:], T.ldc[:])
+    for s in total:
+        need("g", s, total[s])

@@ -1,3 +1,4 @@
+import math
 from concourse.bass import DstId, RemoteDMATransfer
 from concourse.mybir import AluOpType, ActivationFunctionType
 
@@ -7,68 +8,73 @@ V, R, RO, H, CAP, NEED = 4096, 1280, 2, 3, 96, 9
 TOP = 2 ** 20 - 1
 D = float(2 ** 21)
 XW = R + 8
+S = 2048
 
 _S = {
-    "ones": ([128, V], "float32"),
+    "et": ([128, V], "float32"),
     "cio": ([128, V], "float32"),
     "wg": ([128, 4 * 2048], "bfloat16"),
     "lo": ([128, V], "float32"), "hi": ([128, V], "float32"),
     "bl": ([128, V], "float32"), "bh": ([128, V], "float32"),
-    "xs": ([128, 4 * R], "int32"), "xl": ([128, XW], "float32"), "xh": ([128, XW], "float32"),
-    "wr": ([128, R], "float32"), "fl": ([128, 3 * R], "bfloat16"), "ft": ([128, V], "bfloat16"),
-    "yb": ([128, R], "float32"), "x5": ([128, R], "float32"), "xf": ([128, R], "float32"),
-    "s1": ([128, 1024], "float32"), "s2": ([128, 512], "float32"),
-    "lof": ([128, 512], "float32"), "lt": ([128, 512], "float32"), "odd": ([128, 512], "float32"),
-    "pre": ([128, 520], "float32"), "c96": ([128, 512], "float32"),
-    "far": ([128, 512], "bfloat16"), "cv": ([128, 512], "bfloat16"), "fb": ([128, 512], "float32"),
+    "xs": ([128, 4 * S + XW], "float32"), "xh": ([128, XW], "float32"), "pxi": ([128, R], "int32"),
+    "s1": ([128, 1024], "float32"), "s2": ([128, 512], "float32"), "fb": ([128, 512], "float32"),
+    "wr": ([128, R], "float32"), "fl": ([128, 3 * R], "bfloat16"), "ft": ([128, 256], "bfloat16"),
+    "yi": ([128, R], "int32"), "x5": ([128, R], "float32"), "xf": ([128, R], "float32"),
+    "lof": ([128, 512], "float32"), "lt": ([128, 512], "float32"), "odd": ([128, 512], "bfloat16"),
+    "pre": ([128, 528], "bfloat16"), "c96": ([128, 512], "bfloat16"), "far": ([128, 512], "bfloat16"),
     "ci0": ([128, 512], "int32"), "ci1": ([128, 512], "int32"),
-    "cf0": ([128, 512], "float32"), "cf1": ([128, 512], "float32"),
-    "cu0": ([128, 512], "uint16"), "cu1": ([128, 512], "uint16"),
-    "off": ([128, 512], "uint16"), "tm": ([128, 512], "float32"),
-    "ri": ([128, 320], "int32"), "rf": ([128, 320], "float32"), "ru": ([128, 320], "uint16"),
-    "rd": ([128, 240], "float32"), "lq": ([128, 240], "uint16"), "lf": ([128, 240], "float32"),
-    "ef": ([128, 240], "float32"), "eg": ([128, 240], "float32"), "t1": ([128, 80], "float32"),
+    "cu0": ([128, 512], "uint16"), "cu1": ([128, 512], "uint16"), "tm": ([128, 512], "float32"),
+    "off": ([128, 512], "uint16"), "of0": ([128, 512], "uint16"),
+    "rh": ([128, 80], "int32"), "lh": ([128, 80], "uint16"), "one": ([128, 256], "float32"),
+    "ri": ([128, 320], "int32"), "rd": ([128, 240], "float32"), "li": ([128, 240], "int32"),
+    "lq0": ([128, 240], "uint16"), "lq1": ([128, 240], "uint16"),
+    "ua": ([128, 240], "int32"), "ub": ([128, 240], "int32"), "uu": ([128, 240], "uint16"), "bf": ([128, 3, 80], "float32"),
+    "pw": ([128, 240], "bfloat16"), "p2": ([128, 240], "bfloat16"),
+    "ef": ([128, 240], "int32"), "eg": ([128, 240], "float32"), "t1": ([128, 80], "float32"),
     "t2": ([128, 80], "float32"), "t3": ([128, 80], "float32"), "t4": ([128, 80], "float32"),
-    "kk": ([128, 80], "float32"), "k2": ([128, 80], "float32"), "so": ([128, 80], "uint16"),
-    "cu": ([128, 80], "float32"), "cn": ([128, 80], "float32"), "rc": ([128, 80], "float32"),
-    "dsel": ([128, 16 * 128], "bfloat16"), "selo": ([128, 8 * 128], "bfloat16"),
-    "bones": ([128, 128], "bfloat16"), "ni": ([128, 128], "bfloat16"), "nv": ([128, 128], "bfloat16"),
-    "eye": ([128, 128], "float32"), "mi": ([128, 128], "int32"), "mj": ([128, 128], "int32"),
-    "mf": ([128, 128], "float32"), "mg": ([128, 128], "float32"),
-    "pi": ([128, 8], "int32"), "pf": ([128, 8], "float32"), "cm": ([128, 16], "float32"), "sm": ([128, 8], "float32"),
-    "thi": ([128, 1], "int32"), "thf": ([128, 1], "float32"),
+    "so": ([128, 80], "uint16"), "cu": ([128, 80], "float32"), "cn": ([128, 80], "float32"),
+    "rc": ([128, 160], "float32"),
+    "wd": ([128, 144], "bfloat16"), "wf": ([128, 144], "bfloat16"), "lm": ([128, 512], "bfloat16"),
+    "bones": ([128, 128], "bfloat16"), "ni": ([128, 128], "bfloat16"), "nh": ([128, 128], "bfloat16"),
+    "nv": ([128, 128], "bfloat16"), "mv": ([128, 128], "float32"),
+    "mi": ([128, 136], "int32"), "ma": ([128, 136], "int32"), "mb": ([128, 136], "int32"), "mc": ([128, 136], "int32"),
+    "mf": ([128, 136], "float32"), "mg": ([128, 136], "float32"),
+    "pf": ([128, 16], "float32"), "pb": ([128, 8], "bfloat16"),
+    "thi": ([128, 1], "int32"), "thn": ([128, 2], "float32"), "thf": ([128, 2], "float32"),
 }
 SCRATCH = {k: ("sbuf", s, d) for k, (s, d) in _S.items()}
-for _k, _w, _d in (("c0", 64, "int32"), ("r", 40, "int32"), ("p", 160, "int32"), ("c1", 64, "int32"),
+for _k, _w, _d in (("o0", 32, "uint16"), ("o1", 32, "uint16"), ("r", 40, "int32"), ("p", 160, "int32"), ("c1", 64, "int32"),
                    ("y0", 80, "float32"), ("y1", 80, "float32"), ("c", 10, "float32")):
     SCRATCH["st" + _k] = ("dram", [8, 128, _w], _d)
     SCRATCH["ld" + _k] = ("dram", [8, 128, _w], _d)
 SCRATCH["stt"] = ("dram", [128, 1], "int32")
 SCRATCH["ldt"] = ("dram", [8, 128, 1], "int32")
-SCRATCH["fd"] = ("dram", [16, V], "float32")
 SCRATCH["pp"] = ("psum", [128, 2048], "float32")
 for _k in range(4):
     SCRATCH["z%d" % _k] = ("psum", [128, 512], "float32")
 PSUM = ("pp", "z0", "z1", "z2", "z3")
 
-CLASSES = ("c0", "r", "p", "t", "c1", "y0", "y1", "c")
-TWO_CALLS = ("c0", "p", "c1", "y0", "y1", "r")
+CLASSES = ("o0", "o1", "r", "p", "t", "c1", "y0", "y1", "c")
+TWO_CALLS = ("p", "c1", "y0", "y1", "r")
 SEMAPHORES = (["q_v", "q_a", "q_t", "q_g", "sent"] + ["arr_" + k for k in CLASSES] + ["stg_" + k for k in CLASSES]
               + ["own_" + k for k in CLASSES] + ["get_" + k for k in CLASSES]
-              + ["rl0", "rl1", "rh0", "rh1", "fs0", "fs1", "fg0", "fg1"])
+              + ["rl0", "rl1", "rh0", "rh1", "fg0", "fg1", "xc0", "xc1", "in_r", "in_c"])
 
 
 def plan(core, cores, topo, two):
     r = cores.index(core)
     order = [cores[(r + k) % len(cores)] for k in range(1, len(cores))]
     near = [d for d in order if d in topo.cores_of(core)]
-    far = [d for d in order if d not in near]
+    mate = [d for d in order if topo.mates(core, d)]
+    plane = [d for d in order if topo.same_plane(core, d)]
+    both = [d for d in order if d not in near + mate + plane]
+    far = both + [mate[0], plane[0], mate[1], plane[1]]
     fe = topo.engines(core, far[0])
-    ne = [e for e in topo.engines(core, near[0]) if e not in fe]
+    ne = [e for e in topo.engines(core, near[0]) if e not in fe][:4]
     if two:
         first = [(d, fe[2 * k:2 * k + 2]) for k, d in enumerate(far[:4])]
         second = [(d, fe[4 * k:4 * k + 4]) for k, d in enumerate(far[4:])]
-        return [second + [(near[0], ne)], first]
+        return [first, second + [(near[0], ne)]]
     return [[(d, fe[k:k + 1]) for k, d in enumerate(far)] + [(near[0], ne)]]
 
 
@@ -164,34 +170,43 @@ def rank_program(g, core, T, topo):
         total["arr_" + c] = n
         record("far", [("ld" + c, 0, q, True), ("ld" + c, q + 1, 8, True)], "arr_" + c, n)
 
-    dma("s", "stg_c0", [], [("stc0", 0, 8)], T.stc0[:], T.cand[:, 0:512])
-    dma("a", "stg_r", [], [("str", 0, 8)], T["str"][:], T.ray[:])
-    dma("s", "stg_p", [], [("stp", 0, 8)], T.stp[:], T.px[:])
-    dma("a", "own_c0", [], [("ldc0", q, q + 1)], T.ldc0[q], T.cand[16 * q:16 * q + 16, 0:512])
-    dma("a", "own_r", [], [("ldr", q, q + 1)], T.ldr[q], T.ray[16 * q:16 * q + 16, :])
-    dma("s", "own_p", [], [("ldp", q, q + 1)], T.ldp[q], T.px[16 * q:16 * q + 16, :])
-    op("g", [], [("pi", 0, 1)], lambda e: e.iota(T.pi[:, 0:1], [[0, 1]], 0, 1))
-    send("r", lambda d: T["str"][d])
-    send("c0", lambda d: T.stc0[d])
+    def grp(a):
+        return slice(16 * a, 16 * a + 16)
+
+    mine = grp(q)
+
+    def stage(qn, c, src, cols):
+        dma(qn, "stg_" + c, [], [("st" + c, 0, 8)], T["st" + c][:], src[:, cols])
+
+    def fetch(qn, c, to, cols):
+        wr = [] if to in ("yx", "yc") else [(to, cols.start, cols.stop)]
+        if q > 0:
+            dma(qn, "get_" + c, [("ld" + c, 0, q)], wr, T[to][0:16 * q, cols], T["ld" + c][0:q])
+        if q < 7:
+            dma(qn, "get_" + c, [("ld" + c, q + 1, 8)], wr, T[to][16 * q + 16:128, cols], T["ld" + c][q + 1:8])
+
+    dma("a", "in_r", [], [("rh", 0, 80)], T.rh[:], T.ray[:, 0:80])
+    stage("s", "p", T.px, slice(0, R))
+    dma("a", "in_c", [], [("ci0", 0, 512)], T.ci0[:], T.cand[:, 0:512])
+    op("g", [], [("mi", 128, 129)], lambda e: e.iota(T.mi[:, 128:129], [[0, 1]], 0, 1))
+    op("g", [], [("cio", 3072, V)],
+       lambda e: e.iota(T.cio[:, 3072:V], [[1, 1024]], 3072, 0, allow_small_or_imprecise_dtypes=True))
     send("p", lambda d: T.stp[d])
-    dma("s", "get_r", [("ldr", 0, 8)], [("ri", 0, 320)], T.ri[:], T.ldr[:])
-    dma("s", "get_c0", [("ldc0", 0, 8)], [("ci0", 0, 512)], T.ci0[:], T.ldc0[:])
-    dma("s", "get_p", [("ldp", 0, 8)], [("xs", 0, R)], T.xs[:, 0:R], T.ldp[:])
-    dma("s", "stg_t", [], [("stt", 0, 8)], T.stt[:], T.th[:])
-    dma("s", "own_t", [], [("ldt", q, q + 1)], T.ldt[q], T.th[:])
-    dma("s", "stg_c1", [], [("stc1", 0, 8)], T.stc1[:], T.cand[:, 512:1024])
-    dma("s", "own_c1", [], [("ldc1", q, q + 1)], T.ldc1[q], T.cand[16 * q:16 * q + 16, 512:1024])
-    send("t", lambda d: T.stt[:])
-    send("c1", lambda d: T.stc1[d])
 
     def ap(b):
         return T[b[0]][:, b[1]:b[2]]
 
-    def ts(out, in0, s1, s2, o0, o1=None, extra=()):
+    def val(x):
+        return ap(x) if isinstance(x, tuple) else x
+
+    def aps(*xs):
+        return [x for x in xs if isinstance(x, tuple)]
+
+    def ts(out, in0, s1, s2, o0, o1=None):
         if o1 is None:
-            op("v", [in0] + list(extra), [out], lambda e: e.tensor_scalar(ap(out), ap(in0), s1, None, o0))
+            op("v", aps(in0, s1), [out], lambda e: e.tensor_scalar(ap(out), ap(in0), val(s1), None, o0))
         else:
-            op("v", [in0] + list(extra), [out], lambda e: e.tensor_scalar(ap(out), ap(in0), s1, s2, o0, o1))
+            op("v", aps(in0, s1, s2), [out], lambda e: e.tensor_scalar(ap(out), ap(in0), val(s1), val(s2), o0, o1))
 
     def tt(out, in0, in1, o):
         op("v", [in0, in1], [out], lambda e: e.tensor_tensor(ap(out), ap(in0), ap(in1), o))
@@ -202,235 +217,396 @@ def rank_program(g, core, T, topo):
     def fill(out, c):
         op("v", [], [out], lambda e: e.memset(ap(out), c))
 
-    def act(out, in_, scale=1.0, bias=0.0, extra=()):
-        op("a", [in_] + list(extra), [out], lambda e: e.activation(ap(out), ap(in_), AF.Identity, bias=bias, scale=scale))
+    def act(out, in_, scale=1.0, bias=0.0, func=AF.Identity):
+        op("a", aps(in_, bias), [out], lambda e: e.activation(ap(out), ap(in_), func, bias=val(bias), scale=scale))
 
-    def act_gather(out, win, lst, bias=0.0, scale=1.0):
-        op("a", [win, lst], [out],
-           lambda e: e.activation(ap(out), ap(win).indirect(ap(lst)), AF.Identity, bias=bias, scale=scale))
+    def gather(qn, out, win, lst, bias=0.0):
+        if qn == "a":
+            op("a", [win, lst], [out],
+               lambda e: e.activation(ap(out), ap(win).indirect(ap(lst)), AF.Identity, bias=bias, scale=1.0))
+        else:
+            op("v", [win, lst], [out], lambda e: e.tensor_scalar(ap(out), ap(win).indirect(ap(lst)), bias, None, A.add))
 
     def tt_gather(out, win, lst, in1, o):
         op("v", [win, lst, in1], [out], lambda e: e.tensor_tensor(ap(out), ap(win).indirect(ap(lst)), ap(in1), o))
 
-    fill(("ones", 0, V), 1.0)
-    op("v", [("ones", 0, V)], [("cio", 0, V)],
-       lambda e: e.tensor_tensor_scan(T.cio[:], T.ones[:], T.ones[:], -1.0, A.add, A.mult))
-    ts(("pi", 1, 2), ("pi", 0, 1), 15, None, A.bitwise_and)
-    ts(("pi", 2, 3), ("pi", 0, 1), 4, None, A.arith_shift_right)
-    copy(("pf", 0, 3), ("pi", 0, 3))
-    ts(("pf", 3, 4), ("pf", 1, 2), -1.0, 255.0, A.mult, A.add)
-    pcol, c16, bcol, k255 = (T.pf[:, k:k + 1] for k in range(4))
-    pfr = [("pf", 0, 4)]
-    copy(("mi", 0, 128), ("cio", 0, 128))
-    ts(("eye", 0, 128), ("cio", 0, 128), pcol, None, A.is_equal, extra=pfr)
-    ts(("cm", 0, 16), ("cio", 0, 16), c16, -2048.0, A.is_equal, A.mult, extra=pfr)
-    ts(("sm", 0, 8), ("cio", 0, 8), 16.0, pcol, A.mult, A.is_equal, extra=pfr)
-    ts(("rc", 0, 80), ("cio", 0, 80), 16.0, c16, A.mult, A.add, extra=pfr)
-    ts(("mj", 0, 128), ("mi", 0, 128), 31, None, A.bitwise_and)
-    copy(("mf", 0, 128), ("mj", 0, 128))
-    ts(("nv", 0, 128), ("mf", 0, 128), -16.0, k255, A.mult, A.add, extra=pfr)
-    ts(("ni", 0, 128), ("eye", 0, 128), -2048.0, None, A.mult)
-    for i in range(16):
-        ts(("dsel", 128 * i, 128 * i + 128), ("eye", 0, 128), T.cm[:, i:i + 1], None, A.mult, extra=[("cm", 0, 16)])
-    fill(("xl", R, XW), D)
-    fill(("xh", R, XW), -1.0)
-    copy(("ru", 0, 320), ("ri", 0, 320))
-    ts(("mi", 0, 128), ("mi", 0, 128), 4, None, A.arith_shift_right)
-    copy(("mg", 0, 128), ("mi", 0, 128))
-    ts(("bones", 0, 128), ("mg", 0, 128), bcol, None, A.is_equal, extra=pfr)
-    fill(("c96", 0, 512), float(CAP))
-    fill(("pre", 7, 8), 0.0)
-    copy(("rf", 0, 320), ("ri", 0, 320))
-    tt(("rd", 0, 240), ("rf", 80, 320), ("rf", 0, 240), A.subtract)
-    copy(("cu0", 0, 512), ("ci0", 0, 512))
-    copy(("cf0", 0, 512), ("ci0", 0, 512))
+    def mms(out, rd, pairs):
+        n = len(pairs)
+        ops("t", rd, [out], [lambda e, k=k, l=l, r=r: e.matmul(ap(out), l, r, k == 0, k == n - 1)
+                             for k, (l, r) in enumerate(pairs)])
 
-    def extract(bank, ncol, buf, base, with_v):
-        fns = []
-        for i in range(16):
-            fns.append(lambda e, i=i: e.matmul(T[bank][:, 0:ncol], T.dsel[:, 128 * i:128 * i + 128],
-                                               T[buf][:, base + i:base + 16 * ncol:16], i == 0, (not with_v) and i == 15))
-        rd = [("dsel", 0, 2048), (buf, base, base + 16 * ncol)]
-        if with_v:
-            fns.append(lambda e: e.matmul(T[bank][:, 0:ncol], T.ni[:], T.nv[:, 0:ncol], False, True))
-            rd += [("ni", 0, 128), ("nv", 0, 128)]
-        ops("t", rd, [(bank, 0, 512)], fns)
+    fill(("one", 0, 256), 1.0)
+    op("v", [("one", 0, 256)], [("cio", 0, 256)],
+       lambda e: e.tensor_tensor_scan(T.cio[:, 0:256], T.one[:], T.one[:], -1.0, A.add, A.mult))
+    ts(("cio", 256, 512), ("cio", 0, 256), 256.0, None, A.add)
+    for k in range(1, 5):
+        act(("cio", 512 * k, 512 * k + 512), ("cio", 0, 512), bias=512.0 * k)
+    ts(("cio", 2560, 3072), ("cio", 0, 512), 2560.0, None, A.add)
+    cols, allc = ("cio", 0, 128), 129
+    copy(("mi", 0, 128), cols)
 
-    def reduce_ranks(b, o, last):
-        act(("pp", 0, 1024), (b, 0, 1024))
-        act(("pp", 1024, 2048), (b, 1024, 2048))
-        tt(("s1", 0, 1024), ("pp", 0, 1024), (b, 2048, 3072), o)
-        tt(("pp", 0, 1024), ("pp", 1024, 2048), (b, 3072, 4096), o)
-        tt(("s2", 0, 512), ("pp", 0, 512), ("s1", 0, 512), o)
-        tt(("pp", 1024, 1536), ("pp", 512, 1024), ("s1", 512, 1024), o)
-        tt(last, ("pp", 1024, 1536), ("s2", 0, 512), o)
+    def bits(to, shift, mask):
+        ts((to, 0, allc), ("mi", 0, allc), shift, mask, A.arith_shift_right, A.bitwise_and)
 
-    def relayout(s, b, to, p, split):
-        for o in (2 * p, 2 * p + 1):
-            for a in range(8):
-                qn = "a" if split and o % 2 else "s"
-                dma(qn, s, [(b, 512 * o, 512 * o + 512)], [(to, 512 * a, 512 * a + 512)],
-                    T[to][16 * o:16 * o + 16, 512 * a:512 * a + 512], T[b][16 * a:16 * a + 16, 512 * o:512 * o + 512])
+    def col(k):
+        return ("pf", k, k + 1)
 
-    for t in range(RO):
-        cu, cf = "cu%d" % t, "cf%d" % t
-        lst = "ru" if t == 0 else "lq"
+    pcol, c16, k255, g16, dcol, tcol, hcol = (col(k) for k in range(7))
+    copy(pcol, ("mi", 128, 129))
+    bits("ma", 0, 15)
+    copy(c16, ("ma", 128, 129))
+    ts(k255, c16, -1.0, 255.0, A.mult, A.add)
+    ts(col(8), c16, -1000.0, pcol, A.mult, A.add)
+    ts(dcol, col(8), 16.0, None, A.add)
+    ts(("wd", 0, 144), ("cio", 0, 144), dcol, -2048.0, A.is_equal, A.mult)
+    ts(("ni", 0, 128), cols, pcol, -2048.0, A.is_equal, A.mult)
+    bits("ma", 0, 31)
+    ts(("nv", 0, 128), ("ma", 0, 128), -16.0, k255, A.mult, A.add)
 
-        def see(qn, j, k):
+    def constants():
+        ts(("nh", 0, 128), cols, pcol, -0.5, A.is_equal, A.mult)
+        act(("pb", 0, 1), c16, scale=math.log(2.0), func=AF.Exp)
+        ts(col(9), c16, -1.0, pcol, A.mult, A.add)
+        ts(g16, col(9), 16.0, None, A.add)
+        copy(col(12), ("pb", 0, 1))
+        ts(("wf", 0, 144), ("cio", 0, 144), g16, col(12), A.is_equal, A.mult)
+        ts(hcol, c16, 0.0, 0.5, A.is_equal, A.mult)
+        ts(("t1", 0, 80), ("cio", 0, 80), 16.0, c16, A.mult, A.add)
+        ts(("rc", 0, 80), ("t1", 0, 80), 1.0 / S, None, A.mult)
+        ts(("rc", 80, 160), ("t1", 0, 80), 1.0 / S, 3.0, A.mult, A.add)
+        bits("ma", 5, 3)
+        bits("mc", 0, 1)
+        ts(("mf", 0, allc), ("ma", 0, allc), 2.0, None, A.mult)
+        tt(("mf", 0, allc), ("mf", 0, allc), ("mc", 0, allc), A.add)
+        ts(("bones", 0, 128), ("mf", 0, 128), ("mf", 128, 129), None, A.is_equal)
+        bits("mb", 4, 1)
+        ts(col(10), ("ma", 128, 129), 32.0, None, A.mult)
+        ts(col(11), c16, 2.0, col(10), A.mult, A.add)
+        tt(tcol, col(11), ("mb", 128, 129), A.add)
+        ts(("mv", 0, 128), cols, tcol, None, A.is_equal)
+        bits("ma", 2, 3)
+        bits("mb", 1, 1)
+        ts(("mf", 0, 128), ("ma", 0, 128), 32.0, None, A.mult)
+        tt(("mf", 0, 128), ("mf", 0, 128), ("mb", 0, 128), A.add)
+        ts(("mg", 0, 128), ("mf", 0, 128), pcol, None, A.is_equal)
+        tt(("lm", 128, 256), ("mg", 0, 128), ("mc", 0, 128), A.mult)
+        tt(("lm", 0, 128), ("mg", 0, 128), ("lm", 128, 256), A.subtract)
+        ts(("lm", 256, 512), ("lm", 0, 256), -1.0, None, A.mult)
+        for k in range(4):
+            act(("xs", k * S + R, k * S + S), ("cio", 0, S - R))
+        for b, at, c in (("xs", 0, D), ("xs", 4 * S, D), ("xh", 0, -1.0)):
+            fill((b, at + R, at + XW), c)
+        fill(("c96", 0, 512), float(CAP))
+        fill(("pre", 15, 16), 0.0)
+
+    def extract(out, w, buf, base, extra):
+        n = out[2] - out[1]
+        tr = [(T[w][:, 16 - i:144 - i], T[buf][:, base + i:base + 16 * n:16]) for i in range(16)]
+        mms(out, [(w, 0, 144), (buf, base, base + 16 * n), (extra[0], 0, 128), extra[1]],
+            tr + [(T[extra[0]][:], ap(extra[1]))])
+
+    def prepare(src, parts):
+        ts(("ub", 0, 240), src, 8, None, A.arith_shift_right)
+        ts(("ua", 0, 240), src, 255, None, A.bitwise_and)
+        op("v", [("ub", 0, 240)], [("bf", 0, 240)], lambda e: e.tensor_copy(T.bf[:], T.ub[:]))
+        copy(("uu", 0, 240), ("ua", 0, 240))
+        n = 80 // parts
+        for h in range(parts):
+            op("a", [("bf", 0, 240)], [("pw", 3 * n * h, 3 * n * h + 3 * n)],
+               lambda e: e.activation(T.pw[:, 3 * n * h:3 * n * h + 3 * n], T.bf[:, :, n * h:n * h + n], AF.Exp, bias=0.0,
+                                      scale=-math.log(2.0)))
+        op("a", [("bf", 0, 240)], [("p2", 0, 240)],
+           lambda e: e.activation(T.p2[:], T.bf[:], AF.Exp, bias=0.0, scale=math.log(2.0)))
+
+    def slots(t):
+        return [S * k for k in range(4)] if t == 0 else [S * (4 - k) for k in range(4)]
+
+    def rest(qn, lst, a, b):
+        gather(qn, ("wr", 16 * a, 16 * b), ("cio", 0, V), (lst, a, b))
+
+    def see(t, qn, j, *ks):
+        for k in ks:
             b = 2048 * (j // 2) + 512 * k
             c = 256 * (j % 2) + b // 16
-            out, win, off = ("wg", 2048 * j + 512 * k, 2048 * j + 512 * k + 512), ("wr", 0, R), (cu, c, c + 32)
-            if qn == "a":
-                act_gather(out, win, off, -(b + 255.0))
-            else:
-                op("v", [win, off], [out],
-                   lambda e: e.tensor_scalar(ap(out), ap(win).indirect(ap(off)), b + 255.0, None, A.subtract))
+            gather(qn, ("wg", 2048 * j + 512 * k, 2048 * j + 512 * k + 512), ("wr", 0, R), ("cu%d" % t, c, c + 32), -(b + 255.0))
 
-        def lists(j):
-            h, m = j // 2, j % 2
-            tt(("tm", 128 * j, 128 * j + 128), ("z%d" % j, 0, 128), (cf, 256 * m + 128 * h, 256 * m + 128 * h + 128), A.max)
-            ts(("off", 128 * j, 128 * j + 128), ("tm", 128 * j, 128 * j + 128), float(R), None, A.min)
+    def seen(j):
+        extract(("z%d" % j, 0, 128), "wd", "wg", 2048 * j, ("ni", ("nv", 0, 128)))
 
-        def first(b, x, p):
+    def lists(t, j):
+        c = 256 * (j % 2) + 128 * (j // 2)
+        tt(("tm", 128 * j, 128 * j + 128), ("z%d" % j, 0, 128), ("ci%d" % t, c, c + 128), A.max)
+        ts(("off", 128 * j, 128 * j + 128), ("tm", 128 * j, 128 * j + 128), float(R), None, A.min)
+
+    def ship(h):
+        c, cs = "o%d" % h, slice(256 * h, 256 * h + 256)
+        dma("s", "stg_" + c, [("off", cs.start, cs.stop)], [("st" + c, 0, 8)], T["st" + c][:], T.off[:, cs])
+        dma("s", "get_" + c, [("off", cs.start, cs.stop)], [("of0", cs.start, cs.stop)], T.of0[mine, cs], T.off[mine, cs])
+        send(c, lambda d: T["st" + c][d])
+
+    def twin(t, qn):
+        a = slots(t)[0]
+        dma(qn, "xc%d" % t, [("xs", a, a + R)], [("xh", 0, R)], T.xh[:, 0:R], T.xs[:, a:a + R])
+
+    def window(t, b):
+        return ("xs", slots(t)[0], slots(t)[0] + XW) if b == "lo" else ("xh", 0, XW)
+
+    def first(t, b, *ps):
+        for p in ps:
             c = 256 * (p // 2) + 64 * (p % 2)
-            act_gather((b, 1024 * p, 1024 * p + 1024), (x, 0, XW), ("off", c, c + 64))
+            gather("a", (b, 1024 * p, 1024 * p + 1024), window(t, b), ("off" if t else "of0", c, c + 64))
 
-        def second(b, x, p, o):
+    def second(t, b, *ps):
+        for p in ps:
             c = 256 * (p // 2) + 128 + 64 * (p % 2)
-            tt_gather((b, 1024 * p, 1024 * p + 1024), (x, 0, XW), ("off", c, c + 64), (b, 1024 * p, 1024 * p + 1024), o)
+            blk, to = (b, 1024 * p, 1024 * p + 1024), "b" + b[0]
+            tt_gather(blk, window(t, b), ("off" if t else "of0", c, c + 64), blk, A.min if b == "lo" else A.max)
+            for a in range(8):
+                dma("s", "r%s%d" % (b[0], t), [blk], [(to, 512 * a, 512 * a + 512)],
+                    T[to][32 * p:32 * p + 32, 512 * a:512 * a + 512], T[b][grp(a), blk[1]:blk[2]])
 
-        act_gather(("wr", 0, R), ("cio", 0, V), (lst, 0, 80))
-        for k in range(4):
-            see("a", 0, k)
-            see("v", 1, k)
-        extract("z0", 128, "wg", 0, True)
-        extract("z1", 128, "wg", 2048, True)
-        for k in range(4):
-            see("a", 2, k)
-        see("a", 3, 0)
-        extract("z2", 128, "wg", 4096, True)
-        if t == 0:
-            copy(("xl", 0, R), ("xs", 0, R))
-        see("v", 3, 1)
-        lists(0)
-        first("lo", "xl", 0)
-        see("v", 3, 2)
-        see("v", 3, 3)
-        extract("z3", 128, "wg", 6144, True)
-        first("lo", "xl", 1)
-        lists(1)
+    def lift(b):
+        act(("pp", 0, 1024), (b, 0, 1024))
+        act(("pp", 1024, 2048), (b, 1024, 2048))
 
-        second("lo", "xl", 0, A.min)
-        relayout("rl%d" % t, "lo", "bl", 0, False)
-        lists(2)
-        second("lo", "xl", 1, A.min)
-        relayout("rl%d" % t, "lo", "bl", 1, False)
-        lists(3)
-        for p in (2, 3):
-            first("lo", "xl", p)
-            second("lo", "xl", p, A.min)
-            relayout("rl%d" % t, "lo", "bl", p, False)
-        act(("xh", 0, R), ("xl", 0, R))
-        for p in range(4):
-            first("hi", "xh", p)
-        for p in range(4):
-            second("hi", "xh", p, A.max)
-            if p < 3:
-                relayout("rh%d" % t, "hi", "bh", p, False)
-        reduce_ranks("bl", A.min, ("lof", 0, 512))
-        relayout("rh%d" % t, "hi", "bh", 3, True)
-        act(("x5", 0, R), ("xl", 0, R), scale=1.25)
-        if t == 0:
-            dma("s", "get_t", [("ldt", 0, 8)], [("thi", 0, 1)], T.thi[:], T.ldt[:, 16 * q:16 * q + 16, :])
-            copy(("thf", 0, 1), ("thi", 0, 1))
-            for o in range(8):
-                ts(("selo", 128 * o, 128 * o + 128), ("cio", 0, 128), 0.0, T.sm[:, o:o + 1], A.is_ge, A.mult,
-                   extra=[("sm", 0, 8)])
-        else:
-            copy(("xs", 0, R), ("xl", 0, R))
+    def fold(b, o, last):
+        return [lambda: tt(("s1", 0, 1024), ("pp", 0, 1024), (b, 2048, 3072), o),
+                lambda: tt(("pp", 0, 1024), ("pp", 1024, 2048), (b, 3072, 4096), o),
+                lambda: tt(("s2", 0, 512), ("pp", 0, 512), ("s1", 0, 512), o),
+                lambda: tt(("pp", 1024, 1536), ("pp", 512, 1024), ("s1", 512, 1024), o),
+                lambda: tt(last, ("pp", 1024, 1536), ("s2", 0, 512), o)]
+
+    def spread(t):
         act(("fb", 0, 512), ("lof", 0, 512), scale=-0.25, bias=-0.375)
-        act(("lt", 0, 512), ("lof", 0, 512), bias=T.thf[:, 0:1], extra=[("thf", 0, 1)])
-        for o in range(8):
-            dma("s", "fs%d" % t, [("fb", 0, 512)], [("fd", 512 * o, 512 * o + 512)],
-                T.fd[:, 512 * o:512 * o + 512], T.fb[16 * o:16 * o + 16, :])
         for a in range(8):
-            dma("s", "fg%d" % t, [("fd", 0, V)], [("ones", 0, V)], T.ones[16 * a:16 * a + 16, :], T.fd[:])
-        if t == 0:
-            dma("s", "get_c1", [("ldc1", 0, 8)], [("ci1", 0, 512)], T.ci1[:], T.ldc1[:])
-        reduce_ranks("bh", A.max, ("pp", 1536, 2048))
+            for p in range(4):
+                dma("s", "fg%d" % t, [("fb", 0, 512)], [("et", 1024 * p, 1024 * p + 1024)],
+                    T.et[grp(a), 1024 * p:1024 * p + 1024], T.fb[32 * p:32 * p + 32, :])
 
-        tt(("far", 0, 512), ("pp", 1536, 2048), ("lt", 0, 512), A.is_gt)
-        ops("t", [("bones", 0, 128), ("far", 0, 512)], [("z0", 0, 512)],
-            [lambda e: e.matmul(T.z0[:], T.bones[:], T.far[:], True, True)])
+    def weave(*chains):
+        for k in range(max(len(c) for c in chains)):
+            for c in chains:
+                if k < len(c):
+                    c[k]()
+
+    def count():
+        tt(("far", 0, 512), ("z3", 0, 512), ("lt", 0, 512), A.is_gt)
+        mms(("z0", 0, 512), [("bones", 0, 128), ("far", 0, 512)], [(T.bones[:], T.far[:])])
+
+    def carve():
         ts(("odd", 0, 512), ("z0", 0, 512), float(NEED), None, A.is_ge)
-        op("v", [("odd", 0, 512), ("c96", 0, 512)], [("pre", 8, 520)],
-           lambda e: e.tensor_tensor_scan(T.pre[:, 8:520], T.odd[:], T.c96[:], 0.0, A.add, A.min))
-        tt(("cv", 0, 512), ("pre", 8, 520), ("pre", 7, 519), A.subtract)
-        for o in range(8):
-            z = "z%d" % (o % 4)
-            ops("t", [("selo", 128 * o, 128 * o + 128), ("cv", 0, 512)], [(z, 0, 512)],
-                [lambda e, z=z, o=o: e.matmul(T[z][:], T.selo[:, 128 * o:128 * o + 128], T.cv[:], True, True)])
-            act(("ft", 512 * o, 512 * o + 512), (z, 0, 512))
+        op("v", [("odd", 0, 512), ("c96", 0, 512)], [("pre", 16, 528)],
+           lambda e: e.tensor_tensor_scan(T.pre[:, 16:528], T.odd[:], T.c96[:], 0.0, A.add, A.min))
+        mms(("z2", 0, 256), [("lm", 0, 512), ("pre", 0, 528)],
+            [(T.lm[:, 128 * k:128 * k + 128], T.pre[:, 16 - k // 2 + 256 * (k % 2):272 - k // 2 + 256 * (k % 2)])
+             for k in range(4)])
 
-        for s in range(H):
-            act_gather(("fl", R * s, R * s + R), ("ft", 0, V), (lst, 80 * s, 80 * s + 80), scale=-1.0 / 2048.0)
-            extract("z%d" % s, 80, "fl", R * s, False)
-        for s in range(H):
-            tt_gather(("yb", 0, R), ("ones", 0, V), (lst, 80 * s, 80 * s + 80), ("x5", 0, R), A.add)
-            ts(("xs", R * s + R, R * s + 2 * R), ("yb", 0, R), 0.0, float(TOP), A.max, A.min)
-            if s < H - 1:
-                ts(("x5", 0, R), ("xs", R * s + R, R * s + 2 * R), 1.25, None, A.mult)
-            if t == 0 and s == 0:
-                copy(("cu1", 0, 512), ("ci1", 0, 512))
-                copy(("cf1", 0, 512), ("ci1", 0, 512))
-        e1, e2, e3 = ("ef", 0, 80), ("ef", 80, 160), ("ef", 160, 240)
-        copy(e1, ("z0", 0, 80))
-        tt(e2, ("z1", 0, 80), e1, A.mult)
-        tt(e3, ("z2", 0, 80), e2, A.mult)
-        if t == 0:
-            tt(("eg", 0, 240), ("ef", 0, 240), ("rd", 0, 240), A.mult)
-            tt(("t1", 0, 80), ("eg", 0, 80), ("rf", 0, 80), A.add)
-            tt(("t2", 0, 80), ("eg", 80, 160), ("eg", 160, 240), A.add)
-            tt(("lf", 0, 80), ("t1", 0, 80), ("t2", 0, 80), A.add)
-            copy(("lq", 0, 80), ("lf", 0, 80))
-        tt(("k2", 0, 80), e1, e2, A.add)
-        tt(("kk", 0, 80), ("k2", 0, 80), e3, A.add)
-        ts(("t4", 0, 80), ("kk", 0, 80), float(R), None, A.mult)
-        tt(("t4", 0, 80), ("t4", 0, 80), ("rc", 0, 80), A.add)
-        copy(("so", 0, 80), ("t4", 0, 80))
+    def table():
+        act(("ft", 0, 256), ("z2", 0, 256), bias=hcol)
 
-        def pick(to, h):
-            op("v", [("xs", 0, 4 * R), ("so", 0, 80)], [(to, 640 * h, 640 * h + 640)],
-               lambda e: e.tensor_copy(T[to][:, 640 * h:640 * h + 640], T.xs[:].indirect(T.so[:, 40 * h:40 * h + 40])))
+    def step(t, s, h):
+        a, b, to = 640 * h, 640 * h + 640, slots(t)[s + 1]
+        return [lambda: tt_gather(("yi", a, b), ("et", 0, V), ("lq%d" % t, 80 * s + 40 * h, 80 * s + 40 * h + 40),
+                                  ("x5", a, b), A.add),
+                lambda: ts(("xs", to + a, to + b), ("yi", a, b), 0.0, float(TOP), A.max, A.min)]
 
-        if t == 0:
-            pick("xl", 0)
-            pick("xl", 1)
-            tt(("t1", 0, 80), e1, ("rd", 80, 160), A.mult)
-            tt(("t2", 0, 80), e2, ("rd", 160, 240), A.mult)
-            tt(("t3", 0, 80), e1, ("rd", 160, 240), A.mult)
-            tt(("t1", 0, 80), ("t1", 0, 80), ("rf", 80, 160), A.add)
-            tt(("lf", 80, 160), ("t1", 0, 80), ("t2", 0, 80), A.add)
-            tt(("lf", 160, 240), ("t3", 0, 80), ("rf", 160, 240), A.add)
-            copy(("lq", 80, 240), ("lf", 80, 240))
-            copy(("cu", 0, 80), ("kk", 0, 80))
-        else:
-            pick("xf", 0)
-            dma("s", "stg_y0", [("xf", 0, 640)], [("sty0", 0, 8)], T.sty0[:], T.xf[:, 0:640])
-            pick("xf", 1)
-            dma("a", "stg_y1", [("xf", 640, R)], [("sty1", 0, 8)], T.sty1[:], T.xf[:, 640:R])
-            tt(("t1", 0, 80), ("cu", 0, 80), ("kk", 0, 80), A.add)
-            ts(("cn", 0, 80), ("t1", 0, 80), 3.0, None, A.min)
+    def five(t, s, h):
+        a, b, at = 640 * h, 640 * h + 640, slots(t)[s]
+        act(("x5", a, b), ("xs", at + a, at + b), scale=1.25)
+
+    def flags(qn, s, a, b):
+        gather(qn, ("fl", R * s + 16 * a, R * s + 16 * b), ("ft", 0, 256), ("uu", 80 * s + a, 80 * s + b))
+
+    def flagged(z, s, a, b):
+        extract((z, (b - a) * s, (b - a) * (s + 1)), "wf", "fl", R * s + 16 * a, ("nh", ("p2", 80 * s + a, 80 * s + b)))
+
+    def tests(at, n):
+        return [("ef", at + n * s, at + n * s + n) for s in range(3)]
+
+    def bit_test(z, at, n):
+        e1, e2, e3 = tests(at, n)
+        return [lambda: tt(("ua", at, at + 3 * n), (z, 0, 3 * n), ("pw", at, at + 3 * n), A.mult),
+                lambda: ts(("ef", at, at + 3 * n), ("ua", at, at + 3 * n), 1, None, A.bitwise_and),
+                lambda: tt(e2, e2, e1, A.mult),
+                lambda: tt(e3, e3, e2, A.mult)]
+
+    def choose(t, es, a, b):
+        o = A.subtract if t else A.add
+        return [lambda: (tt(("t3", a, b), ("rc", 80 * t + a, 80 * t + b), es[0], o), tt(("t4", a, b), es[1], es[2], A.add)),
+                lambda: tt(("t3", a, b), ("t3", a, b), ("t4", a, b), o),
+                lambda: ts(("so", a, b), ("t3", a, b), float(S), None, A.mult)]
+
+    def pick(t, qn, h):
+        to, w = (("xf", 0), S) if t else (("xs", 4 * S), 0)
+        gather(qn, (to[0], to[1] + 640 * h, to[1] + 640 * h + 640), ("xs", w, w + 3 * S + R), ("so", 40 * h, 40 * h + 40))
+
+    copy(("lh", 0, 80), ("rh", 0, 80))
+    rest("a", "lh", 0, 40)
+    copy(("cu0", 0, 512), ("ci0", 0, 512))
+    rest("v", "lh", 40, 80)
+    see(0, "a", 0, 0, 1, 2, 3)
+    see(0, "v", 1, 0, 1, 2, 3)
+    seen(0)
+    seen(1)
+    see(0, "a", 2, 0, 1, 2, 3)
+    see(0, "v", 3, 0, 1)
+    lists(0, 0)
+    lists(0, 1)
+    ship(0)
+    see(0, "v", 3, 2, 3)
+    seen(2)
+    seen(3)
+    lists(0, 2)
+    lists(0, 3)
+    ship(1)
+    dma("s", "get_p", [], [("pxi", 0, R)], T.pxi[mine, :], T.px[mine, :])
+    fetch("s", "p", "pxi", slice(0, R))
+    constants()
+    copy(("xs", 0, R), ("pxi", 0, R))
+    twin(0, "a")
+    fetch("s", "o0", "of0", slice(0, 256))
+    fetch("s", "o1", "of0", slice(256, 512))
+    dma("s", "stg_t", [], [("stt", 0, 8)], T.stt[:], T.th[:])
+    dma("s", "own_t", [], [("ldt", q, q + 1)], T.ldt[q], T.th[:])
+    stage("s", "r", T.ray, slice(0, 320))
+    dma("s", "get_r", [], [("ri", 0, 320)], T.ri[mine, :], T.ray[mine, :])
+    send("t", lambda d: T.stt[:])
+    send("r", lambda d: T["str"][d])
+    first(0, "lo", 0, 1, 2, 3)
+    second(0, "lo", 0, 1, 2, 3)
+    dma("s", "get_t", [("ldt", 0, 8)], [("thi", 0, 1)], T.thi[:], T.ldt[:, mine, :])
+    fetch("s", "r", "ri", slice(0, 320))
+    first(0, "hi", 0, 1, 2, 3)
+    second(0, "hi", 0, 1, 2, 3)
+    stage("s", "c1", T.cand, slice(512, 1024))
+    dma("s", "get_c1", [], [("ci1", 0, 512)], T.ci1[mine, :], T.cand[mine, 512:1024])
+    send("c1", lambda d: T.stc1[d])
+    lift("bl")
+    five(0, 0, 0)
+    five(0, 0, 1)
+    copy(("thn", 0, 1), ("thi", 0, 1))
+    copy(("thn", 1, 2), ("thi", 0, 1))
+    mms(("z0", 0, 2), [("mv", 0, 128), ("thn", 0, 2)], [(T.mv[:], T.thn[:])])
+    weave(fold("bl", A.min, ("lof", 0, 512)),
+          [lambda: None, lambda: copy(("thf", 0, 2), ("z0", 0, 2)), lambda: None, lambda: copy(("lq0", 0, 240), ("ri", 0, 240))])
+    spread(0)
+    fetch("s", "c1", "ci1", slice(0, 512))
+    lift("bh")
+    act(("lt", 0, 512), ("lof", 0, 512), bias=("thf", 0, 1))
+    prepare(("ri", 0, 240), 1)
+    weave(fold("bh", A.max, ("z3", 0, 512)))
+    count()
+    tt(("rd", 0, 240), ("ri", 80, 320), ("ri", 0, 240), A.subtract)
+    carve()
+    table()
+    for s in range(3):
+        flags("a", s, 0, 40)
+        flags("v", s, 40, 80)
+        flagged("z0" if s == 2 else "z1", s, 0, 80)
+    e1, e2, e3 = es = tests(0, 80)
+    weave([lambda: tt(("ua", 0, 160), ("z1", 0, 160), ("pw", 0, 160), A.mult),
+           lambda: ts(("ef", 0, 160), ("ua", 0, 160), 1, None, A.bitwise_and),
+           lambda: (tt(e2, e2, e1, A.mult), tt(("t1", 0, 80), e1, ("rd", 0, 80), A.mult),
+                    tt(("ua", 160, 240), ("z0", 160, 240), ("pw", 160, 240), A.mult)),
+           lambda: (tt(("eg", 80, 160), e2, ("rd", 80, 160), A.mult), tt(("t1", 0, 80), ("t1", 0, 80), ("ri", 0, 80), A.add),
+                    ts(e3, ("ua", 160, 240), 1, None, A.bitwise_and), tt(("t2", 0, 80), e2, ("rd", 160, 240), A.mult)),
+           lambda: (tt(("t1", 0, 80), ("t1", 0, 80), ("eg", 80, 160), A.add), tt(("t2", 0, 80), ("t2", 0, 80), e3, A.mult)),
+           lambda: tt(("li", 0, 80), ("t1", 0, 80), ("t2", 0, 80), A.add),
+           lambda: copy(("lq1", 0, 80), ("li", 0, 80))],
+          [lambda k=k: copy(("cu1", 128 * k, 128 * k + 128), ("ci1", 128 * k, 128 * k + 128)) for k in range(2)]
+          + [lambda: None] * 2 + [lambda: tt(e3, e3, e2, A.mult), lambda: copy(("cu1", 256, 512), ("ci1", 256, 512))])
+
+    rest("a", "lq1", 0, 80)
+    weave(step(0, 0, 0), step(0, 0, 1))
+    see(1, "a", 0, 0)
+    five(0, 1, 0)
+    five(0, 1, 1)
+    see(1, "v", 1, 0)
+    see(1, "a", 0, 1, 2)
+    weave(step(0, 1, 0), step(0, 1, 1))
+    see(1, "a", 0, 3)
+    seen(0)
+    five(0, 2, 0)
+    five(0, 2, 1)
+    see(1, "v", 1, 1)
+    see(1, "a", 1, 2, 3)
+    seen(1)
+    see(1, "a", 2, 0, 1, 2, 3)
+    seen(2)
+    weave(choose(0, es, 0, 80), step(0, 2, 0), step(0, 2, 1))
+    lists(1, 0)
+    pick(0, "v", 0)
+    pick(0, "v", 1)
+    twin(1, "s")
+    see(1, "a", 3, 0, 1)
+    first(1, "lo", 0)
+    lists(1, 1)
+    see(1, "v", 3, 2, 3)
+    seen(3)
+    first(1, "lo", 1)
+    second(1, "lo", 0)
+    lists(1, 2)
+    first(1, "lo", 2, 3)
+    second(1, "lo", 1)
+    lists(1, 3)
+    second(1, "lo", 2, 3)
+    first(1, "hi", 0, 1, 2, 3)
+    second(1, "hi", 0, 1, 2, 3)
+    lift("bl")
+    five(1, 0, 0)
+    five(1, 0, 1)
+    weave(fold("bl", A.min, ("lof", 0, 512)),
+          [lambda: (tt(("cu", 0, 80), ("t4", 0, 80), e1, A.add), tt(("t3", 0, 80), e1, ("rd", 160, 240), A.mult)),
+           lambda: tt(("eg", 0, 160), ("ef", 0, 160), ("rd", 80, 240), A.mult),
+           lambda: tt(("li", 160, 240), ("t3", 0, 80), ("ri", 160, 240), A.add),
+           lambda: tt(("t1", 0, 80), ("eg", 0, 80), ("eg", 80, 160), A.add)])
+    spread(1)
+    lift("bh")
+    act(("lt", 0, 512), ("lof", 0, 512), bias=("thf", 0, 1))
+    tt(("li", 80, 160), ("t1", 0, 80), ("ri", 80, 160), A.add)
+    prepare(("li", 0, 240), 2)
+    weave(fold("bh", A.max, ("z3", 0, 512)))
+    count()
+    copy(("lq1", 80, 240), ("li", 80, 240))
+    carve()
+    table()
+
+    for s in range(3):
+        flags("a", s, 0, 40)
+        flagged("z1", s, 0, 40)
+    weave(step(1, 0, 0), step(1, 0, 1))
+    five(1, 1, 0)
+    five(1, 1, 1)
+    flags("a", 0, 40, 80)
+    flagged("z3", 0, 40, 80)
+    es, later = tests(0, 40), tests(120, 40)
+    weave(bit_test("z1", 0, 40), step(1, 1, 0) + step(1, 1, 1))
+    five(1, 2, 0)
+    flags("a", 1, 40, 80)
+    flagged("z3", 1, 40, 80)
+    five(1, 2, 1)
+    flags("a", 2, 40, 80)
+    flagged("z3", 2, 40, 80)
+    weave(choose(1, es, 0, 40), step(1, 2, 0))
+    pick(1, "a", 0)
+    dma("a", "stg_y0", [("xf", 0, 640)], [("sty0", 0, 8)], T.sty0[:], T.xf[:, 0:640])
+    weave(step(1, 2, 1) + [lambda: tt(("t1", 0, 40), ("cu", 0, 40), es[0], A.add)],
+          bit_test("z3", 120, 40) + choose(1, later, 40, 80))
+    pick(1, "a", 1)
+    dma("a", "stg_y1", [("xf", 640, R)], [("sty1", 0, 8)], T.sty1[:], T.xf[:, 640:R])
+    tt(("t1", 40, 80), ("cu", 40, 80), later[0], A.add)
+    tt(("t1", 0, 80), ("t1", 0, 80), ("t4", 0, 80), A.add)
+    ts(("cn", 0, 80), ("t1", 0, 80), 3.0, None, A.min)
 
     dma("s", "stg_c", [("cn", 0, 80)], [("stc", 0, 8)], T.stc[:], T.cn[:])
     send("y0", lambda d: T.sty0[d])
     send("y1", lambda d: T.sty1[d])
     send("c", lambda d: T.stc[d])
-    dma("a", "own_y0", [("sty0", 0, 8)], [("ldy0", q, q + 1)], T.ldy0[q], T.sty0[q])
-    dma("a", "own_y1", [("sty1", 0, 8)], [("ldy1", q, q + 1)], T.ldy1[q], T.sty1[q])
-    dma("a", "own_c", [("stc", 0, 8)], [("ldc", q, q + 1)], T.ldc[q], T.stc[q])
-    dma("s", "get_y0", [("ldy0", 0, 8)], [], T.yx[:, 0:640], T.ldy0[:])
-    dma("s", "get_y1", [("ldy1", 0, 8)], [], T.yx[:, 640:R], T.ldy1[:])
-    dma("a", "get_c", [("ldc", 0, 8)], [], T.yc[:], T.ldc[:])
+    dma("s", "own_y0", [("xf", 0, 640)], [], T.yx[mine, 0:640], T.xf[mine, 0:640])
+    dma("s", "own_y1", [("xf", 640, R)], [], T.yx[mine, 640:R], T.xf[mine, 640:R])
+    dma("s", "own_c", [("cn", 0, 80)], [], T.yc[mine, :], T.cn[mine, :])
+    fetch("s", "y0", "yx", slice(0, 640))
+    fetch("s", "y1", "yx", slice(640, R))
+    fetch("a", "c", "yc", slice(0, 80))
     for s in total:
         need("g", s, total[s])

@@ -16,20 +16,20 @@ _S = {
     "wg": ([128, 4 * 2048], "bfloat16"),
     "lo": ([128, V], "float32"), "hi": ([128, V], "float32"),
     "bl": ([128, V], "float32"), "bh": ([128, V], "float32"),
-    "xs": ([128, 4 * S + XW], "float32"), "xh": ([128, XW], "float32"), "pxi": ([128, R], "int32"),
+    "xs": ([128, 3 * S + XW], "float32"), "xh": ([128, XW], "float32"), "xi": ([128, 3 * S + R], "int32"),
     "s1": ([128, 1024], "float32"), "s2": ([128, 512], "float32"), "fb": ([128, 512], "float32"),
-    "wr": ([128, R], "float32"), "fl": ([128, 3 * R], "bfloat16"), "ft": ([128, 256], "bfloat16"),
-    "yi": ([128, R], "int32"), "x5": ([128, R], "float32"), "xf": ([128, R], "float32"),
+    "wr": ([128, R], "float32"), "ft": ([128, 256], "bfloat16"),
+    "yi": ([128, R], "int32"), "x5": ([128, R], "float32"),
     "lof": ([128, 512], "float32"), "lt": ([128, 512], "float32"), "odd": ([128, 512], "bfloat16"),
     "pre": ([128, 528], "bfloat16"), "c96": ([128, 512], "bfloat16"), "far": ([128, 512], "bfloat16"),
-    "ci0": ([128, 512], "int32"), "ci1": ([128, 512], "int32"),
+    "ci0": ([128, 2, 256], "int32"), "ci1": ([128, 2, 256], "int32"),
     "cu0": ([128, 512], "uint16"), "cu1": ([128, 512], "uint16"), "tm": ([128, 512], "float32"),
     "off": ([128, 512], "uint16"), "of0": ([128, 512], "uint16"),
     "rh": ([128, 80], "int32"), "lh": ([128, 80], "uint16"), "one": ([128, 256], "float32"),
     "ri": ([128, 320], "int32"), "rd": ([128, 240], "float32"), "li": ([128, 240], "int32"),
     "lq0": ([128, 240], "uint16"), "lq1": ([128, 240], "uint16"),
-    "ua": ([128, 240], "int32"), "ub": ([128, 240], "int32"), "uu": ([128, 240], "uint16"), "bf": ([128, 3, 80], "float32"),
-    "pw": ([128, 240], "bfloat16"), "p2": ([128, 240], "bfloat16"),
+    "ua": ([128, 240], "int32"), "ub": ([128, 240], "int32"), "uu": ([128, 240], "uint16"),
+    "bf": ([128, 3, 80], "float32"), "pw": ([128, 240], "bfloat16"), "p2": ([128, 240], "bfloat16"),
     "ef": ([128, 240], "int32"), "eg": ([128, 240], "float32"), "t1": ([128, 80], "float32"),
     "t2": ([128, 80], "float32"), "t3": ([128, 80], "float32"), "t4": ([128, 80], "float32"),
     "so": ([128, 80], "uint16"), "cu": ([128, 80], "float32"), "cn": ([128, 80], "float32"),
@@ -43,22 +43,22 @@ _S = {
     "thi": ([128, 1], "int32"), "thn": ([128, 2], "float32"), "thf": ([128, 2], "float32"),
 }
 SCRATCH = {k: ("sbuf", s, d) for k, (s, d) in _S.items()}
-for _k, _w, _d in (("o0", 32, "uint16"), ("o1", 32, "uint16"), ("r", 40, "int32"), ("p", 160, "int32"), ("c1", 64, "int32"),
+for _k, _w, _d in (("o0", 16, "uint16"), ("o1", 16, "uint16"), ("o2", 16, "uint16"), ("o3", 16, "uint16"),
+                   ("r", 40, "int32"), ("p", 160, "int32"), ("c1", 64, "int32"),
                    ("y0", 80, "float32"), ("y1", 80, "float32"), ("c", 10, "float32")):
     SCRATCH["st" + _k] = ("dram", [8, 128, _w], _d)
     SCRATCH["ld" + _k] = ("dram", [8, 128, _w], _d)
 SCRATCH["stt"] = ("dram", [128, 1], "int32")
 SCRATCH["ldt"] = ("dram", [8, 128, 1], "int32")
-SCRATCH["pp"] = ("psum", [128, 2048], "float32")
-for _k in range(4):
-    SCRATCH["z%d" % _k] = ("psum", [128, 512], "float32")
-PSUM = ("pp", "z0", "z1", "z2", "z3")
+SCRATCH["pp"] = ("psum", [128, 4096], "float32")
+PSUM = ("pp",)
 
-CLASSES = ("o0", "o1", "r", "p", "t", "c1", "y0", "y1", "c")
+CLASSES = ("o0", "o1", "o2", "o3", "r", "p", "t", "c1", "y0", "y1", "c")
 TWO_CALLS = ("p", "c1", "y0", "y1", "r")
 SEMAPHORES = (["q_v", "q_a", "q_t", "q_g", "sent"] + ["arr_" + k for k in CLASSES] + ["stg_" + k for k in CLASSES]
               + ["own_" + k for k in CLASSES] + ["get_" + k for k in CLASSES]
-              + ["rl0", "rl1", "rh0", "rh1", "fg0", "fg1", "xc0", "xc1", "in_r", "in_c"])
+              + ["rl0", "rl1", "rh0", "rh1", "fg0", "fg1", "xc0", "xc1", "in_r", "in_c", "in_d"]
+              + [k + c + "2" for k in ("arr_", "stg_") for c in TWO_CALLS])
 
 
 def plan(core, cores, topo, two):
@@ -150,44 +150,64 @@ def rank_program(g, core, T, topo):
         total[s] = total.get(s, 0) + 16
         record(qn, acc, s, None)
 
+    def call_of(src, dst, c):
+        return [k for k, call in enumerate(plan(src, cores, topo, c in TWO_CALLS)) if dst in [d for d, eng in call]][0]
+
     def send(c, piece):
-        need("g", "stg_" + c, None)
-        for call in plan(core, cores, topo, c in TWO_CALLS):
+        for k, call in enumerate(plan(core, cores, topo, c in TWO_CALLS)):
+            if "stg_" + c + "2" * k in total:
+                need("g", "stg_" + c + "2" * k, None)
             tr = []
             for d, eng in call:
                 rid, pid = topo.addr(d, core)
                 m = sum(1 << e for e in eng)
                 assert m & topo.mask(core, d) == m
                 tr.append(RemoteDMATransfer(dst_ids=[DstId(rid=rid, pnc=pid)], dma_engine_mask=m,
-                                            remote_sem=sem["arr_" + c], srcs=[piece(T.rank_of(d))], dsts=[T["ld" + c][q]]))
+                                            remote_sem=sem["arr_" + c + "2" * k],
+                                            srcs=[piece(T.rank_of(d))], dsts=[T["ld" + c][q]]))
                 total["sent"] = total.get("sent", 0) + len(eng)
             g.remote_dma_fused(tr, local_sem=sem.sent)
-        n = 0
-        for o in cores:
-            if o != core:
-                for call in plan(o, cores, topo, c in TWO_CALLS):
-                    n += sum(len(eng) for d, eng in call if d == core)
-        total["arr_" + c] = n
-        record("far", [("ld" + c, 0, q, True), ("ld" + c, q + 1, 8, True)], "arr_" + c, n)
+        for k in range(1 + (c in TWO_CALLS)):
+            senders = [o for o in cores if o != core and call_of(o, core, c) == k]
+            n = sum(len(eng) for o in senders for d, eng in plan(o, cores, topo, c in TWO_CALLS)[k] if d == core)
+            total["arr_" + c + "2" * k] = n
+            record("far", [("ld" + c, T.rank_of(o), T.rank_of(o) + 1, True) for o in senders], "arr_" + c + "2" * k, n)
 
     def grp(a):
         return slice(16 * a, 16 * a + 16)
 
     mine = grp(q)
 
-    def stage(qn, c, src, cols):
-        dma(qn, "stg_" + c, [], [("st" + c, 0, 8)], T["st" + c][:], src[:, cols])
+    def runs(ranks):
+        out = []
+        for a in sorted(ranks):
+            if out and out[-1][1] == a:
+                out[-1][1] = a + 1
+            else:
+                out.append([a, a + 1])
+        return out
 
-    def fetch(qn, c, to, cols):
+    def stage(qn, c, src, cols, rd=(), by_call=False):
+        if not by_call:
+            return dma(qn, "stg_" + c, list(rd), [("st" + c, 0, 8)], T["st" + c][:], src[:, cols])
+        for k, call in enumerate(plan(core, cores, topo, True)):
+            for a, b in runs([T.rank_of(d) for d, eng in call]):
+                dma(qn, "stg_" + c + "2" * k, list(rd), [("st" + c, a, b)], T["st" + c][a:b], src[16 * a:16 * b, cols])
+
+    def fetch(qn, c, to, cols, by_call=False):
         wr = [] if to in ("yx", "yc") else [(to, cols.start, cols.stop)]
-        if q > 0:
-            dma(qn, "get_" + c, [("ld" + c, 0, q)], wr, T[to][0:16 * q, cols], T["ld" + c][0:q])
-        if q < 7:
-            dma(qn, "get_" + c, [("ld" + c, q + 1, 8)], wr, T[to][16 * q + 16:128, cols], T["ld" + c][q + 1:8])
+        others = [o for o in cores if o != core]
+        for part in ([[o for o in others if call_of(o, core, c) == k] for k in range(2)] if by_call else [others]):
+            for a, b in runs([T.rank_of(o) for o in part]):
+                dma(qn, "get_" + c, [("ld" + c, a, b)], wr,
+                    T[to][16 * a:16 * b] if to == "ci1" else T[to][16 * a:16 * b, cols], T["ld" + c][a:b])
 
     dma("a", "in_r", [], [("rh", 0, 80)], T.rh[:], T.ray[:, 0:80])
-    stage("s", "p", T.px, slice(0, R))
-    dma("a", "in_c", [], [("ci0", 0, 512)], T.ci0[:], T.cand[:, 0:512])
+    for m in range(2):
+        dma("sa"[m], "in_c", [], [("ci0", 0, 128)], T.ci0[:, m, 0:128], T.cand[:, 256 * m:256 * m + 128])
+    stage("s", "p", T.px, slice(0, R), by_call=True)
+    for m in range(2):
+        dma("s", "in_d", [], [("ci0", 128, 256)], T.ci0[:, m, 128:256], T.cand[:, 256 * m + 128:256 * m + 256])
     op("g", [], [("mi", 128, 129)], lambda e: e.iota(T.mi[:, 128:129], [[0, 1]], 0, 1))
     op("g", [], [("cio", 3072, V)],
        lambda e: e.iota(T.cio[:, 3072:V], [[1, 1024]], 3072, 0, allow_small_or_imprecise_dtypes=True))
@@ -195,6 +215,9 @@ def rank_program(g, core, T, topo):
 
     def ap(b):
         return T[b[0]][:, b[1]:b[2]]
+
+    def z(k, a, b):
+        return ("pp", 2048 + 512 * k + a, 2048 + 512 * k + b)
 
     def val(x):
         return ap(x) if isinstance(x, tuple) else x
@@ -235,6 +258,15 @@ def rank_program(g, core, T, topo):
         ops("t", rd, [out], [lambda e, k=k, l=l, r=r: e.matmul(ap(out), l, r, k == 0, k == n - 1)
                              for k, (l, r) in enumerate(pairs)])
 
+    def weave(*chains):
+        for k in range(max(len(c) for c in chains)):
+            for c in chains:
+                if k < len(c):
+                    c[k]()
+
+    def skip():
+        pass
+
     fill(("one", 0, 256), 1.0)
     op("v", [("one", 0, 256)], [("cio", 0, 256)],
        lambda e: e.tensor_tensor_scan(T.cio[:, 0:256], T.one[:], T.one[:], -1.0, A.add, A.mult))
@@ -252,361 +284,368 @@ def rank_program(g, core, T, topo):
         return ("pf", k, k + 1)
 
     pcol, c16, k255, g16, dcol, tcol, hcol = (col(k) for k in range(7))
-    copy(pcol, ("mi", 128, 129))
-    bits("ma", 0, 15)
-    copy(c16, ("ma", 128, 129))
-    ts(k255, c16, -1.0, 255.0, A.mult, A.add)
-    ts(col(8), c16, -1000.0, pcol, A.mult, A.add)
-    ts(dcol, col(8), 16.0, None, A.add)
-    ts(("wd", 0, 144), ("cio", 0, 144), dcol, -2048.0, A.is_equal, A.mult)
-    ts(("ni", 0, 128), cols, pcol, -2048.0, A.is_equal, A.mult)
-    bits("ma", 0, 31)
-    ts(("nv", 0, 128), ("ma", 0, 128), -16.0, k255, A.mult, A.add)
+    weights = [lambda: act(("pb", 0, 1), c16, scale=math.log(2.0), func=AF.Exp),
+               lambda: ts(col(9), c16, -1.0, pcol, A.mult, A.add),
+               lambda: ts(("nh", 0, 128), cols, pcol, -0.5, A.is_equal, A.mult),
+               lambda: ts(g16, col(9), 16.0, None, A.add),
+               lambda: ts(hcol, c16, 0.0, 0.5, A.is_equal, A.mult),
+               lambda: ts(("t1", 0, 80), ("cio", 0, 80), 16.0, c16, A.mult, A.add),
+               lambda: copy(col(12), ("pb", 0, 1)),
+               lambda: ts(("rc", 0, 80), ("t1", 0, 80), 1.0 / S, None, A.mult),
+               lambda: ts(("wf", 0, 144), ("cio", 0, 144), g16, col(12), A.is_equal, A.mult),
+               lambda: ts(("rc", 80, 160), ("t1", 0, 80), 1.0 / S, 3.0, A.mult, A.add)]
+    owners = [lambda: (bits("ma", 5, 3), bits("mc", 0, 1), bits("mb", 4, 1)),
+              lambda: (ts(("mf", 0, allc), ("ma", 0, allc), 2.0, None, A.mult),
+                       ts(col(10), ("ma", 128, 129), 32.0, None, A.mult)),
+              lambda: (tt(("mf", 0, allc), ("mf", 0, allc), ("mc", 0, allc), A.add),
+                       ts(col(11), c16, 2.0, col(10), A.mult, A.add)),
+              lambda: (ts(("bones", 0, 128), ("mf", 0, 128), ("mf", 128, 129), None, A.is_equal),
+                       tt(tcol, col(11), ("mb", 128, 129), A.add)),
+              lambda: (ts(("mv", 0, 128), cols, tcol, None, A.is_equal),
+                       bits("ma", 2, 3), bits("mb", 1, 1)),
+              lambda: ts(("mf", 0, 128), ("ma", 0, 128), 32.0, None, A.mult),
+              lambda: tt(("mf", 0, 128), ("mf", 0, 128), ("mb", 0, 128), A.add),
+              lambda: ts(("mg", 0, 128), ("mf", 0, 128), pcol, None, A.is_equal),
+              lambda: tt(("lm", 128, 256), ("mg", 0, 128), ("mc", 0, 128), A.mult),
+              lambda: tt(("lm", 0, 128), ("mg", 0, 128), ("lm", 128, 256), A.subtract),
+              lambda: ts(("lm", 256, 512), ("lm", 0, 256), -1.0, None, A.mult)]
 
-    def constants():
-        ts(("nh", 0, 128), cols, pcol, -0.5, A.is_equal, A.mult)
-        act(("pb", 0, 1), c16, scale=math.log(2.0), func=AF.Exp)
-        ts(col(9), c16, -1.0, pcol, A.mult, A.add)
-        ts(g16, col(9), 16.0, None, A.add)
-        copy(col(12), ("pb", 0, 1))
-        ts(("wf", 0, 144), ("cio", 0, 144), g16, col(12), A.is_equal, A.mult)
-        ts(hcol, c16, 0.0, 0.5, A.is_equal, A.mult)
-        ts(("t1", 0, 80), ("cio", 0, 80), 16.0, c16, A.mult, A.add)
-        ts(("rc", 0, 80), ("t1", 0, 80), 1.0 / S, None, A.mult)
-        ts(("rc", 80, 160), ("t1", 0, 80), 1.0 / S, 3.0, A.mult, A.add)
-        bits("ma", 5, 3)
-        bits("mc", 0, 1)
-        ts(("mf", 0, allc), ("ma", 0, allc), 2.0, None, A.mult)
-        tt(("mf", 0, allc), ("mf", 0, allc), ("mc", 0, allc), A.add)
-        ts(("bones", 0, 128), ("mf", 0, 128), ("mf", 128, 129), None, A.is_equal)
-        bits("mb", 4, 1)
-        ts(col(10), ("ma", 128, 129), 32.0, None, A.mult)
-        ts(col(11), c16, 2.0, col(10), A.mult, A.add)
-        tt(tcol, col(11), ("mb", 128, 129), A.add)
-        ts(("mv", 0, 128), cols, tcol, None, A.is_equal)
-        bits("ma", 2, 3)
-        bits("mb", 1, 1)
-        ts(("mf", 0, 128), ("ma", 0, 128), 32.0, None, A.mult)
-        tt(("mf", 0, 128), ("mf", 0, 128), ("mb", 0, 128), A.add)
-        ts(("mg", 0, 128), ("mf", 0, 128), pcol, None, A.is_equal)
-        tt(("lm", 128, 256), ("mg", 0, 128), ("mc", 0, 128), A.mult)
-        tt(("lm", 0, 128), ("mg", 0, 128), ("lm", 128, 256), A.subtract)
-        ts(("lm", 256, 512), ("lm", 0, 256), -1.0, None, A.mult)
-        for k in range(4):
+    def fills():
+        for k in range(3):
             act(("xs", k * S + R, k * S + S), ("cio", 0, S - R))
-        for b, at, c in (("xs", 0, D), ("xs", 4 * S, D), ("xh", 0, -1.0)):
+        for k in range(3):
+            fill(("xi", k * S + R, k * S + S), 0)
+        for b, at, c in (("xs", 0, D), ("xs", 3 * S, D), ("xh", 0, -1.0)):
             fill((b, at + R, at + XW), c)
         fill(("c96", 0, 512), float(CAP))
         fill(("pre", 15, 16), 0.0)
 
-    def extract(out, w, buf, base, extra):
+    def extract(out, w, base, extra):
         n = out[2] - out[1]
-        tr = [(T[w][:, 16 - i:144 - i], T[buf][:, base + i:base + 16 * n:16]) for i in range(16)]
-        mms(out, [(w, 0, 144), (buf, base, base + 16 * n), (extra[0], 0, 128), extra[1]],
+        tr = [(T[w][:, 16 - i:144 - i], T.wg[:, base + i:base + 16 * n:16]) for i in range(16)]
+        mms(out, [(w, 0, 144), ("wg", base, base + 16 * n), (extra[0], 0, 128), extra[1]],
             tr + [(T[extra[0]][:], ap(extra[1]))])
 
     def prepare(src, parts):
-        ts(("ub", 0, 240), src, 8, None, A.arith_shift_right)
-        ts(("ua", 0, 240), src, 255, None, A.bitwise_and)
-        op("v", [("ub", 0, 240)], [("bf", 0, 240)], lambda e: e.tensor_copy(T.bf[:], T.ub[:]))
-        copy(("uu", 0, 240), ("ua", 0, 240))
         n = 80 // parts
-        for h in range(parts):
-            op("a", [("bf", 0, 240)], [("pw", 3 * n * h, 3 * n * h + 3 * n)],
-               lambda e: e.activation(T.pw[:, 3 * n * h:3 * n * h + 3 * n], T.bf[:, :, n * h:n * h + n], AF.Exp, bias=0.0,
-                                      scale=-math.log(2.0)))
-        op("a", [("bf", 0, 240)], [("p2", 0, 240)],
-           lambda e: e.activation(T.p2[:], T.bf[:], AF.Exp, bias=0.0, scale=math.log(2.0)))
+
+        def powers():
+            op("v", [("ub", 0, 240)], [("bf", 0, 240)], lambda e: e.tensor_copy(T.bf[:], T.ub[:]))
+            for h in range(parts):
+                op("a", [("bf", 0, 240)], [("pw", 3 * n * h, 3 * n * h + 3 * n)],
+                   lambda e: e.activation(T.pw[:, 3 * n * h:3 * n * h + 3 * n], T.bf[:, :, n * h:n * h + n], AF.Exp,
+                                          bias=0.0, scale=-math.log(2.0)))
+            op("a", [("bf", 0, 240)], [("p2", 0, 240)],
+               lambda e: e.activation(T.p2[:], T.bf[:], AF.Exp, bias=0.0, scale=math.log(2.0)))
+
+        return [lambda: ts(("ub", 0, 240), src, 8, None, A.arith_shift_right), powers,
+                lambda: ts(("ua", 0, 240), src, 255, None, A.bitwise_and), lambda: copy(("uu", 0, 240), ("ua", 0, 240))]
 
     def slots(t):
-        return [S * k for k in range(4)] if t == 0 else [S * (4 - k) for k in range(4)]
+        return [S * k for k in range(4)] if t == 0 else [S * (3 - k) for k in range(4)]
 
     def rest(qn, lst, a, b):
         gather(qn, ("wr", 16 * a, 16 * b), ("cio", 0, V), (lst, a, b))
 
-    def see(t, qn, j, *ks):
+    def offsets(t, p):
+        op("v", [("ci%d" % t, 64 * p, 64 * p + 64)], [("cu%d" % t, 128 * p, 128 * p + 128)],
+           lambda e: e.tensor_copy(T["cu%d" % t][:, 128 * p:128 * p + 128], T["ci%d" % t][:, :, 64 * p:64 * p + 64]))
+
+    def see(t, qn, p, *ks):
         for k in ks:
-            b = 2048 * (j // 2) + 512 * k
-            c = 256 * (j % 2) + b // 16
-            gather(qn, ("wg", 2048 * j + 512 * k, 2048 * j + 512 * k + 512), ("wr", 0, R), ("cu%d" % t, c, c + 32), -(b + 255.0))
+            c = 128 * p + 32 * k
+            gather(qn, ("wg", 16 * c, 16 * c + 512), ("wr", 0, R), ("cu%d" % t, c, c + 32), -(1024 * p + 512 * (k % 2) + 255.0))
 
-    def seen(j):
-        extract(("z%d" % j, 0, 128), "wd", "wg", 2048 * j, ("ni", ("nv", 0, 128)))
+    def seen(p):
+        extract(z(p, 0, 128), "wd", 2048 * p, ("ni", ("nv", 0, 128)))
 
-    def lists(t, j):
-        c = 256 * (j % 2) + 128 * (j // 2)
-        tt(("tm", 128 * j, 128 * j + 128), ("z%d" % j, 0, 128), ("ci%d" % t, c, c + 128), A.max)
-        ts(("off", 128 * j, 128 * j + 128), ("tm", 128 * j, 128 * j + 128), float(R), None, A.min)
+    def lists(t, p):
+        tm = ("tm", 128 * p, 128 * p + 128)
+        return [lambda: op("v", [z(p, 0, 128), ("ci%d" % t, 64 * p, 64 * p + 64)], [tm],
+                           lambda e: e.tensor_tensor(ap(tm), ap(z(p, 0, 128)), T["ci%d" % t][:, :, 64 * p:64 * p + 64], A.max)),
+                lambda: ts(("off", tm[1], tm[2]), tm, float(R), None, A.min)]
 
-    def ship(h):
-        c, cs = "o%d" % h, slice(256 * h, 256 * h + 256)
-        dma("s", "stg_" + c, [("off", cs.start, cs.stop)], [("st" + c, 0, 8)], T["st" + c][:], T.off[:, cs])
-        dma("s", "get_" + c, [("off", cs.start, cs.stop)], [("of0", cs.start, cs.stop)], T.of0[mine, cs], T.off[mine, cs])
+    def ship(p, qn):
+        c, cs = "o%d" % p, slice(128 * p, 128 * p + 128)
+        stage(qn, c, T.off, cs, [("off", cs.start, cs.stop)])
+        dma(qn, "get_" + c, [("off", cs.start, cs.stop)], [("of0", cs.start, cs.stop)], T.of0[mine, cs], T.off[mine, cs])
         send(c, lambda d: T["st" + c][d])
 
-    def twin(t, qn):
+    def twin(t):
         a = slots(t)[0]
-        dma(qn, "xc%d" % t, [("xs", a, a + R)], [("xh", 0, R)], T.xh[:, 0:R], T.xs[:, a:a + R])
+        dma("s", "xc%d" % t, [("xs", a, a + R)], [("xh", 0, R)], T.xh[:, 0:R], T.xs[:, a:a + R])
 
     def window(t, b):
         return ("xs", slots(t)[0], slots(t)[0] + XW) if b == "lo" else ("xh", 0, XW)
 
-    def first(t, b, *ps):
+    def first(t, b, *ps, es=(0, 2)):
         for p in ps:
-            c = 256 * (p // 2) + 64 * (p % 2)
-            gather("a", (b, 1024 * p, 1024 * p + 1024), window(t, b), ("off" if t else "of0", c, c + 64))
+            gather("a", (b, 1024 * p + 512 * es[0], 1024 * p + 512 * es[1]), window(t, b),
+                   ("off" if t else "of0", 128 * p + 32 * es[0], 128 * p + 32 * es[1]))
 
-    def second(t, b, *ps):
+    def second(t, b, *ps, es=(0, 2)):
         for p in ps:
-            c = 256 * (p // 2) + 128 + 64 * (p % 2)
-            blk, to = (b, 1024 * p, 1024 * p + 1024), "b" + b[0]
-            tt_gather(blk, window(t, b), ("off" if t else "of0", c, c + 64), blk, A.min if b == "lo" else A.max)
-            for a in range(8):
-                dma("s", "r%s%d" % (b[0], t), [blk], [(to, 512 * a, 512 * a + 512)],
-                    T[to][32 * p:32 * p + 32, 512 * a:512 * a + 512], T[b][grp(a), blk[1]:blk[2]])
+            blk, to = (b, 1024 * p + 512 * es[0], 1024 * p + 512 * es[1]), "b" + b[0]
+            tt_gather(blk, window(t, b), ("off" if t else "of0", 128 * p + 64 + 32 * es[0], 128 * p + 64 + 32 * es[1]), blk,
+                      A.min if b == "lo" else A.max)
+            for a in range(8 if es[1] == 2 else 0):
+                dma("s", "r%s%d" % (b[0], t), [(b, 1024 * p, 1024 * p + 1024)], [(to, 512 * a, 512 * a + 512)],
+                    T[to][32 * p:32 * p + 32, 512 * a:512 * a + 512], T[b][grp(a), 1024 * p:1024 * p + 1024])
 
-    def lift(b):
-        act(("pp", 0, 1024), (b, 0, 1024))
-        act(("pp", 1024, 2048), (b, 1024, 2048))
+    def lift(b, k):
+        at = 1024 * k + (2048 if b == "bh" else 0)
+        act(("pp", at, at + 1024), (b, 1024 * k, 1024 * k + 1024))
 
     def fold(b, o, last):
-        return [lambda: tt(("s1", 0, 1024), ("pp", 0, 1024), (b, 2048, 3072), o),
-                lambda: tt(("pp", 0, 1024), ("pp", 1024, 2048), (b, 3072, 4096), o),
-                lambda: tt(("s2", 0, 512), ("pp", 0, 512), ("s1", 0, 512), o),
-                lambda: tt(("pp", 1024, 1536), ("pp", 512, 1024), ("s1", 512, 1024), o),
-                lambda: tt(last, ("pp", 1024, 1536), ("s2", 0, 512), o)]
+        def pp(lo, hi):
+            return ("pp", lo + (2048 if b == "bh" else 0), hi + (2048 if b == "bh" else 0))
+        return [lambda: tt(("s1", 0, 1024), pp(0, 1024), (b, 2048, 3072), o),
+                lambda: tt(pp(0, 1024), pp(1024, 2048), (b, 3072, 4096), o),
+                lambda: tt(("s2", 0, 512), pp(0, 512), ("s1", 0, 512), o),
+                lambda: tt(pp(1024, 1536), pp(512, 1024), ("s1", 512, 1024), o),
+                lambda: tt(last, pp(1024, 1536), ("s2", 0, 512), o)]
 
     def spread(t):
-        act(("fb", 0, 512), ("lof", 0, 512), scale=-0.25, bias=-0.375)
+        act(("fb", 0, 512), ("lof", 0, 512), scale=-0.25 if t else -0.2, bias=-0.375 if t else -0.3)
         for a in range(8):
             for p in range(4):
                 dma("s", "fg%d" % t, [("fb", 0, 512)], [("et", 1024 * p, 1024 * p + 1024)],
                     T.et[grp(a), 1024 * p:1024 * p + 1024], T.fb[32 * p:32 * p + 32, :])
 
-    def weave(*chains):
-        for k in range(max(len(c) for c in chains)):
-            for c in chains:
-                if k < len(c):
-                    c[k]()
-
     def count():
-        tt(("far", 0, 512), ("z3", 0, 512), ("lt", 0, 512), A.is_gt)
-        mms(("z0", 0, 512), [("bones", 0, 128), ("far", 0, 512)], [(T.bones[:], T.far[:])])
+        tt(("far", 0, 512), ("pp", 0, 512), ("lt", 0, 512), A.is_gt)
+        mms(z(0, 0, 512), [("bones", 0, 128), ("far", 0, 512)], [(T.bones[:], T.far[:])])
 
     def carve():
-        ts(("odd", 0, 512), ("z0", 0, 512), float(NEED), None, A.is_ge)
+        ts(("odd", 0, 512), z(0, 0, 512), float(NEED), None, A.is_ge)
         op("v", [("odd", 0, 512), ("c96", 0, 512)], [("pre", 16, 528)],
            lambda e: e.tensor_tensor_scan(T.pre[:, 16:528], T.odd[:], T.c96[:], 0.0, A.add, A.min))
-        mms(("z2", 0, 256), [("lm", 0, 512), ("pre", 0, 528)],
+        mms(z(2, 0, 256), [("lm", 0, 512), ("pre", 0, 528)],
             [(T.lm[:, 128 * k:128 * k + 128], T.pre[:, 16 - k // 2 + 256 * (k % 2):272 - k // 2 + 256 * (k % 2)])
              for k in range(4)])
-
-    def table():
-        act(("ft", 0, 256), ("z2", 0, 256), bias=hcol)
+        act(("ft", 0, 256), z(2, 0, 256), bias=hcol)
 
     def step(t, s, h):
         a, b, to = 640 * h, 640 * h + 640, slots(t)[s + 1]
-        return [lambda: tt_gather(("yi", a, b), ("et", 0, V), ("lq%d" % t, 80 * s + 40 * h, 80 * s + 40 * h + 40),
-                                  ("x5", a, b), A.add),
+        lst = ("lq%d" % t, 80 * s + 40 * h, 80 * s + 40 * h + 40)
+        if t == 0:
+            return [lambda: tt_gather(("x5", a, b), ("et", 0, V), lst, ("xi", to - S + a, to - S + b), A.add),
+                    lambda: ts(("xi", to + a, to + b), ("x5", a, b), 1.25, 0.0, A.mult, A.max)]
+        return [lambda: tt_gather(("yi", a, b), ("et", 0, V), lst, ("x5", a, b), A.add),
                 lambda: ts(("xs", to + a, to + b), ("yi", a, b), 0.0, float(TOP), A.max, A.min)]
 
-    def five(t, s, h):
-        a, b, at = 640 * h, 640 * h + 640, slots(t)[s]
+    def five(s, h):
+        a, b, at = 640 * h, 640 * h + 640, slots(1)[s]
         act(("x5", a, b), ("xs", at + a, at + b), scale=1.25)
 
     def flags(qn, s, a, b):
-        gather(qn, ("fl", R * s + 16 * a, R * s + 16 * b), ("ft", 0, 256), ("uu", 80 * s + a, 80 * s + b))
+        gather(qn, ("wg", R * s + 16 * a, R * s + 16 * b), ("ft", 0, 256), ("uu", 80 * s + a, 80 * s + b))
 
-    def flagged(z, s, a, b):
-        extract((z, (b - a) * s, (b - a) * (s + 1)), "wf", "fl", R * s + 16 * a, ("nh", ("p2", 80 * s + a, 80 * s + b)))
+    def flagged(k, s, a, b):
+        extract(z(k, (b - a) * s, (b - a) * (s + 1)), "wf", R * s + 16 * a, ("nh", ("p2", 80 * s + a, 80 * s + b)))
 
     def tests(at, n):
         return [("ef", at + n * s, at + n * s + n) for s in range(3)]
 
-    def bit_test(z, at, n):
-        e1, e2, e3 = tests(at, n)
-        return [lambda: tt(("ua", at, at + 3 * n), (z, 0, 3 * n), ("pw", at, at + 3 * n), A.mult),
-                lambda: ts(("ef", at, at + 3 * n), ("ua", at, at + 3 * n), 1, None, A.bitwise_and),
-                lambda: tt(e2, e2, e1, A.mult),
-                lambda: tt(e3, e3, e2, A.mult)]
+    def pick(t, qn, a, b):
+        if t:
+            return gather(qn, ("wr", 16 * a, 16 * b), ("xs", 0, 3 * S + R), ("so", a, b))
+        out, win = ("xs", 3 * S + 16 * a, 3 * S + 16 * b), ("xi", 0, 3 * S + R)
+        op("v", [win, ("so", a, b)], [out],
+           lambda e: e.tensor_scalar(ap(out), ap(win).indirect(T.so[:, a:b]), float(TOP), None, A.min))
 
-    def choose(t, es, a, b):
-        o = A.subtract if t else A.add
-        return [lambda: (tt(("t3", a, b), ("rc", 80 * t + a, 80 * t + b), es[0], o), tt(("t4", a, b), es[1], es[2], A.add)),
-                lambda: tt(("t3", a, b), ("t3", a, b), ("t4", a, b), o),
-                lambda: ts(("so", a, b), ("t3", a, b), float(S), None, A.mult)]
-
-    def pick(t, qn, h):
-        to, w = (("xf", 0), S) if t else (("xs", 4 * S), 0)
-        gather(qn, (to[0], to[1] + 640 * h, to[1] + 640 * h + 640), ("xs", w, w + 3 * S + R), ("so", 40 * h, 40 * h + 40))
-
+    copy(pcol, ("mi", 128, 129))
+    bits("ma", 0, 15)
+    bits("mb", 0, 31)
+    copy(c16, ("ma", 128, 129))
     copy(("lh", 0, 80), ("rh", 0, 80))
+    ts(k255, c16, -1.0, 255.0, A.mult, A.add)
+    ts(col(8), c16, -1000.0, pcol, A.mult, A.add)
     rest("a", "lh", 0, 40)
-    copy(("cu0", 0, 512), ("ci0", 0, 512))
+    offsets(0, 0)
+    ts(dcol, col(8), 16.0, None, A.add)
     rest("v", "lh", 40, 80)
-    see(0, "a", 0, 0, 1, 2, 3)
-    see(0, "v", 1, 0, 1, 2, 3)
+    ts(("ni", 0, 128), cols, pcol, -2048.0, A.is_equal, A.mult)
+    see(0, "a", 0, 0, 1)
+    see(0, "v", 0, 2)
+    ts(("wd", 0, 144), ("cio", 0, 144), dcol, -2048.0, A.is_equal, A.mult)
+    ts(("nv", 0, 128), ("mb", 0, 128), -16.0, k255, A.mult, A.add)
+    see(0, "v", 0, 3)
     seen(0)
+    offsets(0, 1)
+    see(0, "a", 1, 0, 1)
+    offsets(0, 2)
+    see(0, "v", 1, 2, 3)
     seen(1)
-    see(0, "a", 2, 0, 1, 2, 3)
-    see(0, "v", 3, 0, 1)
-    lists(0, 0)
-    lists(0, 1)
-    ship(0)
-    see(0, "v", 3, 2, 3)
-    seen(2)
-    seen(3)
-    lists(0, 2)
-    lists(0, 3)
-    ship(1)
-    dma("s", "get_p", [], [("pxi", 0, R)], T.pxi[mine, :], T.px[mine, :])
-    fetch("s", "p", "pxi", slice(0, R))
-    constants()
-    copy(("xs", 0, R), ("pxi", 0, R))
-    twin(0, "a")
-    fetch("s", "o0", "of0", slice(0, 256))
-    fetch("s", "o1", "of0", slice(256, 512))
+    offsets(0, 3)
+    for p in (2, 3):
+        see(0, "a", p, 0, 1, 2)
+        weave(lists(0, p - 2), [lambda: see(0, "v", p, 3)])
+        ship(p - 2, "s")
+        seen(p)
+    weave(owners[:2], weights[:2])
+    weave(lists(0, 2), owners[2:4])
+    ship(2, "s")
+    weave(owners[4:6], weights[2:4])
+    weave(lists(0, 3), owners[6:8])
+    ship(3, "a")
+    fills()
+    dma("s", "get_p", [], [("xi", 0, R)], T.xi[mine, 0:R], T.px[mine, :])
+    fetch("s", "p", "xi", slice(0, R), True)
+    weave(owners[8:], weights[4:])
+    copy(("xs", 0, R), ("xi", 0, R))
+    for p in range(4):
+        fetch("s", "o%d" % p, "of0", slice(128 * p, 128 * p + 128))
+    twin(0)
     dma("s", "stg_t", [], [("stt", 0, 8)], T.stt[:], T.th[:])
     dma("s", "own_t", [], [("ldt", q, q + 1)], T.ldt[q], T.th[:])
     stage("s", "r", T.ray, slice(0, 320))
     dma("s", "get_r", [], [("ri", 0, 320)], T.ri[mine, :], T.ray[mine, :])
     send("t", lambda d: T.stt[:])
     send("r", lambda d: T["str"][d])
-    first(0, "lo", 0, 1, 2, 3)
-    second(0, "lo", 0, 1, 2, 3)
+    for es in ((0, 1), (1, 2)):
+        first(0, "lo", 0, es=es)
+        second(0, "lo", 0, es=es)
+    first(0, "lo", 1, 2, 3)
+    second(0, "lo", 1, 2, 3)
     dma("s", "get_t", [("ldt", 0, 8)], [("thi", 0, 1)], T.thi[:], T.ldt[:, mine, :])
     fetch("s", "r", "ri", slice(0, 320))
     first(0, "hi", 0, 1, 2, 3)
     second(0, "hi", 0, 1, 2, 3)
     stage("s", "c1", T.cand, slice(512, 1024))
-    dma("s", "get_c1", [], [("ci1", 0, 512)], T.ci1[mine, :], T.cand[mine, 512:1024])
+    dma("s", "get_c1", [], [("ci1", 0, 256)], T.ci1[mine], T.cand[mine, 512:1024])
     send("c1", lambda d: T.stc1[d])
-    lift("bl")
-    five(0, 0, 0)
-    five(0, 0, 1)
+    lift("bl", 0)
+    lift("bl", 1)
     copy(("thn", 0, 1), ("thi", 0, 1))
     copy(("thn", 1, 2), ("thi", 0, 1))
-    mms(("z0", 0, 2), [("mv", 0, 128), ("thn", 0, 2)], [(T.mv[:], T.thn[:])])
+    mms(z(3, 0, 2), [("mv", 0, 128), ("thn", 0, 2)], [(T.mv[:], T.thn[:])])
     weave(fold("bl", A.min, ("lof", 0, 512)),
-          [lambda: None, lambda: copy(("thf", 0, 2), ("z0", 0, 2)), lambda: None, lambda: copy(("lq0", 0, 240), ("ri", 0, 240))])
+          [skip, lambda: copy(("thf", 0, 2), z(3, 0, 2)), skip, lambda: copy(("lq0", 0, 240), ("ri", 0, 240))])
+    lift("bh", 0)
     spread(0)
-    fetch("s", "c1", "ci1", slice(0, 512))
-    lift("bh")
+    fetch("s", "c1", "ci1", slice(0, 256))
+    lift("bh", 1)
     act(("lt", 0, 512), ("lof", 0, 512), bias=("thf", 0, 1))
-    prepare(("ri", 0, 240), 1)
-    weave(fold("bh", A.max, ("z3", 0, 512)))
+    weave(fold("bh", A.max, ("pp", 0, 512)), prepare(("ri", 0, 240), 1))
     count()
     tt(("rd", 0, 240), ("ri", 80, 320), ("ri", 0, 240), A.subtract)
     carve()
-    table()
     for s in range(3):
         flags("a", s, 0, 40)
         flags("v", s, 40, 80)
-        flagged("z0" if s == 2 else "z1", s, 0, 80)
-    e1, e2, e3 = es = tests(0, 80)
-    weave([lambda: tt(("ua", 0, 160), ("z1", 0, 160), ("pw", 0, 160), A.mult),
+        flagged(0 if s == 2 else 1, s, 0, 80)
+    ahead = step(0, 0, 0), step(0, 0, 1)
+    ahead[0][0]()
+    e1, e2, e3 = tests(0, 80)
+    weave([lambda: tt(("ua", 0, 160), z(1, 0, 160), ("pw", 0, 160), A.mult),
            lambda: ts(("ef", 0, 160), ("ua", 0, 160), 1, None, A.bitwise_and),
            lambda: (tt(e2, e2, e1, A.mult), tt(("t1", 0, 80), e1, ("rd", 0, 80), A.mult),
-                    tt(("ua", 160, 240), ("z0", 160, 240), ("pw", 160, 240), A.mult)),
+                    tt(("ua", 160, 240), z(0, 160, 240), ("pw", 160, 240), A.mult)),
            lambda: (tt(("eg", 80, 160), e2, ("rd", 80, 160), A.mult), tt(("t1", 0, 80), ("t1", 0, 80), ("ri", 0, 80), A.add),
                     ts(e3, ("ua", 160, 240), 1, None, A.bitwise_and), tt(("t2", 0, 80), e2, ("rd", 160, 240), A.mult)),
            lambda: (tt(("t1", 0, 80), ("t1", 0, 80), ("eg", 80, 160), A.add), tt(("t2", 0, 80), ("t2", 0, 80), e3, A.mult)),
            lambda: tt(("li", 0, 80), ("t1", 0, 80), ("t2", 0, 80), A.add),
            lambda: copy(("lq1", 0, 80), ("li", 0, 80))],
-          [lambda k=k: copy(("cu1", 128 * k, 128 * k + 128), ("ci1", 128 * k, 128 * k + 128)) for k in range(2)]
-          + [lambda: None] * 2 + [lambda: tt(e3, e3, e2, A.mult), lambda: copy(("cu1", 256, 512), ("ci1", 256, 512))])
+          [lambda: offsets(1, 0), skip, skip, skip, skip, lambda: offsets(1, 1)])
 
     rest("a", "lq1", 0, 80)
-    weave(step(0, 0, 0), step(0, 0, 1))
-    see(1, "a", 0, 0)
-    five(0, 1, 0)
-    five(0, 1, 1)
-    see(1, "v", 1, 0)
-    see(1, "a", 0, 1, 2)
-    weave(step(0, 1, 0), step(0, 1, 1))
-    see(1, "a", 0, 3)
+    weave(ahead[1], [lambda: tt(e3, e3, e2, A.mult), ahead[0][1]])
+    offsets(1, 2)
+    offsets(1, 3)
+    see(1, "a", 0, 0, 1, 2, 3)
     seen(0)
-    five(0, 2, 0)
-    five(0, 2, 1)
-    see(1, "v", 1, 1)
-    see(1, "a", 1, 2, 3)
+    weave(step(0, 1, 0), step(0, 1, 1))
+    see(1, "a", 1, 0, 1, 2, 3)
     seen(1)
+    weave([lambda: (tt(("t3", 0, 80), ("rc", 0, 80), e1, A.add), tt(("t4", 0, 80), e2, e3, A.add)),
+           lambda: tt(("t3", 0, 80), ("t3", 0, 80), ("t4", 0, 80), A.add),
+           lambda: ts(("so", 0, 80), ("t3", 0, 80), float(S), None, A.mult)], step(0, 2, 0), step(0, 2, 1))
     see(1, "a", 2, 0, 1, 2, 3)
     seen(2)
-    weave(choose(0, es, 0, 80), step(0, 2, 0), step(0, 2, 1))
-    lists(1, 0)
-    pick(0, "v", 0)
-    pick(0, "v", 1)
-    twin(1, "s")
-    see(1, "a", 3, 0, 1)
+    weave(lists(1, 0), [lambda: pick(0, "v", 0, 40), lambda: pick(0, "v", 40, 80)])
+    twin(1)
+    see(1, "a", 3, 2)
     first(1, "lo", 0)
-    lists(1, 1)
-    see(1, "v", 3, 2, 3)
+    weave(lists(1, 1), [lambda: see(1, "v", 3, 0), lambda: see(1, "v", 3, 1, 3)])
     seen(3)
     first(1, "lo", 1)
-    second(1, "lo", 0)
-    lists(1, 2)
-    first(1, "lo", 2, 3)
-    second(1, "lo", 1)
-    lists(1, 3)
+    weave(lists(1, 2), [lambda: second(1, "lo", 0)])
+    first(1, "lo", 2)
+    weave([lambda: second(1, "lo", 1)] + lists(1, 3))
+    first(1, "lo", 3)
     second(1, "lo", 2, 3)
     first(1, "hi", 0, 1, 2, 3)
     second(1, "hi", 0, 1, 2, 3)
-    lift("bl")
-    five(1, 0, 0)
-    five(1, 0, 1)
+    lift("bl", 0)
+    lift("bl", 1)
+    five(0, 0)
+    five(0, 1)
     weave(fold("bl", A.min, ("lof", 0, 512)),
-          [lambda: (tt(("cu", 0, 80), ("t4", 0, 80), e1, A.add), tt(("t3", 0, 80), e1, ("rd", 160, 240), A.mult)),
+          [lambda: (ts(("cu", 0, 80), ("t3", 0, 80), 3.0, None, A.add), tt(("t2", 0, 80), e1, ("rd", 160, 240), A.mult)),
            lambda: tt(("eg", 0, 160), ("ef", 0, 160), ("rd", 80, 240), A.mult),
-           lambda: tt(("li", 160, 240), ("t3", 0, 80), ("ri", 160, 240), A.add),
+           lambda: tt(("li", 160, 240), ("t2", 0, 80), ("ri", 160, 240), A.add),
            lambda: tt(("t1", 0, 80), ("eg", 0, 80), ("eg", 80, 160), A.add)])
+    lift("bh", 0)
     spread(1)
-    lift("bh")
+    lift("bh", 1)
     act(("lt", 0, 512), ("lof", 0, 512), bias=("thf", 0, 1))
     tt(("li", 80, 160), ("t1", 0, 80), ("ri", 80, 160), A.add)
-    prepare(("li", 0, 240), 2)
-    weave(fold("bh", A.max, ("z3", 0, 512)))
+    weave(fold("bh", A.max, ("pp", 0, 512)), prepare(("li", 0, 240), 2))
     count()
     copy(("lq1", 80, 240), ("li", 80, 240))
     carve()
-    table()
 
+    def settle(h):
+        at, a, b = 120 * h, 40 * h, 40 * h + 40
+        e1, e2, e3 = tests(at, 40)
+        t3 = ("t3", a, b)
+        return ([lambda: tt(("ua", at, at + 80), z(1 + 2 * h, 0, 80), ("pw", at, at + 80), A.mult),
+                 lambda: ts(("ef", at, at + 80), ("ua", at, at + 80), 1, None, A.bitwise_and),
+                 lambda: (tt(e2, e2, e1, A.mult), tt(t3, ("rc", 80 + a, 80 + b), e1, A.subtract)),
+                 lambda: tt(t3, t3, e2, A.subtract)],
+                [lambda: tt(("ua", at + 80, at + 120), z(2 * h, 80, 120), ("pw", at + 80, at + 120), A.mult),
+                 lambda: ts(e3, ("ua", at + 80, at + 120), 1, None, A.bitwise_and),
+                 lambda: tt(e3, e3, e2, A.mult),
+                 lambda: tt(t3, t3, e3, A.subtract),
+                 lambda: ts(("so", a, b), t3, float(S), None, A.mult)])
+
+    def last_flags(s, h):
+        flags("a", s, 40 * h, 40 * h + 40)
+        flagged(2 * h + (s < 2), s, 40 * h, 40 * h + 40)
+
+    (early0, late0), (early1, late1) = settle(0), settle(1)
     for s in range(3):
-        flags("a", s, 0, 40)
-        flagged("z1", s, 0, 40)
+        last_flags(s, 0)
     weave(step(1, 0, 0), step(1, 0, 1))
-    five(1, 1, 0)
-    five(1, 1, 1)
-    flags("a", 0, 40, 80)
-    flagged("z3", 0, 40, 80)
-    es, later = tests(0, 40), tests(120, 40)
-    weave(bit_test("z1", 0, 40), step(1, 1, 0) + step(1, 1, 1))
-    five(1, 2, 0)
-    flags("a", 1, 40, 80)
-    flagged("z3", 1, 40, 80)
-    five(1, 2, 1)
-    flags("a", 2, 40, 80)
-    flagged("z3", 2, 40, 80)
-    weave(choose(1, es, 0, 40), step(1, 2, 0))
-    pick(1, "a", 0)
-    dma("a", "stg_y0", [("xf", 0, 640)], [("sty0", 0, 8)], T.sty0[:], T.xf[:, 0:640])
-    weave(step(1, 2, 1) + [lambda: tt(("t1", 0, 40), ("cu", 0, 40), es[0], A.add)],
-          bit_test("z3", 120, 40) + choose(1, later, 40, 80))
-    pick(1, "a", 1)
-    dma("a", "stg_y1", [("xf", 640, R)], [("sty1", 0, 8)], T.sty1[:], T.xf[:, 640:R])
-    tt(("t1", 40, 80), ("cu", 40, 80), later[0], A.add)
-    tt(("t1", 0, 80), ("t1", 0, 80), ("t4", 0, 80), A.add)
+    five(1, 0)
+    five(1, 1)
+    last_flags(0, 1)
+    weave(step(1, 1, 0) + step(1, 1, 1), early0, [skip, skip] + late0[:2])
+    five(2, 0)
+    last_flags(1, 1)
+    five(2, 1)
+    last_flags(2, 1)
+    weave(late0[2:], step(1, 2, 0), [skip] + early1[:2])
+    pick(1, "a", 0, 40)
+    stage("s", "y0", T.wr, slice(0, 640), [("wr", 0, 640)], True)
+    last = step(1, 2, 1)
+    weave(early1[2:3], last[:1], late1[:1])
+    weave(early1[3:] + late1[1:], [skip, last[1]])
+    pick(1, "a", 40, 60)
+    tt(("t1", 0, 80), ("cu", 0, 80), ("t3", 0, 80), A.subtract)
+    pick(1, "v", 60, 80)
+    stage("a", "y1", T.wr, slice(640, R), [("wr", 640, R)], True)
     ts(("cn", 0, 80), ("t1", 0, 80), 3.0, None, A.min)
 
     dma("s", "stg_c", [("cn", 0, 80)], [("stc", 0, 8)], T.stc[:], T.cn[:])
     send("y0", lambda d: T.sty0[d])
     send("y1", lambda d: T.sty1[d])
     send("c", lambda d: T.stc[d])
-    dma("s", "own_y0", [("xf", 0, 640)], [], T.yx[mine, 0:640], T.xf[mine, 0:640])
-    dma("s", "own_y1", [("xf", 640, R)], [], T.yx[mine, 640:R], T.xf[mine, 640:R])
+    dma("s", "own_y0", [("wr", 0, R)], [], T.yx[mine, :], T.wr[mine, :])
     dma("s", "own_c", [("cn", 0, 80)], [], T.yc[mine, :], T.cn[mine, :])
     fetch("s", "y0", "yx", slice(0, 640))
-    fetch("s", "y1", "yx", slice(640, R))
+    fetch("s", "y1", "yx", slice(640, R), True)
     fetch("a", "c", "yc", slice(0, 80))
     for s in total:
         need("g", s, total[s])

@@ -8,7 +8,8 @@ V, R, RO, H, CAP, NEED = 4096, 1280, 2, 3, 96, 9
 TOP = 2 ** 20 - 1
 D = float(2 ** 21)
 XW = R + 8
-S = 2048
+CUT = (0, 20, 40, 60, 80)
+PIECES = len(CUT) - 1
 
 _S = {
     "et": ([128, V], "float32"),
@@ -16,36 +17,35 @@ _S = {
     "wg": ([128, 4 * 2048], "bfloat16"),
     "lo": ([128, V], "float32"), "hi": ([128, V], "float32"),
     "bl": ([128, V], "float32"), "bh": ([128, V], "float32"),
-    "xs": ([128, 3 * S + XW], "float32"), "xh": ([128, XW], "float32"), "xi": ([128, 3 * S + R], "int32"),
-    "s1": ([128, 1024], "float32"), "s2": ([128, 512], "float32"), "fb": ([128, 512], "float32"),
-    "wr": ([128, R], "float32"), "ft": ([128, 256], "bfloat16"),
-    "yi": ([128, R], "int32"), "x5": ([128, R], "float32"),
+    "xs": ([128, 3 * R + XW], "float32"), "xn": ([128, XW], "float32"), "xh": ([128, XW], "float32"),
+    "s1": ([128, 1536], "float32"), "fb": ([128, 512], "float32"),
+    "wr": ([128, R], "float32"), "ft": ([128, 256], "bfloat16"), "yi": ([128, R], "int32"),
+    "u5": ([128, 80, 5], "int32"), "e5": ([128, 400], "int32"), "he": ([128, 400], "float32"),
+    "hv": ([128, 400], "float32"), "hx0": ([128, 400], "float32"), "hx1": ([128, 400], "float32"),
+    "hs": ([128, 400], "float32"), "hc": ([128, 400], "float32"),
     "lof": ([128, 512], "float32"), "lt": ([128, 512], "float32"), "odd": ([128, 512], "bfloat16"),
     "pre": ([128, 528], "bfloat16"), "c96": ([128, 512], "bfloat16"), "far": ([128, 512], "bfloat16"),
-    "ci0": ([128, 2, 256], "int32"), "ci1": ([128, 2, 256], "int32"),
-    "cu0": ([128, 512], "uint16"), "cu1": ([128, 512], "uint16"), "tm": ([128, 512], "float32"),
+    "ci0": ([128, 2, 256], "int32"), "cw": ([128, 2, 256], "int32"), "ci1": ([128, 512], "float32"),
+    "cu0": ([128, 512], "uint16"), "tm": ([128, 512], "float32"),
+    "wq": ([128, 832], "uint16"), "wn": ([128, 832], "uint16"),
     "off": ([128, 512], "uint16"), "of0": ([128, 512], "uint16"),
-    "rh": ([128, 80], "int32"), "lh": ([128, 80], "uint16"), "one": ([128, 256], "float32"),
-    "ri": ([128, 320], "int32"), "rd": ([128, 240], "float32"), "li": ([128, 240], "int32"),
-    "lq0": ([128, 240], "uint16"), "lq1": ([128, 240], "uint16"),
+    "rh": ([128, 320], "int32"), "one": ([128, 128], "float32"),
+    "li": ([128, 240], "int32"), "lq1": ([128, 240], "uint16"),
     "ua": ([128, 240], "int32"), "ub": ([128, 240], "int32"), "uu": ([128, 240], "uint16"),
-    "bf": ([128, 3, 80], "float32"), "pw": ([128, 240], "bfloat16"), "p2": ([128, 240], "bfloat16"),
-    "ef": ([128, 240], "int32"), "eg": ([128, 240], "float32"), "t1": ([128, 80], "float32"),
-    "t2": ([128, 80], "float32"), "t3": ([128, 80], "float32"), "t4": ([128, 80], "float32"),
+    "bf": ([128, 240], "float32"), "pw": ([128, 240], "bfloat16"), "p2": ([128, 240], "bfloat16"),
+    "t1": ([128, 80], "float32"), "t2": ([128, 80], "float32"),
     "so": ([128, 80], "uint16"), "cu": ([128, 80], "float32"), "cn": ([128, 80], "float32"),
-    "rc": ([128, 160], "float32"),
     "wd": ([128, 144], "bfloat16"), "wf": ([128, 144], "bfloat16"), "lm": ([128, 512], "bfloat16"),
-    "bones": ([128, 128], "bfloat16"), "ni": ([128, 128], "bfloat16"), "nh": ([128, 128], "bfloat16"),
-    "nv": ([128, 128], "bfloat16"), "mv": ([128, 128], "float32"),
-    "mi": ([128, 136], "int32"), "ma": ([128, 136], "int32"), "mb": ([128, 136], "int32"), "mc": ([128, 136], "int32"),
-    "mf": ([128, 136], "float32"), "mg": ([128, 136], "float32"),
-    "pf": ([128, 16], "float32"), "pb": ([128, 8], "bfloat16"),
+    "bo": ([128, 128], "bfloat16"), "bt": ([128, 8], "bfloat16"), "ni": ([128, 128], "bfloat16"),
+    "km": ([128, 144], "bfloat16"), "kp": ([128, 128], "bfloat16"),
+    "nv": ([128, 128], "bfloat16"), "mv": ([128, 128], "float32"), "mi": ([128, 8], "int32"),
+    "pf": ([128, 8], "float32"), "pb": ([128, 8], "bfloat16"),
     "thi": ([128, 1], "int32"), "thn": ([128, 2], "float32"), "thf": ([128, 2], "float32"),
 }
 SCRATCH = {k: ("sbuf", s, d) for k, (s, d) in _S.items()}
 for _k, _w, _d in (("o0", 16, "uint16"), ("o1", 16, "uint16"), ("o2", 16, "uint16"), ("o3", 16, "uint16"),
-                   ("r", 40, "int32"), ("p", 160, "int32"), ("c1", 64, "int32"),
-                   ("y0", 80, "float32"), ("y1", 80, "float32"), ("c", 10, "float32")):
+                   ("w", 64, "uint16"), ("r", 40, "uint16"), ("p", 160, "int32"), ("c", 10, "float32"),
+                   *(("y%d" % h, 2 * (CUT[h + 1] - CUT[h]), "float32") for h in range(PIECES))):
     SCRATCH["st" + _k] = ("dram", [8, 128, _w], _d)
     SCRATCH["ld" + _k] = ("dram", [8, 128, _w], _d)
 SCRATCH["stt"] = ("dram", [128, 1], "int32")
@@ -53,11 +53,11 @@ SCRATCH["ldt"] = ("dram", [8, 128, 1], "int32")
 SCRATCH["pp"] = ("psum", [128, 4096], "float32")
 PSUM = ("pp",)
 
-CLASSES = ("o0", "o1", "o2", "o3", "r", "p", "t", "c1", "y0", "y1", "c")
-TWO_CALLS = ("p", "c1", "y0", "y1", "r")
+CLASSES = ("o0", "o1", "o2", "o3", "w", "r", "p", "t", "c") + tuple("y%d" % h for h in range(PIECES))
+TWO_CALLS = ("p",)
 SEMAPHORES = (["q_v", "q_a", "q_t", "q_g", "sent"] + ["arr_" + k for k in CLASSES] + ["stg_" + k for k in CLASSES]
               + ["own_" + k for k in CLASSES] + ["get_" + k for k in CLASSES]
-              + ["rl0", "rl1", "rh0", "rh1", "fg0", "fg1", "xc0", "xc1", "in_r", "in_c", "in_d"]
+              + ["rl0", "rl1", "rh0", "rh1", "fg0", "fg1", "xc0", "xc1", "xq", "in_r", "in_c", "in_d", "in_w"]
               + [k + c + "2" for k in ("arr_", "stg_") for c in TWO_CALLS])
 
 
@@ -75,7 +75,8 @@ def plan(core, cores, topo, two):
         first = [(d, fe[2 * k:2 * k + 2]) for k, d in enumerate(far[:4])]
         second = [(d, fe[4 * k:4 * k + 4]) for k, d in enumerate(far[4:])]
         return [first, second + [(near[0], ne)]]
-    return [[(d, fe[k:k + 1]) for k, d in enumerate(far)] + [(near[0], ne)]]
+    return [[(d, fe[4 * k:4 * k + 4:2]) for k, d in enumerate(both)]
+            + [(d, fe[2 * k + 1:2 * k + 2]) for k, d in enumerate(far[2:])] + [(near[0], ne)]]
 
 
 def rank_program(g, core, T, topo):
@@ -127,7 +128,7 @@ def rank_program(g, core, T, topo):
             h.append((lo, hi, w, qn, s, val))
 
     def accs(rd, wr):
-        return [(n, a, b, False) for n, a, b in rd] + [(n, a, b, True) for n, a, b in wr]
+        return [(*b[:3], False) for b in rd] + [(*b[:3], True) for b in wr]
 
     def ops(qn, rd, wr, fns):
         s = csem[qn]
@@ -153,7 +154,7 @@ def rank_program(g, core, T, topo):
     def call_of(src, dst, c):
         return [k for k, call in enumerate(plan(src, cores, topo, c in TWO_CALLS)) if dst in [d for d, eng in call]][0]
 
-    def send(c, piece):
+    def send(c, piece=None):
         for k, call in enumerate(plan(core, cores, topo, c in TWO_CALLS)):
             if "stg_" + c + "2" * k in total:
                 need("g", "stg_" + c + "2" * k, None)
@@ -164,7 +165,7 @@ def rank_program(g, core, T, topo):
                 assert m & topo.mask(core, d) == m
                 tr.append(RemoteDMATransfer(dst_ids=[DstId(rid=rid, pnc=pid)], dma_engine_mask=m,
                                             remote_sem=sem["arr_" + c + "2" * k],
-                                            srcs=[piece(T.rank_of(d))], dsts=[T["ld" + c][q]]))
+                                            srcs=[piece or T["st" + c][T.rank_of(d)]], dsts=[T["ld" + c][q]]))
                 total["sent"] = total.get("sent", 0) + len(eng)
             g.remote_dma_fused(tr, local_sem=sem.sent)
         for k in range(1 + (c in TWO_CALLS)):
@@ -194,27 +195,30 @@ def rank_program(g, core, T, topo):
             for a, b in runs([T.rank_of(d) for d, eng in call]):
                 dma(qn, "stg_" + c + "2" * k, list(rd), [("st" + c, a, b)], T["st" + c][a:b], src[16 * a:16 * b, cols])
 
+    def hand(qn, c, own, src, to, a, b):
+        stage(qn, c, T[src], slice(a, b), [(src, a, b)])
+        dma(qn, own + c, [(src, a, b)], [(to, a, b)], T[to][mine, a:b], T[src][mine, a:b])
+
     def fetch(qn, c, to, cols, by_call=False):
         wr = [] if to in ("yx", "yc") else [(to, cols.start, cols.stop)]
         others = [o for o in cores if o != core]
         for part in ([[o for o in others if call_of(o, core, c) == k] for k in range(2)] if by_call else [others]):
             for a, b in runs([T.rank_of(o) for o in part]):
-                dma(qn, "get_" + c, [("ld" + c, a, b)], wr,
-                    T[to][16 * a:16 * b] if to == "ci1" else T[to][16 * a:16 * b, cols], T["ld" + c][a:b])
+                dma(qn, "get_" + c, [("ld" + c, a, b)], wr, T[to][16 * a:16 * b, cols], T["ld" + c][a:b])
 
-    dma("a", "in_r", [], [("rh", 0, 80)], T.rh[:], T.ray[:, 0:80])
-    for m in range(2):
-        dma("sa"[m], "in_c", [], [("ci0", 0, 128)], T.ci0[:, m, 0:128], T.cand[:, 256 * m:256 * m + 128])
+    dma("s", "stg_t", [], [("stt", 0, 8)], T.stt[:], T.th[:])
+    dma("a", "in_r", [], [("rh", 0, 320)], T.rh[:], T.ray[:])
     stage("s", "p", T.px, slice(0, R), by_call=True)
     for m in range(2):
-        dma("s", "in_d", [], [("ci0", 128, 256)], T.ci0[:, m, 128:256], T.cand[:, 256 * m + 128:256 * m + 256])
-    op("g", [], [("mi", 128, 129)], lambda e: e.iota(T.mi[:, 128:129], [[0, 1]], 0, 1))
-    op("g", [], [("cio", 3072, V)],
-       lambda e: e.iota(T.cio[:, 3072:V], [[1, 1024]], 3072, 0, allow_small_or_imprecise_dtypes=True))
-    send("p", lambda d: T.stp[d])
+        dma("a", "in_c", [], [("ci0", 0, 256)], T.ci0[:, m, 0:128], T.cand[:, 256 * m:256 * m + 128])
+    for m in range(2):
+        dma("s", "in_d", [], [("ci0", 256, 512)], T.ci0[:, m, 128:256], T.cand[:, 256 * m + 128:256 * m + 256])
+    dma("s", "own_t", [], [("ldt", q, q + 1)], T.ldt[q], T.th[:])
+    dma("s", "own_p", [], [("yi", 0, R)], T.yi[mine, :], T.px[mine, :])
+    dma("s", "in_w", [], [("cw", 0, 512)], T.cw[:], T.cand[:, 512:1024])
 
     def ap(b):
-        return T[b[0]][:, b[1]:b[2]]
+        return T[b[0]][:, b[1]:b[2]] if len(b) == 3 else T[b[0]][:, b[1]:b[2]:b[3]]
 
     def z(k, a, b):
         return ("pp", 2048 + 512 * k + a, 2048 + 512 * k + b)
@@ -237,8 +241,8 @@ def rank_program(g, core, T, topo):
     def copy(out, in_):
         op("v", [in_], [out], lambda e: e.tensor_copy(ap(out), ap(in_)))
 
-    def fill(out, c):
-        op("v", [], [out], lambda e: e.memset(ap(out), c))
+    def scan(out, d0, d1):
+        op("v", [d0, d1], [out], lambda e: e.tensor_tensor_scan(ap(out), ap(d0), ap(d1), 0.0, A.add, A.mult))
 
     def act(out, in_, scale=1.0, bias=0.0, func=AF.Identity):
         op("a", aps(in_, bias), [out], lambda e: e.activation(ap(out), ap(in_), func, bias=val(bias), scale=scale))
@@ -267,58 +271,63 @@ def rank_program(g, core, T, topo):
     def skip():
         pass
 
-    fill(("one", 0, 256), 1.0)
-    op("v", [("one", 0, 256)], [("cio", 0, 256)],
-       lambda e: e.tensor_tensor_scan(T.cio[:, 0:256], T.one[:], T.one[:], -1.0, A.add, A.mult))
+    c16, k255, hcol, c3r = (("pf", k, k + 1) for k in range(4))
+
+    def iota(out, pattern, base, view=None):
+        view = ap(out) if view is None else view
+        op("g", [], [out], lambda e: e.iota(view, pattern, base, 0, allow_small_or_imprecise_dtypes=True))
+
+    def select(out, in_, pattern, base, step=1, how=A.is_equal, rows=128):
+        op("g", [in_], [out], lambda e: e.affine_select(T[out[0]][0:rows, out[1]:out[2]], T[in_[0]][0:rows, in_[1]:in_[2]],
+                                                        pattern, how, 0.0, base, step))
+
+    def columns():
+        act(("pb", 0, 1), c16, scale=math.log(2.0), func=AF.Exp)
+        act(hcol, c16, scale=-1.0, bias=0.5, func=AF.Relu)
+        act(c3r, c16, bias=3.0 * R)
+        act(("wf", 0, 144), ("cio", 0, 144), scale=0.0, bias=("pb", 0, 1))
+
+    def carving():
+        iota(("kp", 0, 128), [[0, 128]], 2048)
+        for k in range(4):
+            select(("lm", 128 * k, 128 * k + 128), ("kp" if k > 1 else "km", 0, 128), [[0, 8], [-1, 8], [1000, 2]],
+                   -1000 * (k % 2), rows=8)
+        iota(("pre", 15, 16), [[0, 1]], 0)
+        iota(("c96", 0, 512), [[0, 512]], CAP)
+        select(("wf", 0, 144), ("wf", 0, 144), [[-16, 9], [-1000, 16]], 16, how=A.is_ge)
+        select(("wf", 0, 144), ("wf", 0, 144), [[16, 9], [0, 16]], -1, step=-1, how=A.is_ge)
+
+    def strides():
+        for k in (0, 4):
+            iota(("u5", 0, 400), [[0, 80]], k // 4, T.u5[:, :, k])
+        iota(("hx0", 0, 400), [[0, 400]], -R)
+        for a, b in zip(CUT, CUT[1:]):
+            iota(("hx1", 5 * a, 5 * b), [[0, 5 * (b - a)]], 16 * (b - a))
+
+    def origins():
+        act(("hx0", 4, 400, 5), ("cio", 0, 80), scale=16.0, bias=c3r)
+        for a, b in zip(CUT, CUT[1:]):
+            act(("hx1", 5 * a + 4, 5 * b, 5), ("cio", 0, b - a), scale=16.0, bias=c16)
+
+    op("g", [], [("mi", 0, 1)], lambda e: e.iota(T.mi[:, 0:1], [[0, 1]], 0, 1))
+    iota(("cio", 0, 256), [[1, 256]], 0)
+    iota(("cio", 3328, V), [[1, 768]], 3328)
+    send("t", T.stt[:])
+    iota(("km", 0, 144), [[0, 144]], -2048)
+    select(("wd", 0, 144), ("km", 0, 144), [[-16, 9], [1000, 16]], 16)
+    send("p")
+    select(("ni", 0, 128), ("km", 0, 128), [[-1, 128]], 0)
+    op("v", [], [("one", 0, 128)], lambda e: e.memset(T.one[:], 1.0))
+    ts(("mi", 1, 2), ("mi", 0, 1), 15, None, A.bitwise_and)
     ts(("cio", 256, 512), ("cio", 0, 256), 256.0, None, A.add)
-    for k in range(1, 5):
-        act(("cio", 512 * k, 512 * k + 512), ("cio", 0, 512), bias=512.0 * k)
-    ts(("cio", 2560, 3072), ("cio", 0, 512), 2560.0, None, A.add)
-    cols, allc = ("cio", 0, 128), 129
-    copy(("mi", 0, 128), cols)
-
-    def bits(to, shift, mask):
-        ts((to, 0, allc), ("mi", 0, allc), shift, mask, A.arith_shift_right, A.bitwise_and)
-
-    def col(k):
-        return ("pf", k, k + 1)
-
-    pcol, c16, k255, g16, dcol, tcol, hcol = (col(k) for k in range(7))
-    weights = [lambda: act(("pb", 0, 1), c16, scale=math.log(2.0), func=AF.Exp),
-               lambda: ts(col(9), c16, -1.0, pcol, A.mult, A.add),
-               lambda: ts(("nh", 0, 128), cols, pcol, -0.5, A.is_equal, A.mult),
-               lambda: ts(g16, col(9), 16.0, None, A.add),
-               lambda: ts(hcol, c16, 0.0, 0.5, A.is_equal, A.mult),
-               lambda: ts(("t1", 0, 80), ("cio", 0, 80), 16.0, c16, A.mult, A.add),
-               lambda: copy(col(12), ("pb", 0, 1)),
-               lambda: ts(("rc", 0, 80), ("t1", 0, 80), 1.0 / S, None, A.mult),
-               lambda: ts(("wf", 0, 144), ("cio", 0, 144), g16, col(12), A.is_equal, A.mult),
-               lambda: ts(("rc", 80, 160), ("t1", 0, 80), 1.0 / S, 3.0, A.mult, A.add)]
-    owners = [lambda: (bits("ma", 5, 3), bits("mc", 0, 1), bits("mb", 4, 1)),
-              lambda: (ts(("mf", 0, allc), ("ma", 0, allc), 2.0, None, A.mult),
-                       ts(col(10), ("ma", 128, 129), 32.0, None, A.mult)),
-              lambda: (tt(("mf", 0, allc), ("mf", 0, allc), ("mc", 0, allc), A.add),
-                       ts(col(11), c16, 2.0, col(10), A.mult, A.add)),
-              lambda: (ts(("bones", 0, 128), ("mf", 0, 128), ("mf", 128, 129), None, A.is_equal),
-                       tt(tcol, col(11), ("mb", 128, 129), A.add)),
-              lambda: (ts(("mv", 0, 128), cols, tcol, None, A.is_equal),
-                       bits("ma", 2, 3), bits("mb", 1, 1)),
-              lambda: ts(("mf", 0, 128), ("ma", 0, 128), 32.0, None, A.mult),
-              lambda: tt(("mf", 0, 128), ("mf", 0, 128), ("mb", 0, 128), A.add),
-              lambda: ts(("mg", 0, 128), ("mf", 0, 128), pcol, None, A.is_equal),
-              lambda: tt(("lm", 128, 256), ("mg", 0, 128), ("mc", 0, 128), A.mult),
-              lambda: tt(("lm", 0, 128), ("mg", 0, 128), ("lm", 128, 256), A.subtract),
-              lambda: ts(("lm", 256, 512), ("lm", 0, 256), -1.0, None, A.mult)]
-
-    def fills():
-        for k in range(3):
-            act(("xs", k * S + R, k * S + S), ("cio", 0, S - R))
-        for k in range(3):
-            fill(("xi", k * S + R, k * S + S), 0)
-        for b, at, c in (("xs", 0, D), ("xs", 3 * S, D), ("xh", 0, -1.0)):
-            fill((b, at + R, at + XW), c)
-        fill(("c96", 0, 512), float(CAP))
-        fill(("pre", 15, 16), 0.0)
+    act(("cio", 512, 768), ("cio", 0, 256), bias=512.0)
+    copy(c16, ("mi", 1, 2))
+    for at in range(768, 3328, 512):
+        if at < 2304:
+            act(("cio", at, at + 512), ("cio", 0, 512), bias=float(at))
+        else:
+            ts(("cio", at, at + 512), ("cio", 0, 512), float(at), None, A.add)
+    ts(k255, c16, -1.0, 255.0, A.mult, A.add)
 
     def extract(out, w, base, extra):
         n = out[2] - out[1]
@@ -326,61 +335,62 @@ def rank_program(g, core, T, topo):
         mms(out, [(w, 0, 144), ("wg", base, base + 16 * n), (extra[0], 0, 128), extra[1]],
             tr + [(T[extra[0]][:], ap(extra[1]))])
 
-    def prepare(src, parts):
-        n = 80 // parts
-
+    def prepare():
         def powers():
-            op("v", [("ub", 0, 240)], [("bf", 0, 240)], lambda e: e.tensor_copy(T.bf[:], T.ub[:]))
-            for h in range(parts):
-                op("a", [("bf", 0, 240)], [("pw", 3 * n * h, 3 * n * h + 3 * n)],
-                   lambda e: e.activation(T.pw[:, 3 * n * h:3 * n * h + 3 * n], T.bf[:, :, n * h:n * h + n], AF.Exp,
-                                          bias=0.0, scale=-math.log(2.0)))
-            op("a", [("bf", 0, 240)], [("p2", 0, 240)],
-               lambda e: e.activation(T.p2[:], T.bf[:], AF.Exp, bias=0.0, scale=math.log(2.0)))
+            copy(("bf", 0, 240), ("ub", 0, 240))
+            act(("pw", 0, 240), ("bf", 0, 240), scale=-math.log(2.0), func=AF.Exp)
+            act(("p2", 0, 240), ("bf", 0, 240), scale=math.log(2.0), bias=-12 * math.log(2.0), func=AF.Exp)
 
-        return [lambda: ts(("ub", 0, 240), src, 8, None, A.arith_shift_right), powers,
-                lambda: ts(("ua", 0, 240), src, 255, None, A.bitwise_and), lambda: copy(("uu", 0, 240), ("ua", 0, 240))]
+        return [lambda: ts(("ub", 0, 240), ("li", 0, 240), 8, None, A.arith_shift_right),
+                lambda: ts(("ua", 0, 240), ("li", 0, 240), 255, None, A.bitwise_and), powers,
+                lambda: copy(("uu", 0, 240), ("ua", 0, 240))]
 
-    def slots(t):
-        return [S * k for k in range(4)] if t == 0 else [S * (3 - k) for k in range(4)]
+    def slot(t, s, a, b):
+        if t == 0:
+            return ("xs", R * (3 - s) + 16 * a, R * (3 - s) + 16 * b)
+        return ("xs", 64 * a + 16 * (b - a) * s, 64 * a + 16 * (b - a) * (s + 1))
+
+    def start(t):
+        return ("xn", 0) if t else ("xs", 3 * R)
 
     def rest(qn, lst, a, b):
-        gather(qn, ("wr", 16 * a, 16 * b), ("cio", 0, V), (lst, a, b))
+        gather(qn, ("wr", 16 * a, 16 * b), ("cio", 0, V), lst)
 
-    def offsets(t, p):
-        op("v", [("ci%d" % t, 64 * p, 64 * p + 64)], [("cu%d" % t, 128 * p, 128 * p + 128)],
-           lambda e: e.tensor_copy(T["cu%d" % t][:, 128 * p:128 * p + 128], T["ci%d" % t][:, :, 64 * p:64 * p + 64]))
+    def offsets(to, src, *ps):
+        for p in ps:
+            op("v", [(src, 128 * p, 128 * p + 128)], [(to, 128 * p, 128 * p + 128)],
+               lambda e: e.tensor_copy(T[to][:, 128 * p:128 * p + 128], T[src][:, :, 64 * p:64 * p + 64]))
 
     def see(t, qn, p, *ks):
         for k in ks:
             c = 128 * p + 32 * k
-            gather(qn, ("wg", 16 * c, 16 * c + 512), ("wr", 0, R), ("cu%d" % t, c, c + 32), -(1024 * p + 512 * (k % 2) + 255.0))
+            gather(qn, ("wg", 16 * c, 16 * c + 512), ("wr", 0, R), ("wn" if t else "cu0", c, c + 32),
+                   -(1024 * p + 512 * (k % 2) + 255.0))
 
     def seen(p):
         extract(z(p, 0, 128), "wd", 2048 * p, ("ni", ("nv", 0, 128)))
 
     def lists(t, p):
-        tm = ("tm", 128 * p, 128 * p + 128)
-        return [lambda: op("v", [z(p, 0, 128), ("ci%d" % t, 64 * p, 64 * p + 64)], [tm],
-                           lambda e: e.tensor_tensor(ap(tm), ap(z(p, 0, 128)), T["ci%d" % t][:, :, 64 * p:64 * p + 64], A.max)),
+        tm, ci = ("tm", 128 * p, 128 * p + 128), ("ci%d" % t, 128 * p, 128 * p + 128)
+        return [lambda: op("v", [z(p, 0, 128), ci], [tm],
+                           lambda e: e.tensor_tensor(ap(tm), ap(z(p, 0, 128)),
+                                                     ap(ci) if t else T.ci0[:, :, 64 * p:64 * p + 64], A.max)),
                 lambda: ts(("off", tm[1], tm[2]), tm, float(R), None, A.min)]
 
     def ship(p, qn):
-        c, cs = "o%d" % p, slice(128 * p, 128 * p + 128)
-        stage(qn, c, T.off, cs, [("off", cs.start, cs.stop)])
-        dma(qn, "get_" + c, [("off", cs.start, cs.stop)], [("of0", cs.start, cs.stop)], T.of0[mine, cs], T.off[mine, cs])
-        send(c, lambda d: T["st" + c][d])
+        hand(qn, "o%d" % p, "get_", "off", "of0", 128 * p, 128 * p + 128)
+        send("o%d" % p)
 
     def twin(t):
-        a = slots(t)[0]
-        dma("s", "xc%d" % t, [("xs", a, a + R)], [("xh", 0, R)], T.xh[:, 0:R], T.xs[:, a:a + R])
+        b, a = start(t)
+        dma("s", "xc%d" % t, [(b, a, a + R)], [("xh", 0, R)], T.xh[:, 0:R], T[b][:, a:a + R])
 
     def window(t, b):
-        return ("xs", slots(t)[0], slots(t)[0] + XW) if b == "lo" else ("xh", 0, XW)
+        return (start(t)[0], start(t)[1], start(t)[1] + XW) if b == "lo" else ("xh", 0, XW)
 
-    def first(t, b, *ps, es=(0, 2)):
+    def first(t, b, *ps, es=(0, 2), qn="a"):
         for p in ps:
-            gather("a", (b, 1024 * p + 512 * es[0], 1024 * p + 512 * es[1]), window(t, b),
+            gather(qn, (b, 1024 * p + 512 * es[0], 1024 * p + 512 * es[1]), window(t, b),
                    ("off" if t else "of0", 128 * p + 32 * es[0], 128 * p + 32 * es[1]))
 
     def second(t, b, *ps, es=(0, 2)):
@@ -392,21 +402,22 @@ def rank_program(g, core, T, topo):
                 dma("s", "r%s%d" % (b[0], t), [(b, 1024 * p, 1024 * p + 1024)], [(to, 512 * a, 512 * a + 512)],
                     T[to][32 * p:32 * p + 32, 512 * a:512 * a + 512], T[b][grp(a), 1024 * p:1024 * p + 1024])
 
-    def lift(b, k):
-        at = 1024 * k + (2048 if b == "bh" else 0)
-        act(("pp", at, at + 1024), (b, 1024 * k, 1024 * k + 1024))
+    def bank(b, k):
+        at = 512 * k + (2048 if b == "bh" else 0)
+        return ("pp", at, at + 512)
+
+    def lift(b, *ks):
+        for k in ks:
+            act(bank(b, k), (b, 512 * k, 512 * k + 512))
 
     def fold(b, o, last):
-        def pp(lo, hi):
-            return ("pp", lo + (2048 if b == "bh" else 0), hi + (2048 if b == "bh" else 0))
-        return [lambda: tt(("s1", 0, 1024), pp(0, 1024), (b, 2048, 3072), o),
-                lambda: tt(pp(0, 1024), pp(1024, 2048), (b, 3072, 4096), o),
-                lambda: tt(("s2", 0, 512), pp(0, 512), ("s1", 0, 512), o),
-                lambda: tt(pp(1024, 1536), pp(512, 1024), ("s1", 512, 1024), o),
-                lambda: tt(last, pp(1024, 1536), ("s2", 0, 512), o)]
+        s1, s2, s3 = (("s1", 512 * k, 512 * k + 512) for k in range(3))
+        to = [s1, bank(b, 1), s2, bank(b, 3)]
+        return ([lambda k=k: tt(to[k], bank(b, k), (b, 2048 + 512 * k, 2560 + 512 * k), o) for k in range(4)]
+                + [lambda: tt(s3, to[1], s1, o), lambda: tt(to[3], to[3], s2, o), lambda: tt(last, to[3], s3, o)])
 
     def spread(t):
-        act(("fb", 0, 512), ("lof", 0, 512), scale=-0.25 if t else -0.2, bias=-0.375 if t else -0.3)
+        act(("fb", 0, 512), ("lof", 0, 512), scale=-0.2, bias=-0.375)
         for a in range(8):
             for p in range(4):
                 dma("s", "fg%d" % t, [("fb", 0, 512)], [("et", 1024 * p, 1024 * p + 1024)],
@@ -414,238 +425,220 @@ def rank_program(g, core, T, topo):
 
     def count():
         tt(("far", 0, 512), ("pp", 0, 512), ("lt", 0, 512), A.is_gt)
-        mms(z(0, 0, 512), [("bones", 0, 128), ("far", 0, 512)], [(T.bones[:], T.far[:])])
+        ops("t", [("bt", 0, 8), ("far", 0, 512)], [z(0, 0, 512)],
+            [lambda e: e.matmul(T.pp[0:8, 2048:2560], T.bt[:], T.far[:], True, True)])
 
-    def carve():
-        ts(("odd", 0, 512), z(0, 0, 512), float(NEED), None, A.is_ge)
+    def odd():
+        op("v", [z(0, 0, 512)], [("odd", 0, 512)],
+           lambda e: e.tensor_scalar(T.odd[0:8, :], T.pp[0:8, 2048:2560], float(NEED), None, A.is_ge))
+
+    def running():
         op("v", [("odd", 0, 512), ("c96", 0, 512)], [("pre", 16, 528)],
-           lambda e: e.tensor_tensor_scan(T.pre[:, 16:528], T.odd[:], T.c96[:], 0.0, A.add, A.min))
+           lambda e: e.tensor_tensor_scan(T.pre[0:8, 16:528], T.odd[0:8, :], T.c96[0:8, :], 0.0, A.add, A.min))
         mms(z(2, 0, 256), [("lm", 0, 512), ("pre", 0, 528)],
-            [(T.lm[:, 128 * k:128 * k + 128], T.pre[:, 16 - k // 2 + 256 * (k % 2):272 - k // 2 + 256 * (k % 2)])
+            [(T.lm[0:8, 128 * k:128 * k + 128], T.pre[0:8, 16 - k // 2 + 256 * (k % 2):272 - k // 2 + 256 * (k % 2)])
              for k in range(4)])
-        act(("ft", 0, 256), z(2, 0, 256), bias=hcol)
+        act(("ft", 0, 256), z(2, 0, 256), scale=-2.0 ** -11, bias=hcol)
 
-    def step(t, s, h):
-        a, b, to = 640 * h, 640 * h + 640, slots(t)[s + 1]
-        lst = ("lq%d" % t, 80 * s + 40 * h, 80 * s + 40 * h + 40)
+    def middle(t, spare):
+        spare = list(spare) + [skip] * 6
+        lift("bl", 0, 1, 2, 3)
+        weave(fold("bl", A.min, ("lof", 0, 512)), [skip] * 5 + spare[:2])
+        lift("bh", 0, 1)
+        spread(t)
+        lift("bh", 2, 3)
+        act(("lt", 0, 512), ("lof", 0, 512), bias=("thf", 0, 1))
         if t == 0:
-            return [lambda: tt_gather(("x5", a, b), ("et", 0, V), lst, ("xi", to - S + a, to - S + b), A.add),
-                    lambda: ts(("xi", to + a, to + b), ("x5", a, b), 1.25, 0.0, A.mult, A.max)]
-        return [lambda: tt_gather(("yi", a, b), ("et", 0, V), lst, ("x5", a, b), A.add),
-                lambda: ts(("xs", to + a, to + b), ("yi", a, b), 0.0, float(TOP), A.max, A.min)]
+            origins()
+        weave(fold("bh", A.max, ("pp", 0, 512)) + [count, odd, running], [skip] * 5 + spare[2:6])
 
-    def five(s, h):
-        a, b, at = 640 * h, 640 * h + 640, slots(1)[s]
-        act(("x5", a, b), ("xs", at + a, at + b), scale=1.25)
+    def step(t, s, a, b):
+        y, x = ("yi", 16 * a, 16 * b), slot(t, s, a, b) if s or not t else ("xn", 16 * a, 16 * b)
+        at = 80 * s + (0 if t else 512)
+        return [lambda: tt_gather(y, ("et", 0, V), ("lq1" if t else "wn", at + a, at + b), x, A.add),
+                lambda: ts(slot(t, s + 1, a, b), y, 1.25, 1.25 * TOP, A.mult, A.min)]
 
-    def flags(qn, s, a, b):
-        gather(qn, ("wg", R * s + 16 * a, R * s + 16 * b), ("ft", 0, 256), ("uu", 80 * s + a, 80 * s + b))
+    def flags(word, *parts):
+        for qn, a, b in parts:
+            gather(qn, ("wg", 48 * a, 48 * b), ("ft", 0, 256), ("uu", 3 * a, 3 * b))
+        a, b = parts[0][1], parts[-1][2]
+        extract(word, "wf", 48 * a, ("ni", ("p2", 3 * a, 3 * b)))
 
-    def flagged(k, s, a, b):
-        extract(z(k, (b - a) * s, (b - a) * (s + 1)), "wf", R * s + 16 * a, ("nh", ("p2", 80 * s + a, 80 * s + b)))
+    def tests(word, a, b):
+        five = (5 * a, 5 * b)
+        return [lambda: op("v", [word, ("pw", 3 * a, 3 * b)], [("u5", *five)],
+                           lambda e: e.tensor_tensor(T.u5[:, a:b, 1:4], ap(word), T.pw[:, 3 * a:3 * b], A.mult)),
+                lambda: op("v", [("u5", *five)], [("e5", *five)],
+                           lambda e: e.tensor_scalar(ap(("e5", *five)), T.u5[:, a:b, :], 1, None, A.bitwise_and)),
+                lambda: copy(("he", *five), ("e5", *five))]
 
-    def tests(at, n):
-        return [("ef", at + n * s, at + n * s + n) for s in range(3)]
+    def horner(to, lst, d0, a, b):
+        return [lambda: scan((to, 5 * a, 5 * b), (d0, 5 * a, 5 * b), ("he", 5 * a, 5 * b)),
+                lambda: copy((lst, a, b), (to, 5 * a + 4, 5 * b, 5))]
 
-    def pick(t, qn, a, b):
-        if t:
-            return gather(qn, ("wr", 16 * a, 16 * b), ("xs", 0, 3 * S + R), ("so", a, b))
-        out, win = ("xs", 3 * S + 16 * a, 3 * S + 16 * b), ("xi", 0, 3 * S + R)
-        op("v", [win, ("so", a, b)], [out],
-           lambda e: e.tensor_scalar(ap(out), ap(win).indirect(T.so[:, a:b]), float(TOP), None, A.min))
+    def pick(t, qn, a, b, win):
+        out, scale = ("wr" if t else "xn", 16 * a, 16 * b), 0.8 if t else 1.0
+        if qn == "a":
+            op("a", [win, ("so", a, b)], [out],
+               lambda e: e.activation(ap(out), ap(win).indirect(T.so[:, a:b]), AF.Relu, bias=0.0, scale=scale))
+        else:
+            op("v", [win, ("so", a, b)], [out],
+               lambda e: e.tensor_scalar(ap(out), ap(win).indirect(T.so[:, a:b]), scale, 0.0, A.mult, A.max))
 
-    copy(pcol, ("mi", 128, 129))
-    bits("ma", 0, 15)
-    bits("mb", 0, 31)
-    copy(c16, ("ma", 128, 129))
-    copy(("lh", 0, 80), ("rh", 0, 80))
-    ts(k255, c16, -1.0, 255.0, A.mult, A.add)
-    ts(col(8), c16, -1000.0, pcol, A.mult, A.add)
-    rest("a", "lh", 0, 40)
-    offsets(0, 0)
-    ts(dcol, col(8), 16.0, None, A.add)
-    rest("v", "lh", 40, 80)
-    ts(("ni", 0, 128), cols, pcol, -2048.0, A.is_equal, A.mult)
-    see(0, "a", 0, 0, 1)
-    see(0, "v", 0, 2)
-    ts(("wd", 0, 144), ("cio", 0, 144), dcol, -2048.0, A.is_equal, A.mult)
-    ts(("nv", 0, 128), ("mb", 0, 128), -16.0, k255, A.mult, A.add)
-    see(0, "v", 0, 3)
+    copy(("wq", 512, 832), ("rh", 0, 320))
+    hand("s", "r", "own_", "wq", "wn", 512, 832)
+    send("r")
+    for b, at, c in (("xs", 3 * R, D), ("xh", 0, -1), ("xn", 0, D)):
+        iota((b, at + R, at + XW), [[0, XW - R]], int(c))
+    select(("mv", 0, 128), ("one", 0, 128), [[-32, 4], [-1, 16], [-16, 2]], 0)
+    select(("bo", 0, 128), ("km", 0, 128), [[-2, 4], [0, 16], [-1, 2]], 0, rows=8)
+    offsets("cu0", "ci0", 0)
+    rest("a", ("wq", 512, 552), 0, 40)
+    rest("v", ("wq", 552, 592), 40, 80)
+    offsets("cu0", "ci0", 1)
+    for k in range(4):
+        act(("nv", 32 * k, 32 * k + 32), ("cio", 0, 32), scale=-16.0, bias=k255)
+    see(0, "a", 0, 0)
+    see(0, "v", 0, 1, 2, 3)
     seen(0)
-    offsets(0, 1)
-    see(0, "a", 1, 0, 1)
-    offsets(0, 2)
-    see(0, "v", 1, 2, 3)
+    see(0, "a", 1, 0, 1, 2)
+    offsets("cu0", "ci0", 2, 3)
+    see(0, "v", 1, 3)
     seen(1)
-    offsets(0, 3)
-    for p in (2, 3):
-        see(0, "a", p, 0, 1, 2)
-        weave(lists(0, p - 2), [lambda: see(0, "v", p, 3)])
-        ship(p - 2, "s")
-        seen(p)
-    weave(owners[:2], weights[:2])
-    weave(lists(0, 2), owners[2:4])
-    ship(2, "s")
-    weave(owners[4:6], weights[2:4])
-    weave(lists(0, 3), owners[6:8])
+    see(0, "a", 2, 0, 1)
+    see(0, "v", 2, 3)
+    weave(lists(0, 0), [lambda: see(0, "v", 2, 2)])
+    ship(0, "s")
+    seen(2)
+    weave(lists(0, 1), [lambda: see(0, "v", 3, 2), lambda: see(0, "v", 3, 3)])
+    ship(1, "s")
+    see(0, "a", 3, 0, 1)
+    seen(3)
+    ops("t", [("bo", 0, 128), ("ni", 0, 128)], [("pp", 0, 8)],
+        [lambda e: e.matmul(T.pp[:, 0:8], T.bo[0:8, :], T.ni[0:8, 0:8], True, True)])
+    fetch("s", "p", "yi", slice(0, R), True)
+    columns()
+    weave(lists(0, 2), [lambda: offsets("wq", "cw", 0), lambda: offsets("wq", "cw", 1, 2)])
+    ship(2, "a")
+    dma("a", "get_t", [("ldt", 0, 8)], [("thi", 0, 1)], T.thi[:], T.ldt[:, mine, :])
+    fetch("a", "r", "wn", slice(512, 832))
+    weave(lists(0, 3), [lambda: offsets("wq", "cw", 3)])
     ship(3, "a")
-    fills()
-    dma("s", "get_p", [], [("xi", 0, R)], T.xi[mine, 0:R], T.px[mine, :])
-    fetch("s", "p", "xi", slice(0, R), True)
-    weave(owners[8:], weights[4:])
-    copy(("xs", 0, R), ("xi", 0, R))
-    for p in range(4):
+    hand("a", "w", "own_", "wq", "wn", 0, 512)
+    fetch("s", "o0", "of0", slice(0, 128))
+    act(("bt", 0, 8), ("pp", 0, 8), scale=2.0 ** -22)
+    ts(slot(0, 0, 0, 80), ("yi", 0, R), 1.25, None, A.mult)
+    ts(("thn", 0, 1), ("thi", 0, 1), 1.25, None, A.mult)
+    ts(("thn", 1, 2), ("thi", 0, 1), 1.25, None, A.mult)
+    mms(z(3, 0, 2), [("mv", 0, 128), ("thn", 0, 2)], [(T.mv[:], T.thn[:])])
+    l0, l1, l2 = (("li", 2 - s, 240, 3) for s in range(3))
+    d0, d1, d2 = (("hv", 3 - s, 400, 5) for s in range(3))
+    for s, to in enumerate((l0, l1, l2, ("hv", 0, 400, 5))):
+        copy(to, ("wn", 512 + 80 * s, 592 + 80 * s))
+    copy(("hv", 4, 400, 5), ("wn", 512, 592))
+    carving()
+    strides()
+    for p in range(1, 4):
         fetch("s", "o%d" % p, "of0", slice(128 * p, 128 * p + 128))
     twin(0)
-    dma("s", "stg_t", [], [("stt", 0, 8)], T.stt[:], T.th[:])
-    dma("s", "own_t", [], [("ldt", q, q + 1)], T.ldt[q], T.th[:])
-    stage("s", "r", T.ray, slice(0, 320))
-    dma("s", "get_r", [], [("ri", 0, 320)], T.ri[mine, :], T.ray[mine, :])
-    send("t", lambda d: T.stt[:])
-    send("r", lambda d: T["str"][d])
     for es in ((0, 1), (1, 2)):
         first(0, "lo", 0, es=es)
         second(0, "lo", 0, es=es)
     first(0, "lo", 1, 2, 3)
     second(0, "lo", 1, 2, 3)
-    dma("s", "get_t", [("ldt", 0, 8)], [("thi", 0, 1)], T.thi[:], T.ldt[:, mine, :])
-    fetch("s", "r", "ri", slice(0, 320))
     first(0, "hi", 0, 1, 2, 3)
     second(0, "hi", 0, 1, 2, 3)
-    stage("s", "c1", T.cand, slice(512, 1024))
-    dma("s", "get_c1", [], [("ci1", 0, 256)], T.ci1[mine], T.cand[mine, 512:1024])
-    send("c1", lambda d: T.stc1[d])
-    lift("bl", 0)
-    lift("bl", 1)
-    copy(("thn", 0, 1), ("thi", 0, 1))
-    copy(("thn", 1, 2), ("thi", 0, 1))
-    mms(z(3, 0, 2), [("mv", 0, 128), ("thn", 0, 2)], [(T.mv[:], T.thn[:])])
-    weave(fold("bl", A.min, ("lof", 0, 512)),
-          [skip, lambda: copy(("thf", 0, 2), z(3, 0, 2)), skip, lambda: copy(("lq0", 0, 240), ("ri", 0, 240))])
-    lift("bh", 0)
-    spread(0)
-    fetch("s", "c1", "ci1", slice(0, 256))
-    lift("bh", 1)
-    act(("lt", 0, 512), ("lof", 0, 512), bias=("thf", 0, 1))
-    weave(fold("bh", A.max, ("pp", 0, 512)), prepare(("ri", 0, 240), 1))
-    count()
-    tt(("rd", 0, 240), ("ri", 80, 320), ("ri", 0, 240), A.subtract)
-    carve()
-    for s in range(3):
-        flags("a", s, 0, 40)
-        flags("v", s, 40, 80)
-        flagged(0 if s == 2 else 1, s, 0, 80)
-    ahead = step(0, 0, 0), step(0, 0, 1)
-    ahead[0][0]()
-    e1, e2, e3 = tests(0, 80)
-    weave([lambda: tt(("ua", 0, 160), z(1, 0, 160), ("pw", 0, 160), A.mult),
-           lambda: ts(("ef", 0, 160), ("ua", 0, 160), 1, None, A.bitwise_and),
-           lambda: (tt(e2, e2, e1, A.mult), tt(("t1", 0, 80), e1, ("rd", 0, 80), A.mult),
-                    tt(("ua", 160, 240), z(0, 160, 240), ("pw", 160, 240), A.mult)),
-           lambda: (tt(("eg", 80, 160), e2, ("rd", 80, 160), A.mult), tt(("t1", 0, 80), ("t1", 0, 80), ("ri", 0, 80), A.add),
-                    ts(e3, ("ua", 160, 240), 1, None, A.bitwise_and), tt(("t2", 0, 80), e2, ("rd", 160, 240), A.mult)),
-           lambda: (tt(("t1", 0, 80), ("t1", 0, 80), ("eg", 80, 160), A.add), tt(("t2", 0, 80), ("t2", 0, 80), e3, A.mult)),
-           lambda: tt(("li", 0, 80), ("t1", 0, 80), ("t2", 0, 80), A.add),
-           lambda: copy(("lq1", 0, 80), ("li", 0, 80))],
-          [lambda: offsets(1, 0), skip, skip, skip, skip, lambda: offsets(1, 1)])
+    act(("thf", 0, 2), z(3, 0, 2))
+    ready = prepare()
+    middle(0, ready + [lambda: (tt(d0, l1, l0, A.subtract), tt(d1, l2, l1, A.subtract)),
+                       lambda: tt(d2, ("hv", 0, 400, 5), l2, A.subtract)])
+    need("g", "fg0", None)
+    send("w")
+    fetch("s", "w", "wn", slice(0, 512))
 
-    rest("a", "lq1", 0, 80)
-    weave(ahead[1], [lambda: tt(e3, e3, e2, A.mult), ahead[0][1]])
-    offsets(1, 2)
-    offsets(1, 3)
+    halves = ((0, 40), (40, 80))
+    steps0 = [[step(0, s, a, b) for a, b in halves] for s in range(3)]
+    flags(z(0, 0, 120), ("a", 0, 20), ("v", 20, 40))
+    flags(z(1, 0, 120), ("a", 40, 80))
+    steps0[0][0][0]()
+    steps0[0][1][0]()
+    weave(tests(z(0, 0, 120), 0, 40) + horner("hs", "lq1", "hv", 0, 40),
+          [steps0[0][0][1], skip, steps0[0][1][1]])
+    rest("a", ("lq1", 0, 40), 0, 40)
+    weave(tests(z(1, 0, 120), 40, 80) + horner("hs", "lq1", "hv", 40, 80),
+          [skip, lambda: copy(("ci1", 0, 256), ("wn", 0, 256)), skip, lambda: copy(("ci1", 256, 512), ("wn", 256, 512))])
+    rest("a", ("lq1", 40, 80), 40, 80)
+
+    weave(*steps0[1])
     see(1, "a", 0, 0, 1, 2, 3)
     seen(0)
-    weave(step(0, 1, 0), step(0, 1, 1))
     see(1, "a", 1, 0, 1, 2, 3)
     seen(1)
-    weave([lambda: (tt(("t3", 0, 80), ("rc", 0, 80), e1, A.add), tt(("t4", 0, 80), e2, e3, A.add)),
-           lambda: tt(("t3", 0, 80), ("t3", 0, 80), ("t4", 0, 80), A.add),
-           lambda: ts(("so", 0, 80), ("t3", 0, 80), float(S), None, A.mult)], step(0, 2, 0), step(0, 2, 1))
+    weave(*steps0[2], horner("hc", "so", "hx0", 0, 80))
     see(1, "a", 2, 0, 1, 2, 3)
-    seen(2)
-    weave(lists(1, 0), [lambda: pick(0, "v", 0, 40), lambda: pick(0, "v", 40, 80)])
+    weave(lists(1, 0), [lambda: pick(0, "v", 0, 40, ("xs", 0, 4 * R)), lambda: pick(0, "v", 40, 80, ("xs", 0, 4 * R))])
     twin(1)
-    see(1, "a", 3, 2)
-    first(1, "lo", 0)
-    weave(lists(1, 1), [lambda: see(1, "v", 3, 0), lambda: see(1, "v", 3, 1, 3)])
+    for a, b in zip(CUT, CUT[1:]):
+        dma("s", "xq", [("xn", 0, R)], [slot(1, 0, a, b)], ap(slot(1, 0, a, b)), T.xn[:, 16 * a:16 * b])
+    seen(2)
+    see(1, "a", 3, 0, 1, 2, 3)
     seen(3)
+    weave(lists(1, 1), [lambda: first(1, "lo", 0, qn="v"), lambda: second(1, "lo", 0)])
     first(1, "lo", 1)
-    weave(lists(1, 2), [lambda: second(1, "lo", 0)])
+    weave(lists(1, 2), [lambda: first(1, "hi", 0, qn="v"), lambda: second(1, "hi", 0)])
     first(1, "lo", 2)
-    weave([lambda: second(1, "lo", 1)] + lists(1, 3))
+    weave(lists(1, 3), [lambda: second(1, "lo", 1)])
     first(1, "lo", 3)
+    first(1, "hi", 1, 2, 3)
     second(1, "lo", 2, 3)
-    first(1, "hi", 0, 1, 2, 3)
-    second(1, "hi", 0, 1, 2, 3)
-    lift("bl", 0)
-    lift("bl", 1)
-    five(0, 0)
-    five(0, 1)
-    weave(fold("bl", A.min, ("lof", 0, 512)),
-          [lambda: (ts(("cu", 0, 80), ("t3", 0, 80), 3.0, None, A.add), tt(("t2", 0, 80), e1, ("rd", 160, 240), A.mult)),
-           lambda: tt(("eg", 0, 160), ("ef", 0, 160), ("rd", 80, 240), A.mult),
-           lambda: tt(("li", 160, 240), ("t2", 0, 80), ("ri", 160, 240), A.add),
-           lambda: tt(("t1", 0, 80), ("eg", 0, 80), ("eg", 80, 160), A.add)])
-    lift("bh", 0)
-    spread(1)
-    lift("bh", 1)
-    act(("lt", 0, 512), ("lof", 0, 512), bias=("thf", 0, 1))
-    tt(("li", 80, 160), ("t1", 0, 80), ("ri", 80, 160), A.add)
-    weave(fold("bh", A.max, ("pp", 0, 512)), prepare(("li", 0, 240), 2))
-    count()
-    copy(("lq1", 80, 240), ("li", 80, 240))
-    carve()
+    second(1, "hi", 1, 2, 3)
+    e0, e1, t1, t2 = ("he", 3, 400, 5), ("he", 2, 400, 5), ("t1", 0, 80), ("t2", 0, 80)
+    ready = prepare()
+    middle(1, [lambda: (tt(t1, e1, d2, A.mult), tt(t2, e0, d2, A.mult), copy(l0, ("hs", 4, 400, 5))),
+               lambda: (tt(t1, t1, d1, A.add), tt(l2, l2, t2, A.add), tt(t1, t1, e0, A.mult),
+                        copy(("lq1", 160, 240), l2), tt(l1, l1, t1, A.add)),
+               ready[0], ready[1], lambda: (ready[2](), ready[3]()), lambda: copy(("lq1", 80, 160), l1)])
+
+    def word(h):
+        return z(h, 0, 3 * (CUT[h + 1] - CUT[h]))
+
+    def last_flags(h):
+        flags(word(h), ("a", CUT[h], CUT[h + 1]))
 
     def settle(h):
-        at, a, b = 120 * h, 40 * h, 40 * h + 40
-        e1, e2, e3 = tests(at, 40)
-        t3 = ("t3", a, b)
-        return ([lambda: tt(("ua", at, at + 80), z(1 + 2 * h, 0, 80), ("pw", at, at + 80), A.mult),
-                 lambda: ts(("ef", at, at + 80), ("ua", at, at + 80), 1, None, A.bitwise_and),
-                 lambda: (tt(e2, e2, e1, A.mult), tt(t3, ("rc", 80 + a, 80 + b), e1, A.subtract)),
-                 lambda: tt(t3, t3, e2, A.subtract)],
-                [lambda: tt(("ua", at + 80, at + 120), z(2 * h, 80, 120), ("pw", at + 80, at + 120), A.mult),
-                 lambda: ts(e3, ("ua", at + 80, at + 120), 1, None, A.bitwise_and),
-                 lambda: tt(e3, e3, e2, A.mult),
-                 lambda: tt(t3, t3, e3, A.subtract),
-                 lambda: ts(("so", a, b), t3, float(S), None, A.mult)])
+        return tests(word(h), CUT[h], CUT[h + 1]) + horner("hs", "so", "hx1", CUT[h], CUT[h + 1])
 
-    def last_flags(s, h):
-        flags("a", s, 40 * h, 40 * h + 40)
-        flagged(2 * h + (s < 2), s, 40 * h, 40 * h + 40)
+    def steps(s, h):
+        return step(1, s, CUT[h], CUT[h + 1])
 
-    (early0, late0), (early1, late1) = settle(0), settle(1)
-    for s in range(3):
-        last_flags(s, 0)
-    weave(step(1, 0, 0), step(1, 0, 1))
-    five(1, 0)
-    five(1, 1)
-    last_flags(0, 1)
-    weave(step(1, 1, 0) + step(1, 1, 1), early0, [skip, skip] + late0[:2])
-    five(2, 0)
-    last_flags(1, 1)
-    five(2, 1)
-    last_flags(2, 1)
-    weave(late0[2:], step(1, 2, 0), [skip] + early1[:2])
-    pick(1, "a", 0, 40)
-    stage("s", "y0", T.wr, slice(0, 640), [("wr", 0, 640)], True)
-    last = step(1, 2, 1)
-    weave(early1[2:3], last[:1], late1[:1])
-    weave(early1[3:] + late1[1:], [skip, last[1]])
-    pick(1, "a", 40, 60)
-    tt(("t1", 0, 80), ("cu", 0, 80), ("t3", 0, 80), A.subtract)
-    pick(1, "v", 60, 80)
-    stage("a", "y1", T.wr, slice(640, R), [("wr", 640, R)], True)
-    ts(("cn", 0, 80), ("t1", 0, 80), 3.0, None, A.min)
+    def leave(h, qn="a"):
+        a, b, c = CUT[h], CUT[h + 1], "y%d" % h
+        pick(1, qn, a, b, ("xs", 64 * a, 64 * b))
+        stage("s", c, T.wr, slice(16 * a, 16 * b), [("wr", 16 * a, 16 * b)])
+        send(c)
 
+    size = 16.0 * (CUT[1] - CUT[0])
+    for h in range(3):
+        last_flags(h)
+    weave(steps(0, 0) + steps(1, 0) + steps(2, 0), steps(0, 1) + steps(1, 1))
+    weave(settle(0), steps(2, 1) + steps(0, 2))
+    leave(0)
+    last_flags(3)
+    weave(settle(1), steps(1, 2) + steps(2, 2))
+    leave(1)
+    weave(settle(2), steps(0, 3) + steps(1, 3) + [lambda: ts(t1, ("hc", 3, 400, 5), -size / R, None, A.mult)])
+    leave(2)
+    weave(settle(3)[:4] + [lambda: tt(t1, t1, ("hs", 3, 400, 5), A.add),
+                           lambda: ts(("cn", 0, 80), t1, 3 * size, 1 / size, A.min, A.mult)],
+          steps(2, 3) + [skip, skip] + settle(3)[4:])
     dma("s", "stg_c", [("cn", 0, 80)], [("stc", 0, 8)], T.stc[:], T.cn[:])
-    send("y0", lambda d: T.sty0[d])
-    send("y1", lambda d: T.sty1[d])
-    send("c", lambda d: T.stc[d])
+    send("c")
+    leave(3)
+
     dma("s", "own_y0", [("wr", 0, R)], [], T.yx[mine, :], T.wr[mine, :])
-    dma("s", "own_c", [("cn", 0, 80)], [], T.yc[mine, :], T.cn[mine, :])
-    fetch("s", "y0", "yx", slice(0, 640))
-    fetch("s", "y1", "yx", slice(640, R), True)
+    dma("a", "own_c", [("cn", 0, 80)], [], T.yc[mine, :], T.cn[mine, :])
+    for h in range(PIECES):
+        fetch("s", "y%d" % h, "yx", slice(16 * CUT[h], 16 * CUT[h + 1]))
     fetch("a", "c", "yc", slice(0, 80))
     for s in total:
         need("g", s, total[s])

@@ -6,45 +6,46 @@ A = AluOpType
 AF = ActivationFunctionType
 V, R, RO, H, CAP, NEED = 4096, 1280, 2, 3, 96, 9
 TOP = 2 ** 20 - 1
-D = float(2 ** 21)
-XW = R + 8
+D = 2 ** 21
+XB, XH = 0, R + 8
 CUT = (0, 20, 40, 60, 80)
 PIECES = len(CUT) - 1
 
 _S = {
     "et": ([128, V], "float32"),
-    "cio": ([128, V], "float32"),
+    "cio": ([128, V + R], "float32"),
     "wg": ([128, 4 * 2048], "bfloat16"),
     "lo": ([128, V], "float32"), "hi": ([128, V], "float32"),
     "bl": ([128, V], "float32"), "bh": ([128, V], "float32"),
-    "xs": ([128, 3 * R + XW], "float32"), "xn": ([128, XW], "float32"), "xh": ([128, XW], "float32"),
+    "xn": ([128, 2 * R + 16], "int32"),
+    "xi": ([128, 4 * R + 8], "int32"), "x5": ([128, R], "float32"),
     "s1": ([128, 1536], "float32"), "fb": ([128, 512], "float32"),
-    "wr": ([128, R], "float32"), "ft": ([128, 256], "bfloat16"), "yi": ([128, R], "int32"),
-    "u5": ([128, 80, 5], "int32"), "e5": ([128, 400], "int32"), "he": ([128, 400], "float32"),
-    "hv": ([128, 400], "float32"), "hx0": ([128, 400], "float32"), "hx1": ([128, 400], "float32"),
-    "hs": ([128, 400], "float32"), "hc": ([128, 400], "float32"),
+    "ft": ([128, 256], "bfloat16"),
+    "u6": ([128, 80, 6], "int32"), "e6": ([128, 480], "int32"), "he": ([128, 480], "float32"),
+    "hv": ([128, 480], "float32"), "hx0": ([128, 480], "float32"), "hx1": ([128, 480], "float32"),
+    "hs": ([128, 480], "float32"), "hc": ([128, 480], "float32"),
     "lof": ([128, 512], "float32"), "lt": ([128, 512], "float32"), "odd": ([128, 512], "bfloat16"),
     "pre": ([128, 528], "bfloat16"), "c96": ([128, 512], "bfloat16"), "far": ([128, 512], "bfloat16"),
-    "ci0": ([128, 2, 256], "int32"), "cw": ([128, 2, 256], "int32"), "ci1": ([128, 512], "float32"),
+    "ci0": ([128, 2, 256], "int32"), "cw": ([128, 2, 256], "int32"), "ci1": ([128, 2, 256], "int32"),
     "cu0": ([128, 512], "uint16"), "tm": ([128, 512], "float32"),
     "wq": ([128, 832], "uint16"), "wn": ([128, 832], "uint16"),
     "off": ([128, 512], "uint16"), "of0": ([128, 512], "uint16"),
     "rh": ([128, 320], "int32"), "one": ([128, 128], "float32"),
-    "li": ([128, 240], "int32"), "lq1": ([128, 240], "uint16"),
-    "ua": ([128, 240], "int32"), "ub": ([128, 240], "int32"), "uu": ([128, 240], "uint16"),
+    "li": ([128, 240], "float32"), "lq1": ([128, 240], "uint16"), "uu": ([128, 240], "uint16"),
+    "rf": ([128, 320], "float32"), "rn": ([128, 240], "float32"), "eye": ([128, 128], "float32"),
     "bf": ([128, 240], "float32"), "pw": ([128, 240], "bfloat16"), "p2": ([128, 240], "bfloat16"),
     "t1": ([128, 80], "float32"), "t2": ([128, 80], "float32"),
-    "so": ([128, 80], "uint16"), "cu": ([128, 80], "float32"), "cn": ([128, 80], "float32"),
+    "so": ([128, 80], "uint16"), "cn": ([128, 80], "float32"),
     "wd": ([128, 144], "bfloat16"), "wf": ([128, 144], "bfloat16"), "lm": ([128, 512], "bfloat16"),
     "bo": ([128, 128], "bfloat16"), "bt": ([128, 8], "bfloat16"), "ni": ([128, 128], "bfloat16"),
     "km": ([128, 144], "bfloat16"), "kp": ([128, 128], "bfloat16"),
     "nv": ([128, 128], "bfloat16"), "mv": ([128, 128], "float32"), "mi": ([128, 8], "int32"),
-    "pf": ([128, 8], "float32"), "pb": ([128, 8], "bfloat16"),
+    "pf": ([128, 16], "float32"), "pb": ([128, 8], "bfloat16"),
     "thi": ([128, 1], "int32"), "thn": ([128, 2], "float32"), "thf": ([128, 2], "float32"),
 }
 SCRATCH = {k: ("sbuf", s, d) for k, (s, d) in _S.items()}
 for _k, _w, _d in (("o0", 16, "uint16"), ("o1", 16, "uint16"), ("o2", 16, "uint16"), ("o3", 16, "uint16"),
-                   ("w", 64, "uint16"), ("r", 40, "uint16"), ("p", 160, "int32"), ("c", 10, "float32"),
+                   ("w", 64, "uint16"), ("v", 64, "int32"), ("r", 40, "uint16"), ("p", 160, "int32"), ("c", 10, "float32"),
                    *(("y%d" % h, 2 * (CUT[h + 1] - CUT[h]), "float32") for h in range(PIECES))):
     SCRATCH["st" + _k] = ("dram", [8, 128, _w], _d)
     SCRATCH["ld" + _k] = ("dram", [8, 128, _w], _d)
@@ -53,7 +54,7 @@ SCRATCH["ldt"] = ("dram", [8, 128, 1], "int32")
 SCRATCH["pp"] = ("psum", [128, 4096], "float32")
 PSUM = ("pp",)
 
-CLASSES = ("o0", "o1", "o2", "o3", "w", "r", "p", "t", "c") + tuple("y%d" % h for h in range(PIECES))
+CLASSES = ("o0", "o1", "o2", "o3", "w", "v", "r", "p", "t", "c") + tuple("y%d" % h for h in range(PIECES))
 TWO_CALLS = ("p",)
 SEMAPHORES = (["q_v", "q_a", "q_t", "q_g", "sent"] + ["arr_" + k for k in CLASSES] + ["stg_" + k for k in CLASSES]
               + ["own_" + k for k in CLASSES] + ["get_" + k for k in CLASSES]
@@ -199,12 +200,13 @@ def rank_program(g, core, T, topo):
         stage(qn, c, T[src], slice(a, b), [(src, a, b)])
         dma(qn, own + c, [(src, a, b)], [(to, a, b)], T[to][mine, a:b], T[src][mine, a:b])
 
-    def fetch(qn, c, to, cols, by_call=False):
+    def fetch(qn, c, to, cols, by_call=False, s=None):
         wr = [] if to in ("yx", "yc") else [(to, cols.start, cols.stop)]
         others = [o for o in cores if o != core]
         for part in ([[o for o in others if call_of(o, core, c) == k] for k in range(2)] if by_call else [others]):
             for a, b in runs([T.rank_of(o) for o in part]):
-                dma(qn, "get_" + c, [("ld" + c, a, b)], wr, T[to][16 * a:16 * b, cols], T["ld" + c][a:b])
+                dma(qn, s or "get_" + c, [("ld" + c, a, b)], wr,
+                    T[to][16 * a:16 * b] if to == "ci1" else T[to][16 * a:16 * b, cols], T["ld" + c][a:b])
 
     dma("s", "stg_t", [], [("stt", 0, 8)], T.stt[:], T.th[:])
     dma("a", "in_r", [], [("rh", 0, 320)], T.rh[:], T.ray[:])
@@ -214,7 +216,8 @@ def rank_program(g, core, T, topo):
     for m in range(2):
         dma("s", "in_d", [], [("ci0", 256, 512)], T.ci0[:, m, 128:256], T.cand[:, 256 * m + 128:256 * m + 256])
     dma("s", "own_t", [], [("ldt", q, q + 1)], T.ldt[q], T.th[:])
-    dma("s", "own_p", [], [("yi", 0, R)], T.yi[mine, :], T.px[mine, :])
+    dma("s", "own_p", [], [("xi", 3 * R, 4 * R)], T.xi[mine, 3 * R:4 * R], T.px[mine, :])
+    dma("s", "xc0", [], [("xn", XH, XH + R)], T.xn[mine, XH:XH + R], T.px[mine, :])
     dma("s", "in_w", [], [("cw", 0, 512)], T.cw[:], T.cand[:, 512:1024])
 
     def ap(b):
@@ -271,7 +274,7 @@ def rank_program(g, core, T, topo):
     def skip():
         pass
 
-    c16, k255, hcol, c3r = (("pf", k, k + 1) for k in range(4))
+    c16, k255, hcol, c3r, c5 = (("pf", k, k + 1) for k in range(5))
 
     def iota(out, pattern, base, view=None):
         view = ap(out) if view is None else view
@@ -281,53 +284,48 @@ def rank_program(g, core, T, topo):
         op("g", [in_], [out], lambda e: e.affine_select(T[out[0]][0:rows, out[1]:out[2]], T[in_[0]][0:rows, in_[1]:in_[2]],
                                                         pattern, how, 0.0, base, step))
 
-    def columns():
-        act(("pb", 0, 1), c16, scale=math.log(2.0), func=AF.Exp)
-        act(hcol, c16, scale=-1.0, bias=0.5, func=AF.Relu)
-        act(c3r, c16, bias=3.0 * R)
-        act(("wf", 0, 144), ("cio", 0, 144), scale=0.0, bias=("pb", 0, 1))
-
     def carving():
-        iota(("kp", 0, 128), [[0, 128]], 2048)
+        iota(("kp", 0, 128), [[0, 128]], 4096)
         for k in range(4):
             select(("lm", 128 * k, 128 * k + 128), ("kp" if k > 1 else "km", 0, 128), [[0, 8], [-1, 8], [1000, 2]],
                    -1000 * (k % 2), rows=8)
         iota(("pre", 15, 16), [[0, 1]], 0)
         iota(("c96", 0, 512), [[0, 512]], CAP)
-        select(("wf", 0, 144), ("wf", 0, 144), [[-16, 9], [-1000, 16]], 16, how=A.is_ge)
-        select(("wf", 0, 144), ("wf", 0, 144), [[16, 9], [0, 16]], -1, step=-1, how=A.is_ge)
 
     def strides():
-        for k in (0, 4):
-            iota(("u5", 0, 400), [[0, 80]], k // 4, T.u5[:, :, k])
-        iota(("hx0", 0, 400), [[0, 400]], -R)
-        for a, b in zip(CUT, CUT[1:]):
-            iota(("hx1", 5 * a, 5 * b), [[0, 5 * (b - a)]], 16 * (b - a))
+        for k in (0, 4, 5):
+            iota(("u6", 0, 480), [[0, 80]], k // 4, T.u6[:, :, k])
+        iota(("hx0", 0, 480), [[0, 480]], -R)
+        for k in (0, 5):
+            iota(("hv", k, 480, 6), [[0, 80]], 0)
+        iota(("hx1", 0, 480), [[0, 480]], 320)
+        iota(("t1", 0, 80), [[0, 4], [16, 20]], 0)
+        iota(("t2", 0, 80), [[-320, 4], [48, 20]], 0)
 
     def origins():
-        act(("hx0", 4, 400, 5), ("cio", 0, 80), scale=16.0, bias=c3r)
-        for a, b in zip(CUT, CUT[1:]):
-            act(("hx1", 5 * a + 4, 5 * b, 5), ("cio", 0, b - a), scale=16.0, bias=c16)
+        act(("hx0", 4, 480, 6), ("cio", 0, 80), scale=16.0, bias=c3r)
+        act(("hx1", 4, 480, 6), ("t1", 0, 80), bias=c16)
+        act(("hx0", 5, 480, 6), ("t2", 0, 80), bias=c5)
 
     op("g", [], [("mi", 0, 1)], lambda e: e.iota(T.mi[:, 0:1], [[0, 1]], 0, 1))
     iota(("cio", 0, 256), [[1, 256]], 0)
-    iota(("cio", 3328, V), [[1, 768]], 3328)
+    iota(("km", 0, 144), [[0, 144]], -4096)
+    iota(("cio", 3840, V), [[1, 256]], 3840)
     send("t", T.stt[:])
-    iota(("km", 0, 144), [[0, 144]], -2048)
-    select(("wd", 0, 144), ("km", 0, 144), [[-16, 9], [1000, 16]], 16)
     send("p")
+    select(("wd", 0, 144), ("km", 0, 144), [[-16, 9], [1000, 16]], 16)
     select(("ni", 0, 128), ("km", 0, 128), [[-1, 128]], 0)
     op("v", [], [("one", 0, 128)], lambda e: e.memset(T.one[:], 1.0))
     ts(("mi", 1, 2), ("mi", 0, 1), 15, None, A.bitwise_and)
     ts(("cio", 256, 512), ("cio", 0, 256), 256.0, None, A.add)
     act(("cio", 512, 768), ("cio", 0, 256), bias=512.0)
     copy(c16, ("mi", 1, 2))
-    for at in range(768, 3328, 512):
+    ts(k255, c16, -1.0, 255.0, A.mult, A.add)
+    for at in range(768, 3840, 512):
         if at < 2304:
             act(("cio", at, at + 512), ("cio", 0, 512), bias=float(at))
         else:
             ts(("cio", at, at + 512), ("cio", 0, 512), float(at), None, A.add)
-    ts(k255, c16, -1.0, 255.0, A.mult, A.add)
 
     def extract(out, w, base, extra):
         n = out[2] - out[1]
@@ -336,25 +334,24 @@ def rank_program(g, core, T, topo):
             tr + [(T[extra[0]][:], ap(extra[1]))])
 
     def prepare():
-        def powers():
-            copy(("bf", 0, 240), ("ub", 0, 240))
-            act(("pw", 0, 240), ("bf", 0, 240), scale=-math.log(2.0), func=AF.Exp)
-            act(("p2", 0, 240), ("bf", 0, 240), scale=math.log(2.0), bias=-12 * math.log(2.0), func=AF.Exp)
+        li, bf, big = ("li", 0, 240), ("bf", 0, 240), 1.5 * 2 ** 31
+        act(bf, li, bias=-127.5)
+        act(bf, bf, bias=big)
+        act(bf, bf, scale=-1.0, bias=big)
+        plus(1, li, bf)
+        act(("pw", 0, 240), bf, scale=math.log(2.0) / 256, func=AF.Exp)
+        act(("p2", 0, 240), bf, scale=-math.log(2.0) / 256, bias=-13 * math.log(2.0), func=AF.Exp)
 
-        return [lambda: ts(("ub", 0, 240), ("li", 0, 240), 8, None, A.arith_shift_right),
-                lambda: ts(("ua", 0, 240), ("li", 0, 240), 255, None, A.bitwise_and), powers,
-                lambda: copy(("uu", 0, 240), ("ua", 0, 240))]
+    def plus(k, x, y):
+        mms(("pp", 512 * k, 512 * k + 240), [("eye", 0, 128), x, y], [(T.eye[:], ap(x)), (T.eye[:], ap(y))])
 
     def slot(t, s, a, b):
         if t == 0:
-            return ("xs", R * (3 - s) + 16 * a, R * (3 - s) + 16 * b)
-        return ("xs", 64 * a + 16 * (b - a) * s, 64 * a + 16 * (b - a) * (s + 1))
-
-    def start(t):
-        return ("xn", 0) if t else ("xs", 3 * R)
+            return ("xi", R * (3 - s) + 16 * a, R * (3 - s) + 16 * b)
+        return ("xi", 64 * a + 16 * (b - a) * s, 64 * a + 16 * (b - a) * (s + 1))
 
     def rest(qn, lst, a, b):
-        gather(qn, ("wr", 16 * a, 16 * b), ("cio", 0, V), lst)
+        gather(qn, ("cio", V + 16 * a, V + 16 * b), ("cio", 0, V), lst)
 
     def offsets(to, src, *ps):
         for p in ps:
@@ -364,7 +361,7 @@ def rank_program(g, core, T, topo):
     def see(t, qn, p, *ks):
         for k in ks:
             c = 128 * p + 32 * k
-            gather(qn, ("wg", 16 * c, 16 * c + 512), ("wr", 0, R), ("wn" if t else "cu0", c, c + 32),
+            gather(qn, ("wg", 16 * c, 16 * c + 512), ("cio", V, V + R), ("wn" if t else "cu0", c, c + 32),
                    -(1024 * p + 512 * (k % 2) + 255.0))
 
     def seen(p):
@@ -373,32 +370,37 @@ def rank_program(g, core, T, topo):
     def lists(t, p):
         tm, ci = ("tm", 128 * p, 128 * p + 128), ("ci%d" % t, 128 * p, 128 * p + 128)
         return [lambda: op("v", [z(p, 0, 128), ci], [tm],
-                           lambda e: e.tensor_tensor(ap(tm), ap(z(p, 0, 128)),
-                                                     ap(ci) if t else T.ci0[:, :, 64 * p:64 * p + 64], A.max)),
+                           lambda e: e.tensor_tensor(ap(tm), ap(z(p, 0, 128)), T[ci[0]][:, :, 64 * p:64 * p + 64], A.max)),
                 lambda: ts(("off", tm[1], tm[2]), tm, float(R), None, A.min)]
 
     def ship(p, qn):
         hand(qn, "o%d" % p, "get_", "off", "of0", 128 * p, 128 * p + 128)
         send("o%d" % p)
 
-    def twin(t):
-        b, a = start(t)
-        dma("s", "xc%d" % t, [(b, a, a + R)], [("xh", 0, R)], T.xh[:, 0:R], T[b][:, a:a + R])
+    def start(t):
+        return ("xn", XB, XB + R) if t else slot(0, 0, 0, 80)
 
     def window(t, b):
-        return (start(t)[0], start(t)[1], start(t)[1] + XW) if b == "lo" else ("xh", 0, XW)
+        name, at = start(t)[:2] if b == "lo" else ("xn", XH)
+        return (name, at, at + R + 8)
 
     def first(t, b, *ps, es=(0, 2), qn="a"):
         for p in ps:
             gather(qn, (b, 1024 * p + 512 * es[0], 1024 * p + 512 * es[1]), window(t, b),
                    ("off" if t else "of0", 128 * p + 32 * es[0], 128 * p + 32 * es[1]))
 
-    def second(t, b, *ps, es=(0, 2)):
+    def second(t, b, *ps, move=True):
         for p in ps:
-            blk, to = (b, 1024 * p + 512 * es[0], 1024 * p + 512 * es[1]), "b" + b[0]
-            tt_gather(blk, window(t, b), ("off" if t else "of0", 128 * p + 64 + 32 * es[0], 128 * p + 64 + 32 * es[1]), blk,
+            blk = (b, 1024 * p, 1024 * p + 1024)
+            tt_gather(blk, window(t, b), ("off" if t else "of0", 128 * p + 64, 128 * p + 128), blk,
                       A.min if b == "lo" else A.max)
-            for a in range(8 if es[1] == 2 else 0):
+            if move:
+                abreast(t, b, p)
+
+    def abreast(t, b, *ps):
+        to = "b" + b[0]
+        for p in ps:
+            for a in range(8):
                 dma("s", "r%s%d" % (b[0], t), [(b, 1024 * p, 1024 * p + 1024)], [(to, 512 * a, 512 * a + 512)],
                     T[to][32 * p:32 * p + 32, 512 * a:512 * a + 512], T[b][grp(a), 1024 * p:1024 * p + 1024])
 
@@ -417,7 +419,7 @@ def rank_program(g, core, T, topo):
                 + [lambda: tt(s3, to[1], s1, o), lambda: tt(to[3], to[3], s2, o), lambda: tt(last, to[3], s3, o)])
 
     def spread(t):
-        act(("fb", 0, 512), ("lof", 0, 512), scale=-0.2, bias=-0.375)
+        act(("fb", 0, 512), ("lof", 0, 512), scale=-0.25, bias=-0.375)
         for a in range(8):
             for p in range(4):
                 dma("s", "fg%d" % t, [("fb", 0, 512)], [("et", 1024 * p, 1024 * p + 1024)],
@@ -438,25 +440,32 @@ def rank_program(g, core, T, topo):
         mms(z(2, 0, 256), [("lm", 0, 512), ("pre", 0, 528)],
             [(T.lm[0:8, 128 * k:128 * k + 128], T.pre[0:8, 16 - k // 2 + 256 * (k % 2):272 - k // 2 + 256 * (k % 2)])
              for k in range(4)])
-        act(("ft", 0, 256), z(2, 0, 256), scale=-2.0 ** -11, bias=hcol)
+        act(("ft", 0, 256), z(2, 0, 256), scale=-2.0 ** -12, bias=hcol)
 
     def middle(t, spare):
-        spare = list(spare) + [skip] * 6
+        spare = list(spare) + [skip] * 7
         lift("bl", 0, 1, 2, 3)
+        if t == 0:
+            places()
+        else:
+            act(("x5", 0, R), start(1), scale=1.25)
         weave(fold("bl", A.min, ("lof", 0, 512)), [skip] * 5 + spare[:2])
+        if t == 0:
+            plus(2, ("rf", 80, 320), ("rn", 0, 240))
         lift("bh", 0, 1)
         spread(t)
         lift("bh", 2, 3)
         act(("lt", 0, 512), ("lof", 0, 512), bias=("thf", 0, 1))
+        prepare()
         if t == 0:
-            origins()
-        weave(fold("bh", A.max, ("pp", 0, 512)) + [count, odd, running], [skip] * 5 + spare[2:6])
+            moves()
+        weave(fold("bh", A.max, ("pp", 0, 512)) + [count, odd, running],
+              [skip] * 5 + spare[2:4] + [lambda: copy(("uu", 0, 240), ("pp", 512, 752))] + spare[4:6])
 
     def step(t, s, a, b):
-        y, x = ("yi", 16 * a, 16 * b), slot(t, s, a, b) if s or not t else ("xn", 16 * a, 16 * b)
-        at = 80 * s + (0 if t else 512)
+        y, x, at = slot(t, s + 1, a, b), ("x5", 16 * a, 16 * b), 80 * s + (0 if t else 512)
         return [lambda: tt_gather(y, ("et", 0, V), ("lq1" if t else "wn", at + a, at + b), x, A.add),
-                lambda: ts(slot(t, s + 1, a, b), y, 1.25, 1.25 * TOP, A.mult, A.min)]
+                lambda qn="v": ts(x, y, 1.25, None, A.mult) if qn == "v" else act(x, y, scale=1.25)][:2 - s // 2]
 
     def flags(word, *parts):
         for qn, a, b in parts:
@@ -465,139 +474,168 @@ def rank_program(g, core, T, topo):
         extract(word, "wf", 48 * a, ("ni", ("p2", 3 * a, 3 * b)))
 
     def tests(word, a, b):
-        five = (5 * a, 5 * b)
-        return [lambda: op("v", [word, ("pw", 3 * a, 3 * b)], [("u5", *five)],
-                           lambda e: e.tensor_tensor(T.u5[:, a:b, 1:4], ap(word), T.pw[:, 3 * a:3 * b], A.mult)),
-                lambda: op("v", [("u5", *five)], [("e5", *five)],
-                           lambda e: e.tensor_scalar(ap(("e5", *five)), T.u5[:, a:b, :], 1, None, A.bitwise_and)),
-                lambda: copy(("he", *five), ("e5", *five))]
+        six = (6 * a, 6 * b)
+        return [lambda: op("v", [word, ("pw", 3 * a, 3 * b)], [("u6", *six)],
+                           lambda e: e.tensor_tensor(T.u6[:, a:b, 1:4], ap(word), T.pw[:, 3 * a:3 * b], A.mult)),
+                lambda: op("v", [("u6", *six)], [("e6", *six)],
+                           lambda e: e.tensor_scalar(ap(("e6", *six)), T.u6[:, a:b, :], 1, None, A.bitwise_and))]
 
     def horner(to, lst, d0, a, b):
-        return [lambda: scan((to, 5 * a, 5 * b), (d0, 5 * a, 5 * b), ("he", 5 * a, 5 * b)),
-                lambda: copy((lst, a, b), (to, 5 * a + 4, 5 * b, 5))]
+        return [lambda: scan((to, 6 * a, 6 * b), (d0, 6 * a, 6 * b), ("e6", 6 * a, 6 * b)),
+                lambda: copy((lst, a, b), (to, 6 * a + 4, 6 * b, 6))]
 
-    def pick(t, qn, a, b, win):
-        out, scale = ("wr" if t else "xn", 16 * a, 16 * b), 0.8 if t else 1.0
-        if qn == "a":
-            op("a", [win, ("so", a, b)], [out],
-               lambda e: e.activation(ap(out), ap(win).indirect(T.so[:, a:b]), AF.Relu, bias=0.0, scale=scale))
-        else:
-            op("v", [win, ("so", a, b)], [out],
-               lambda e: e.tensor_scalar(ap(out), ap(win).indirect(T.so[:, a:b]), scale, 0.0, A.mult, A.max))
+    def pick(t, a, b, qn="v"):
+        out, win = (("cio", V + 16 * a, V + 16 * b), ("xi", 64 * a, 64 * b)) if t else (start(1), ("xi", 0, 4 * R))
+        if qn == "v":
+            return op("v", [win, ("so", a, b)], [out],
+                      lambda e: e.tensor_scalar(ap(out), ap(win).indirect(T.so[:, a:b]), 0.0, float(TOP), A.max, A.min))
+        op("a", [win, ("so", a, b)], [out],
+           lambda e: e.activation(ap(out), ap(win).indirect(T.so[:, a:b]), AF.Relu, bias=float(TOP), scale=-1.0))
+        act(out, out, scale=-1.0, bias=float(TOP), func=AF.Relu)
 
-    copy(("wq", 512, 832), ("rh", 0, 320))
-    hand("s", "r", "own_", "wq", "wn", 512, 832)
-    send("r")
-    for b, at, c in (("xs", 3 * R, D), ("xh", 0, -1), ("xn", 0, D)):
-        iota((b, at + R, at + XW), [[0, XW - R]], int(c))
+    copy(("wq", 512, 592), ("rh", 0, 80))
+    for b, at, c in (("xi", 4 * R, D), ("xn", XH + R, -1), ("xn", XB + R, D)):
+        iota((b, at, at + 8), [[0, 8]], c)
     select(("mv", 0, 128), ("one", 0, 128), [[-32, 4], [-1, 16], [-16, 2]], 0)
+    select(("eye", 0, 128), ("one", 0, 128), [[-1, 128]], 0)
     select(("bo", 0, 128), ("km", 0, 128), [[-2, 4], [0, 16], [-1, 2]], 0, rows=8)
+    for k in range(4):
+        act(("nv", 32 * k, 32 * k + 32), ("cio", 0, 32), scale=-16.0, bias=k255)
     offsets("cu0", "ci0", 0)
     rest("a", ("wq", 512, 552), 0, 40)
     rest("v", ("wq", 552, 592), 40, 80)
     offsets("cu0", "ci0", 1)
-    for k in range(4):
-        act(("nv", 32 * k, 32 * k + 32), ("cio", 0, 32), scale=-16.0, bias=k255)
-    see(0, "a", 0, 0)
-    see(0, "v", 0, 1, 2, 3)
+    see(0, "a", 0, 0, 1)
+    see(0, "v", 0, 2, 3)
     seen(0)
-    see(0, "a", 1, 0, 1, 2)
     offsets("cu0", "ci0", 2, 3)
-    see(0, "v", 1, 3)
+    see(0, "a", 1, 0, 1)
+    see(0, "v", 1, 2, 3)
     seen(1)
-    see(0, "a", 2, 0, 1)
-    see(0, "v", 2, 3)
-    weave(lists(0, 0), [lambda: see(0, "v", 2, 2)])
+    weave(lists(0, 0), [lambda: copy(("wq", 592, 832), ("rh", 80, 320))])
     ship(0, "s")
+    fetch("s", "p", "xi", slice(3 * R, 4 * R), True)
+    fetch("s", "p", "xn", slice(XH, XH + R), s="xc0")
+    see(0, "a", 2, 0, 1, 2)
+    see(0, "v", 2, 3)
     seen(2)
-    weave(lists(0, 1), [lambda: see(0, "v", 3, 2), lambda: see(0, "v", 3, 3)])
+    see(0, "v", 3, 2)
+    weave(lists(0, 1))
     ship(1, "s")
     see(0, "a", 3, 0, 1)
+    see(0, "v", 3, 3)
     seen(3)
     ops("t", [("bo", 0, 128), ("ni", 0, 128)], [("pp", 0, 8)],
         [lambda e: e.matmul(T.pp[:, 0:8], T.bo[0:8, :], T.ni[0:8, 0:8], True, True)])
-    fetch("s", "p", "yi", slice(0, R), True)
-    columns()
-    weave(lists(0, 2), [lambda: offsets("wq", "cw", 0), lambda: offsets("wq", "cw", 1, 2)])
+    weave(lists(0, 2))
     ship(2, "a")
-    dma("a", "get_t", [("ldt", 0, 8)], [("thi", 0, 1)], T.thi[:], T.ldt[:, mine, :])
-    fetch("a", "r", "wn", slice(512, 832))
-    weave(lists(0, 3), [lambda: offsets("wq", "cw", 3)])
-    ship(3, "a")
-    hand("a", "w", "own_", "wq", "wn", 0, 512)
     fetch("s", "o0", "of0", slice(0, 128))
-    act(("bt", 0, 8), ("pp", 0, 8), scale=2.0 ** -22)
-    ts(slot(0, 0, 0, 80), ("yi", 0, R), 1.25, None, A.mult)
-    ts(("thn", 0, 1), ("thi", 0, 1), 1.25, None, A.mult)
-    ts(("thn", 1, 2), ("thi", 0, 1), 1.25, None, A.mult)
-    mms(z(3, 0, 2), [("mv", 0, 128), ("thn", 0, 2)], [(T.mv[:], T.thn[:])])
-    l0, l1, l2 = (("li", 2 - s, 240, 3) for s in range(3))
-    d0, d1, d2 = (("hv", 3 - s, 400, 5) for s in range(3))
-    for s, to in enumerate((l0, l1, l2, ("hv", 0, 400, 5))):
-        copy(to, ("wn", 512 + 80 * s, 592 + 80 * s))
-    copy(("hv", 4, 400, 5), ("wn", 512, 592))
+    weave(lists(0, 3))
+    ship(3, "s")
+    fetch("s", "o1", "of0", slice(128, 256))
+    dma("s", "get_t", [("ldt", 0, 8)], [("thi", 0, 1)], T.thi[:], T.ldt[:, mine, :])
+    hand("s", "r", "own_", "wq", "wn", 512, 832)
+    send("r")
     carving()
     strides()
-    for p in range(1, 4):
-        fetch("s", "o%d" % p, "of0", slice(128 * p, 128 * p + 128))
-    twin(0)
-    for es in ((0, 1), (1, 2)):
-        first(0, "lo", 0, es=es)
-        second(0, "lo", 0, es=es)
-    first(0, "lo", 1, 2, 3)
-    second(0, "lo", 1, 2, 3)
-    first(0, "hi", 0, 1, 2, 3)
-    second(0, "hi", 0, 1, 2, 3)
-    act(("thf", 0, 2), z(3, 0, 2))
-    ready = prepare()
-    middle(0, ready + [lambda: (tt(d0, l1, l0, A.subtract), tt(d1, l2, l1, A.subtract)),
-                       lambda: tt(d2, ("hv", 0, 400, 5), l2, A.subtract)])
-    need("g", "fg0", None)
-    send("w")
-    fetch("s", "w", "wn", slice(0, 512))
+    fetch("s", "o2", "of0", slice(256, 384))
+    first(0, "lo", 0, es=(0, 1))
+    first(0, "lo", 0, es=(1, 2), qn="v")
+    first(0, "hi", 0)
+    first(0, "lo", 1, 2)
+    second(0, "lo", 0)
+    fetch("s", "o3", "of0", slice(384, 512))
+    first(0, "hi", 1)
+    first(0, "lo", 3)
+    first(0, "hi", 2, 3)
+    second(0, "hi", 0)
+    second(0, "lo", 1, 2)
+    fetch("s", "r", "wn", slice(512, 832))
+    second(0, "hi", 1, move=False)
+    second(0, "lo", 3)
+    abreast(0, "hi", 1)
+    second(0, "hi", 2, 3)
+    copy(("rf", 0, 320), ("wn", 512, 832))
+    act(("bt", 0, 8), ("pp", 0, 8), scale=2.0 ** -24)
+    for k in range(2):
+        act(("thn", k, k + 1), ("thi", 0, 1))
+    mms(z(3, 0, 2), [("mv", 0, 128), ("thn", 0, 2)], [(T.mv[:], T.thn[:])])
+    act(("x5", 0, R), start(0), scale=1.25)
+    l0, l1, l2 = (("li", 2 - s, 240, 3) for s in range(3))
+    d0, d1, d2 = (("hv", 3 - s, 480, 6) for s in range(3))
+
+    def places():
+        act(("thf", 0, 2), z(3, 0, 2))
+        act(l0, ("rf", 0, 80))
+        act(("rn", 0, 240), ("rf", 0, 240), scale=-1.0)
+        act(l1, ("rf", 80, 160))
+        act(("hv", 4, 480, 6), ("rf", 0, 80))
+        act(l2, ("rf", 160, 240))
+        act(hcol, c16, scale=-1.0, bias=0.5, func=AF.Relu)
+        act(c3r, c16, bias=3.0 * R)
+        act(c5, c16, scale=3.0, bias=-3.0 * R)
+
+    def moves():
+        act(("pb", 0, 1), c16, scale=math.log(2.0), func=AF.Exp)
+        act(d0, ("pp", 1024, 1104))
+        act(("wf", 0, 144), ("cio", 0, 144), scale=0.0, bias=("pb", 0, 1))
+        select(("wf", 0, 144), ("wf", 0, 144), [[-16, 9], [-1000, 16]], 16, how=A.is_ge)
+        select(("wf", 0, 144), ("wf", 0, 144), [[16, 9], [0, 16]], -1, step=-1, how=A.is_ge)
+        act(d1, ("pp", 1104, 1184))
+        act(d2, ("pp", 1184, 1264))
 
     halves = ((0, 40), (40, 80))
     steps0 = [[step(0, s, a, b) for a, b in halves] for s in range(3)]
-    flags(z(0, 0, 120), ("a", 0, 20), ("v", 20, 40))
-    flags(z(1, 0, 120), ("a", 40, 80))
-    steps0[0][0][0]()
-    steps0[0][1][0]()
-    weave(tests(z(0, 0, 120), 0, 40) + horner("hs", "lq1", "hv", 0, 40),
-          [steps0[0][0][1], skip, steps0[0][1][1]])
-    rest("a", ("lq1", 0, 40), 0, 40)
-    weave(tests(z(1, 0, 120), 40, 80) + horner("hs", "lq1", "hv", 40, 80),
-          [skip, lambda: copy(("ci1", 0, 256), ("wn", 0, 256)), skip, lambda: copy(("ci1", 256, 512), ("wn", 256, 512))])
-    rest("a", ("lq1", 40, 80), 40, 80)
+    middle(0, [skip, lambda: offsets("wq", "cw", 0), skip, skip, skip, lambda: offsets("wq", "cw", 1, 2, 3)])
+    hand("s", "w", "own_", "wq", "wn", 0, 512)
+    stage("s", "v", T.cand, slice(512, 1024))
+    dma("s", "own_v", [], [("ci1", 0, 512)], T.ci1[mine], T.cand[mine, 512:1024])
+    send("w")
+    send("v")
+    fetch("s", "w", "wn", slice(0, 512))
+    fetch("s", "v", "ci1", slice(0, 512))
 
-    weave(*steps0[1])
-    see(1, "a", 0, 0, 1, 2, 3)
-    seen(0)
-    see(1, "a", 1, 0, 1, 2, 3)
-    seen(1)
-    weave(*steps0[2], horner("hc", "so", "hx0", 0, 80))
-    see(1, "a", 2, 0, 1, 2, 3)
-    weave(lists(1, 0), [lambda: pick(0, "v", 0, 40, ("xs", 0, 4 * R)), lambda: pick(0, "v", 40, 80, ("xs", 0, 4 * R))])
-    twin(1)
+    flags(z(0, 0, 120), ("a", 0, 20), ("v", 20, 40))
+    flags(z(1, 0, 120), ("a", 40, 72), ("v", 72, 80))
+    origins()
+    steps0[0][0][0]()
+    weave(tests(z(0, 0, 120), 0, 40) + horner("hs", "lq1", "hv", 0, 40), [skip, skip, steps0[0][0][1]])
+    rest("a", ("lq1", 0, 40), 0, 40)
+    weave(tests(z(1, 0, 120), 40, 80) + horner("hs", "lq1", "hv", 40, 80))
+    rest("a", ("lq1", 40, 60), 40, 60)
+    rest("v", ("lq1", 60, 80), 60, 80)
+
+    for p in range(3):
+        see(1, "a", p, 0, 1, 2, 3)
+        seen(p)
+    weave(steps0[0][1], steps0[1][0][:1])
+    weave(horner("hc", "so", "hx0", 0, 80), steps0[1][1], steps0[1][0][1:])
+    weave(*steps0[2], lists(1, 0)[:1])
+    weave(lists(1, 0)[1:], [lambda: pick(0, 0, 80)])
+    dma("s", "xc1", [start(1)], [("xn", XH, XH + R)], T.xn[:, XH:XH + R], ap(start(1)))
     for a, b in zip(CUT, CUT[1:]):
-        dma("s", "xq", [("xn", 0, R)], [slot(1, 0, a, b)], ap(slot(1, 0, a, b)), T.xn[:, 16 * a:16 * b])
-    seen(2)
-    see(1, "a", 3, 0, 1, 2, 3)
+        dma("s", "xq", [start(1)], [slot(1, 0, a, b)], ap(slot(1, 0, a, b)), T.xn[:, XB + 16 * a:XB + 16 * b])
+    see(1, "a", 3, 0, 1, 2)
+    weave(lists(1, 1), [lambda: see(1, "v", 3, 3), lambda: first(1, "lo", 0, qn="v")])
     seen(3)
-    weave(lists(1, 1), [lambda: first(1, "lo", 0, qn="v"), lambda: second(1, "lo", 0)])
     first(1, "lo", 1)
-    weave(lists(1, 2), [lambda: first(1, "hi", 0, qn="v"), lambda: second(1, "hi", 0)])
+    weave(lists(1, 2), [lambda: second(1, "lo", 0)])
     first(1, "lo", 2)
+    first(1, "hi", 0)
     weave(lists(1, 3), [lambda: second(1, "lo", 1)])
     first(1, "lo", 3)
     first(1, "hi", 1, 2, 3)
-    second(1, "lo", 2, 3)
+    second(1, "lo", 2)
+    second(1, "hi", 0)
+    second(1, "lo", 3)
     second(1, "hi", 1, 2, 3)
-    e0, e1, t1, t2 = ("he", 3, 400, 5), ("he", 2, 400, 5), ("t1", 0, 80), ("t2", 0, 80)
-    ready = prepare()
-    middle(1, [lambda: (tt(t1, e1, d2, A.mult), tt(t2, e0, d2, A.mult), copy(l0, ("hs", 4, 400, 5))),
-               lambda: (tt(t1, t1, d1, A.add), tt(l2, l2, t2, A.add), tt(t1, t1, e0, A.mult),
-                        copy(("lq1", 160, 240), l2), tt(l1, l1, t1, A.add)),
-               ready[0], ready[1], lambda: (ready[2](), ready[3]()), lambda: copy(("lq1", 80, 160), l1)])
+    act(l0, ("hs", 4, 480, 6))
+    act(("hx1", 5, 480, 6), ("hc", 5, 480, 6), scale=-0.25)
+    e0, e1, t1, t2 = ("e6", 3, 480, 6), ("e6", 2, 480, 6), ("t1", 0, 80), ("t2", 0, 80)
+    weave([lambda: tt(t1, e1, d2, A.mult), lambda: tt(t1, t1, d1, A.add)],
+          [lambda: tt(t2, e0, d2, A.mult), lambda: tt(l2, l2, t2, A.add)])
+    later = [lambda: tt(t1, t1, e0, A.mult), lambda: tt(l1, l1, t1, A.add), skip, skip,
+             lambda: (copy(("lq1", 160, 240), l2), copy(("lq1", 80, 160), l1))]
 
     def word(h):
         return z(h, 0, 3 * (CUT[h + 1] - CUT[h]))
@@ -611,31 +649,34 @@ def rank_program(g, core, T, topo):
     def steps(s, h):
         return step(1, s, CUT[h], CUT[h + 1])
 
-    def leave(h, qn="a"):
+    def leave(h, qn="v"):
         a, b, c = CUT[h], CUT[h + 1], "y%d" % h
-        pick(1, qn, a, b, ("xs", 64 * a, 64 * b))
-        stage("s", c, T.wr, slice(16 * a, 16 * b), [("wr", 16 * a, 16 * b)])
+        pick(1, a, b, qn)
+        stage("s", c, T.cio, slice(V + 16 * a, V + 16 * b), [("cio", V + 16 * a, V + 16 * b)])
         send(c)
 
-    size = 16.0 * (CUT[1] - CUT[0])
-    for h in range(3):
-        last_flags(h)
-    weave(steps(0, 0) + steps(1, 0) + steps(2, 0), steps(0, 1) + steps(1, 1))
-    weave(settle(0), steps(2, 1) + steps(0, 2))
+    middle(1, later)
+    last_flags(0)
+    last_flags(1)
+    flags(z(2, 0, 120), ("a", 40, 80))
+    G = [[steps(s, h)[0] for h in range(PIECES)] for s in range(3)]
+    M = [[steps(s, h)[1] for h in range(PIECES)] for s in range(2)]
+    weave([G[0][0], M[0][0], G[1][0], M[1][0], G[2][0]], [G[0][1], M[0][1], G[1][1], M[1][1]])
+    weave(settle(0), [G[2][1], G[0][2], G[0][3], M[0][2]])
     leave(0)
-    last_flags(3)
-    weave(settle(1), steps(1, 2) + steps(2, 2))
-    leave(1)
-    weave(settle(2), steps(0, 3) + steps(1, 3) + [lambda: ts(t1, ("hc", 3, 400, 5), -size / R, None, A.mult)])
+    weave(settle(1), [M[0][3], G[1][2], G[1][3]])
+    M[1][2]("a")
+    M[1][3]("a")
+    leave(1, "a")
+    weave(tests(z(2, 0, 120), 40, 80) + horner("hs", "so", "hx1", 40, 80), [skip, G[2][2], G[2][3]])
+    act(("cn", 0, 80), ("hs", 5, 480, 6), scale=-1 / 320, bias=3.0, func=AF.Relu)
+    act(("cn", 0, 80), ("cn", 0, 80), scale=-1.0, bias=3.0)
+    dma("a", "stg_c", [("cn", 0, 80)], [("stc", 0, 8)], T.stc[:], T.cn[:])
     leave(2)
-    weave(settle(3)[:4] + [lambda: tt(t1, t1, ("hs", 3, 400, 5), A.add),
-                           lambda: ts(("cn", 0, 80), t1, 3 * size, 1 / size, A.min, A.mult)],
-          steps(2, 3) + [skip, skip] + settle(3)[4:])
-    dma("s", "stg_c", [("cn", 0, 80)], [("stc", 0, 8)], T.stc[:], T.cn[:])
-    send("c")
     leave(3)
+    send("c")
 
-    dma("s", "own_y0", [("wr", 0, R)], [], T.yx[mine, :], T.wr[mine, :])
+    dma("s", "own_y0", [("cio", V, V + R)], [], T.yx[mine, :], T.cio[mine, V:V + R])
     dma("a", "own_c", [("cn", 0, 80)], [], T.yc[mine, :], T.cn[mine, :])
     for h in range(PIECES):
         fetch("s", "y%d" % h, "yx", slice(16 * CUT[h], 16 * CUT[h + 1]))

import math
from concourse.bass import DstId, RemoteDMATransfer
from concourse.mybir import AluOpType, ActivationFunctionType

A = AluOpType
AF = ActivationFunctionType
V, R, RO, H, CAP, NEED = 4096, 1280, 2, 3, 96, 9
TOP = 2 ** 20 - 1
D = 2 ** 21
XB, XH = 0, R + 8
CUT = (0, 20, 40, 60, 80)
PIECES = len(CUT) - 1

_S = {
    "et": ([128, V], "float32"),
    "cio": ([128, V + R], "float32"),
    "wg": ([128, 4 * 2048], "bfloat16"),
    "lo": ([128, V], "float32"), "hi": ([128, V], "float32"),
    "bl": ([128, V], "float32"), "bh": ([128, V], "float32"),
    "xn": ([128, 2 * R + 16], "int32"),
    "xi": ([128, 4 * R + 8], "int32"), "x5": ([128, R], "float32"),
    "s1": ([128, 1536], "float32"), "fb": ([128, 512], "float32"),
    "ft": ([128, 256], "bfloat16"),
    "u6": ([128, 80, 6], "int32"), "e6": ([128, 480], "int32"), "he": ([128, 480], "float32"),
    "hv": ([128, 480], "float32"), "hx0": ([128, 480], "float32"), "hx1": ([128, 480], "float32"),
    "hs": ([128, 480], "float32"), "hc": ([128, 480], "float32"),
    "lof": ([128, 512], "float32"), "lt": ([128, 512], "float32"), "odd": ([128, 512], "bfloat16"),
    "pre": ([128, 528], "bfloat16"), "c96": ([128, 512], "bfloat16"), "far": ([128, 512], "bfloat16"),
    "ci0": ([128, 2, 256], "int32"), "cw": ([128, 2, 256], "int32"), "ci1": ([128, 2, 256], "int32"),
    "cu0": ([128, 512], "uint16"), "tm": ([128, 512], "float32"),
    "wq": ([128, 832], "uint16"), "wn": ([128, 832], "uint16"),
    "off": ([128, 512], "uint16"), "of0": ([128, 512], "uint16"),
    "rh": ([128, 320], "int32"), "one": ([128, 128], "float32"),
    "li": ([128, 240], "float32"), "lq1": ([128, 240], "uint16"), "uu": ([128, 240], "uint16"),
    "rf": ([128, 320], "float32"), "rn": ([128, 240], "float32"), "eye": ([128, 128], "float32"),
    "bf": ([128, 240], "float32"), "pw": ([128, 240], "bfloat16"), "p2": ([128, 240], "bfloat16"),
    "t1": ([128, 80], "float32"), "t2": ([128, 80], "float32"),
    "so": ([128, 80], "uint16"), "cn": ([128, 80], "float32"),
    "wd": ([128, 144], "bfloat16"), "wf": ([128, 144], "bfloat16"), "lm": ([128, 512], "bfloat16"),
    "bo": ([128, 128], "bfloat16"), "bt": ([128, 8], "bfloat16"), "ni": ([128, 128], "bfloat16"),
    "km": ([128, 144], "bfloat16"), "kp": ([128, 128], "bfloat16"),
    "nv": ([128, 128], "bfloat16"), "mv": ([128, 128], "float32"), "mi": ([128, 8], "int32"),
    "pf": ([128, 16], "float32"), "pb": ([128, 8], "bfloat16"),
    "thi": ([128, 1], "int32"), "thn": ([128, 2], "float32"), "thf": ([128, 2], "float32"),
}
SCRATCH = {k: ("sbuf", s, d) for k, (s, d) in _S.items()}
for _k, _w, _d in (("o0", 16, "uint16"), ("o1", 16, "uint16"), ("o2", 16, "uint16"), ("o3", 16, "uint16"),
                   ("w", 64, "uint16"), ("v", 64, "int32"), ("r", 40, "uint16"), ("p", 160, "int32"), ("c", 10, "float32"),
                   *(("y%d" % h, 2 * (CUT[h + 1] - CUT[h]), "float32") for h in range(PIECES))):
    SCRATCH["st" + _k] = ("dram", [8, 128, _w], _d)
    SCRATCH["ld" + _k] = ("dram", [8, 128, _w], _d)
SCRATCH["stt"] = ("dram", [128, 1], "int32")
SCRATCH["ldt"] = ("dram", [8, 128, 1], "int32")
SCRATCH["pp"] = ("psum", [128, 4096], "float32")
PSUM = ("pp",)

CLASSES = ("o0", "o1", "o2", "o3", "w", "v", "r", "p", "t", "c") + tuple("y%d" % h for h in range(PIECES))
TWO_CALLS = ("p",)
SEMAPHORES = (["q_v", "q_a", "q_t", "q_g", "sent"] + ["arr_" + k for k in CLASSES] + ["stg_" + k for k in CLASSES]
              + ["own_" + k for k in CLASSES] + ["get_" + k for k in CLASSES]
              + ["rl0", "rl1", "rh0", "rh1", "fg0", "fg1", "xc0", "xc1", "xq", "in_r", "in_c", "in_d", "in_w"]
              + [k + c + "2" for k in ("arr_", "stg_") for c in TWO_CALLS])


def plan(core, cores, topo, two):
    r = cores.index(core)
    order = [cores[(r + k) % len(cores)] for k in range(1, len(cores))]
    near = [d for d in order if d in topo.cores_of(core)]
    mate = [d for d in order if topo.mates(core, d)]
    plane = [d for d in order if topo.same_plane(core, d)]
    both = [d for d in order if d not in near + mate + plane]
    far = both + [mate[0], plane[0], mate[1], plane[1]]
    fe = topo.engines(core, far[0])
    ne = [e for e in topo.engines(core, near[0]) if e not in fe][:4]
    if two:
        first = [(d, fe[2 * k:2 * k + 2]) for k, d in enumerate(far[:4])]
        second = [(d, fe[4 * k:4 * k + 4]) for k, d in enumerate(far[4:])]
        return [first, second + [(near[0], ne)]]
    return [[(d, fe[4 * k:4 * k + 4:2]) for k, d in enumerate(both)]
            + [(d, fe[2 * k + 1:2 * k + 2]) for k, d in enumerate(far[2:])] + [(near[0], ne)]]


def rank_program(g, core, T, topo):
    q = T.rank_of(core)
    if q is None:
        return
    cores = list(T.cores)
    sem = T.sem
    queues = {"v": g.vector, "a": g.scalar, "t": g.tensor, "s": g.sync, "g": g}
    csem = {"v": "q_v", "a": "q_a", "t": "q_t", "g": "q_g"}
    total = {}
    known = {}
    closed = {}
    hist = {}

    def need(qn, s, val):
        if val is None:
            val = total[s]
            closed[s] = True
        if known.get((qn, s), 0) < val:
            queues[qn].wait_ge(sem[s], val)
            known[(qn, s)] = val

    def depend(qn, acc, own):
        wants = {}
        for name, lo, hi, w in acc:
            ps = name in PSUM
            if ps:
                lo, hi = lo // 512 * 512, -(-hi // 512) * 512
            for (l2, h2, w2, q2, s2, v2) in hist.get(name, []):
                if l2 >= hi or h2 <= lo or s2 == own:
                    continue
                if not (w or w2 or (ps and q2 != qn)):
                    continue
                v = total[s2] if v2 is None else v2
                if v2 is None:
                    closed[s2] = True
                wants[s2] = max(wants.get(s2, 0), v)
        for s in wants:
            need(qn, s, wants[s])

    def record(qn, acc, s, val):
        for name, lo, hi, w in acc:
            if name in PSUM:
                lo, hi = lo // 512 * 512, -(-hi // 512) * 512
            h = hist.setdefault(name, [])
            if w:
                h[:] = [e for e in h if not (e[0] >= lo and e[1] <= hi and not (e[4] == s and e[5] is None))]
            h.append((lo, hi, w, qn, s, val))

    def accs(rd, wr):
        return [(*b[:3], False) for b in rd] + [(*b[:3], True) for b in wr]

    def ops(qn, rd, wr, fns):
        s = csem[qn]
        acc = accs(rd, wr)
        depend(qn, acc, None)
        for f in fns[:-1]:
            f(queues[qn])
        fns[-1](queues[qn]).then_inc(sem[s], 1)
        total[s] = total.get(s, 0) + 1
        record(qn, acc, s, total[s])

    def op(qn, rd, wr, fn):
        ops(qn, rd, wr, [fn])

    def dma(qn, s, rd, wr, out, in_):
        assert s not in closed, s
        acc = accs(rd, wr)
        depend(qn, acc, s)
        queues[qn].dma_start(out=out, in_=in_).then_inc(sem[s], 16)
        total[s] = total.get(s, 0) + 16
        record(qn, acc, s, None)

    def call_of(src, dst, c):
        return [k for k, call in enumerate(plan(src, cores, topo, c in TWO_CALLS)) if dst in [d for d, eng in call]][0]

    def send(c, piece=None):
        for k, call in enumerate(plan(core, cores, topo, c in TWO_CALLS)):
            if "stg_" + c + "2" * k in total:
                need("g", "stg_" + c + "2" * k, None)
            tr = []
            for d, eng in call:
                rid, pid = topo.addr(d, core)
                m = sum(1 << e for e in eng)
                assert m & topo.mask(core, d) == m
                tr.append(RemoteDMATransfer(dst_ids=[DstId(rid=rid, pnc=pid)], dma_engine_mask=m,
                                            remote_sem=sem["arr_" + c + "2" * k],
                                            srcs=[piece or T["st" + c][T.rank_of(d)]], dsts=[T["ld" + c][q]]))
                total["sent"] = total.get("sent", 0) + len(eng)
            g.remote_dma_fused(tr, local_sem=sem.sent)
        for k in range(1 + (c in TWO_CALLS)):
            senders = [o for o in cores if o != core and call_of(o, core, c) == k]
            n = sum(len(eng) for o in senders for d, eng in plan(o, cores, topo, c in TWO_CALLS)[k] if d == core)
            total["arr_" + c + "2" * k] = n
            record("far", [("ld" + c, T.rank_of(o), T.rank_of(o) + 1, True) for o in senders], "arr_" + c + "2" * k, n)

    def grp(a):
        return slice(16 * a, 16 * a + 16)

    mine = grp(q)

    def runs(ranks):
        out = []
        for a in sorted(ranks):
            if out and out[-1][1] == a:
                out[-1][1] = a + 1
            else:
                out.append([a, a + 1])
        return out

    def stage(qn, c, src, cols, rd=(), by_call=False):
        if not by_call:
            return dma(qn, "stg_" + c, list(rd), [("st" + c, 0, 8)], T["st" + c][:], src[:, cols])
        for k, call in enumerate(plan(core, cores, topo, True)):
            for a, b in runs([T.rank_of(d) for d, eng in call]):
                dma(qn, "stg_" + c + "2" * k, list(rd), [("st" + c, a, b)], T["st" + c][a:b], src[16 * a:16 * b, cols])

    def hand(qn, c, own, src, to, a, b):
        stage(qn, c, T[src], slice(a, b), [(src, a, b)])
        dma(qn, own + c, [(src, a, b)], [(to, a, b)], T[to][mine, a:b], T[src][mine, a:b])

    def fetch(qn, c, to, cols, by_call=False, s=None):
        wr = [] if to in ("yx", "yc") else [(to, cols.start, cols.stop)]
        others = [o for o in cores if o != core]
        for part in ([[o for o in others if call_of(o, core, c) == k] for k in range(2)] if by_call else [others]):
            for a, b in runs([T.rank_of(o) for o in part]):
                dma(qn, s or "get_" + c, [("ld" + c, a, b)], wr,
                    T[to][16 * a:16 * b] if to == "ci1" else T[to][16 * a:16 * b, cols], T["ld" + c][a:b])

    dma("s", "stg_t", [], [("stt", 0, 8)], T.stt[:], T.th[:])
    dma("a", "in_r", [], [("rh", 0, 320)], T.rh[:], T.ray[:])
    stage("s", "p", T.px, slice(0, R), by_call=True)
    for m in range(2):
        dma("a", "in_c", [], [("ci0", 0, 256)], T.ci0[:, m, 0:128], T.cand[:, 256 * m:256 * m + 128])
    for m in range(2):
        dma("s", "in_d", [], [("ci0", 256, 512)], T.ci0[:, m, 128:256], T.cand[:, 256 * m + 128:256 * m + 256])
    dma("s", "own_t", [], [("ldt", q, q + 1)], T.ldt[q], T.th[:])
    dma("s", "own_p", [], [("xi", 3 * R, 4 * R)], T.xi[mine, 3 * R:4 * R], T.px[mine, :])
    dma("s", "xc0", [], [("xn", XH, XH + R)], T.xn[mine, XH:XH + R], T.px[mine, :])
    dma("s", "in_w", [], [("cw", 0, 512)], T.cw[:], T.cand[:, 512:1024])

    def ap(b):
        return T[b[0]][:, b[1]:b[2]] if len(b) == 3 else T[b[0]][:, b[1]:b[2]:b[3]]

    def z(k, a, b):
        return ("pp", 2048 + 512 * k + a, 2048 + 512 * k + b)

    def val(x):
        return ap(x) if isinstance(x, tuple) else x

    def aps(*xs):
        return [x for x in xs if isinstance(x, tuple)]

    def ts(out, in0, s1, s2, o0, o1=None):
        if o1 is None:
            op("v", aps(in0, s1), [out], lambda e: e.tensor_scalar(ap(out), ap(in0), val(s1), None, o0))
        else:
            op("v", aps(in0, s1, s2), [out], lambda e: e.tensor_scalar(ap(out), ap(in0), val(s1), val(s2), o0, o1))

    def tt(out, in0, in1, o):
        op("v", [in0, in1], [out], lambda e: e.tensor_tensor(ap(out), ap(in0), ap(in1), o))

    def copy(out, in_):
        op("v", [in_], [out], lambda e: e.tensor_copy(ap(out), ap(in_)))

    def scan(out, d0, d1):
        op("v", [d0, d1], [out], lambda e: e.tensor_tensor_scan(ap(out), ap(d0), ap(d1), 0.0, A.add, A.mult))

    def act(out, in_, scale=1.0, bias=0.0, func=AF.Identity):
        op("a", aps(in_, bias), [out], lambda e: e.activation(ap(out), ap(in_), func, bias=val(bias), scale=scale))

    def gather(qn, out, win, lst, bias=0.0):
        if qn == "a":
            op("a", [win, lst], [out],
               lambda e: e.activation(ap(out), ap(win).indirect(ap(lst)), AF.Identity, bias=bias, scale=1.0))
        else:
            op("v", [win, lst], [out], lambda e: e.tensor_scalar(ap(out), ap(win).indirect(ap(lst)), bias, None, A.add))

    def tt_gather(out, win, lst, in1, o):
        op("v", [win, lst, in1], [out], lambda e: e.tensor_tensor(ap(out), ap(win).indirect(ap(lst)), ap(in1), o))

    def mms(out, rd, pairs):
        n = len(pairs)
        ops("t", rd, [out], [lambda e, k=k, l=l, r=r: e.matmul(ap(out), l, r, k == 0, k == n - 1)
                             for k, (l, r) in enumerate(pairs)])

    def weave(*chains):
        for k in range(max(len(c) for c in chains)):
            for c in chains:
                if k < len(c):
                    c[k]()

    def skip():
        pass

    c16, k255, hcol, c3r, c5 = (("pf", k, k + 1) for k in range(5))

    def iota(out, pattern, base, view=None):
        view = ap(out) if view is None else view
        op("g", [], [out], lambda e: e.iota(view, pattern, base, 0, allow_small_or_imprecise_dtypes=True))

    def select(out, in_, pattern, base, step=1, how=A.is_equal, rows=128):
        op("g", [in_], [out], lambda e: e.affine_select(T[out[0]][0:rows, out[1]:out[2]], T[in_[0]][0:rows, in_[1]:in_[2]],
                                                        pattern, how, 0.0, base, step))

    def carving():
        iota(("kp", 0, 128), [[0, 128]], 4096)
        for k in range(4):
            select(("lm", 128 * k, 128 * k + 128), ("kp" if k > 1 else "km", 0, 128), [[0, 8], [-1, 8], [1000, 2]],
                   -1000 * (k % 2), rows=8)
        iota(("pre", 15, 16), [[0, 1]], 0)
        iota(("c96", 0, 512), [[0, 512]], CAP)

    def strides():
        for k in (0, 4, 5):
            iota(("u6", 0, 480), [[0, 80]], k // 4, T.u6[:, :, k])
        iota(("hx0", 0, 480), [[0, 480]], -R)
        for k in (0, 5):
            iota(("hv", k, 480, 6), [[0, 80]], 0)
        iota(("hx1", 0, 480), [[0, 480]], 320)
        iota(("t1", 0, 80), [[0, 4], [16, 20]], 0)
        iota(("t2", 0, 80), [[-320, 4], [48, 20]], 0)

    def origins():
        act(("hx0", 4, 480, 6), ("cio", 0, 80), scale=16.0, bias=c3r)
        act(("hx1", 4, 480, 6), ("t1", 0, 80), bias=c16)
        act(("hx0", 5, 480, 6), ("t2", 0, 80), bias=c5)

    op("g", [], [("mi", 0, 1)], lambda e: e.iota(T.mi[:, 0:1], [[0, 1]], 0, 1))
    iota(("cio", 0, 256), [[1, 256]], 0)
    iota(("km", 0, 144), [[0, 144]], -4096)
    iota(("cio", 3840, V), [[1, 256]], 3840)
    send("t", T.stt[:])
    send("p")
    select(("wd", 0, 144), ("km", 0, 144), [[-16, 9], [1000, 16]], 16)
    select(("ni", 0, 128), ("km", 0, 128), [[-1, 128]], 0)
    op("v", [], [("one", 0, 128)], lambda e: e.memset(T.one[:], 1.0))
    ts(("mi", 1, 2), ("mi", 0, 1), 15, None, A.bitwise_and)
    ts(("cio", 256, 512), ("cio", 0, 256), 256.0, None, A.add)
    act(("cio", 512, 768), ("cio", 0, 256), bias=512.0)
    copy(c16, ("mi", 1, 2))
    ts(k255, c16, -1.0, 255.0, A.mult, A.add)
    for at in range(768, 3840, 512):
        if at < 2304:
            act(("cio", at, at + 512), ("cio", 0, 512), bias=float(at))
        else:
            ts(("cio", at, at + 512), ("cio", 0, 512), float(at), None, A.add)

    def extract(out, w, base, extra):
        n = out[2] - out[1]
        tr = [(T[w][:, 16 - i:144 - i], T.wg[:, base + i:base + 16 * n:16]) for i in range(16)]
        mms(out, [(w, 0, 144), ("wg", base, base + 16 * n), (extra[0], 0, 128), extra[1]],
            tr + [(T[extra[0]][:], ap(extra[1]))])

    def prepare():
        li, bf, big = ("li", 0, 240), ("bf", 0, 240), 1.5 * 2 ** 31
        act(bf, li, bias=-127.5)
        act(bf, bf, bias=big)
        act(bf, bf, scale=-1.0, bias=big)
        plus(1, li, bf)
        act(("pw", 0, 240), bf, scale=math.log(2.0) / 256, func=AF.Exp)
        act(("p2", 0, 240), bf, scale=-math.log(2.0) / 256, bias=-13 * math.log(2.0), func=AF.Exp)

    def plus(k, x, y):
        mms(("pp", 512 * k, 512 * k + 240), [("eye", 0, 128), x, y], [(T.eye[:], ap(x)), (T.eye[:], ap(y))])

    def slot(t, s, a, b):
        if t == 0:
            return ("xi", R * (3 - s) + 16 * a, R * (3 - s) + 16 * b)
        return ("xi", 64 * a + 16 * (b - a) * s, 64 * a + 16 * (b - a) * (s + 1))

    def rest(qn, lst, a, b):
        gather(qn, ("cio", V + 16 * a, V + 16 * b), ("cio", 0, V), lst)

    def offsets(to, src, *ps):
        for p in ps:
            op("v", [(src, 128 * p, 128 * p + 128)], [(to, 128 * p, 128 * p + 128)],
               lambda e: e.tensor_copy(T[to][:, 128 * p:128 * p + 128], T[src][:, :, 64 * p:64 * p + 64]))

    def see(t, qn, p, *ks):
        for k in ks:
            c = 128 * p + 32 * k
            gather(qn, ("wg", 16 * c, 16 * c + 512), ("cio", V, V + R), ("wn" if t else "cu0", c, c + 32),
                   -(1024 * p + 512 * (k % 2) + 255.0))

    def seen(p):
        extract(z(p, 0, 128), "wd", 2048 * p, ("ni", ("nv", 0, 128)))

    def lists(t, p):
        tm, ci = ("tm", 128 * p, 128 * p + 128), ("ci%d" % t, 128 * p, 128 * p + 128)
        return [lambda: op("v", [z(p, 0, 128), ci], [tm],
                           lambda e: e.tensor_tensor(ap(tm), ap(z(p, 0, 128)), T[ci[0]][:, :, 64 * p:64 * p + 64], A.max)),
                lambda: ts(("off", tm[1], tm[2]), tm, float(R), None, A.min)]

    def ship(p, qn):
        hand(qn, "o%d" % p, "get_", "off", "of0", 128 * p, 128 * p + 128)
        send("o%d" % p)

    def start(t):
        return ("xn", XB, XB + R) if t else slot(0, 0, 0, 80)

    def window(t, b):
        name, at = start(t)[:2] if b == "lo" else ("xn", XH)
        return (name, at, at + R + 8)

    def first(t, b, *ps, es=(0, 2), qn="a"):
        for p in ps:
            gather(qn, (b, 1024 * p + 512 * es[0], 1024 * p + 512 * es[1]), window(t, b),
                   ("off" if t else "of0", 128 * p + 32 * es[0], 128 * p + 32 * es[1]))

    def second(t, b, *ps, move=True):
        for p in ps:
            blk = (b, 1024 * p, 1024 * p + 1024)
            tt_gather(blk, window(t, b), ("off" if t else "of0", 128 * p + 64, 128 * p + 128), blk,
                      A.min if b == "lo" else A.max)
            if move:
                abreast(t, b, p)

    def abreast(t, b, *ps):
        to = "b" + b[0]
        for p in ps:
            for a in range(8):
                dma("s", "r%s%d" % (b[0], t), [(b, 1024 * p, 1024 * p + 1024)], [(to, 512 * a, 512 * a + 512)],
                    T[to][32 * p:32 * p + 32, 512 * a:512 * a + 512], T[b][grp(a), 1024 * p:1024 * p + 1024])

    def bank(b, k):
        at = 512 * k + (2048 if b == "bh" else 0)
        return ("pp", at, at + 512)

    def lift(b, *ks):
        for k in ks:
            act(bank(b, k), (b, 512 * k, 512 * k + 512))

    def fold(b, o, last):
        s1, s2, s3 = (("s1", 512 * k, 512 * k + 512) for k in range(3))
        to = [s1, bank(b, 1), s2, bank(b, 3)]
        return ([lambda k=k: tt(to[k], bank(b, k), (b, 2048 + 512 * k, 2560 + 512 * k), o) for k in range(4)]
                + [lambda: tt(s3, to[1], s1, o), lambda: tt(to[3], to[3], s2, o), lambda: tt(last, to[3], s3, o)])

    def spread(t):
        act(("fb", 0, 512), ("lof", 0, 512), scale=-0.25, bias=-0.375)
        for a in range(8):
            for p in range(4):
                dma("s", "fg%d" % t, [("fb", 0, 512)], [("et", 1024 * p, 1024 * p + 1024)],
                    T.et[grp(a), 1024 * p:1024 * p + 1024], T.fb[32 * p:32 * p + 32, :])

    def count():
        tt(("far", 0, 512), ("pp", 0, 512), ("lt", 0, 512), A.is_gt)
        ops("t", [("bt", 0, 8), ("far", 0, 512)], [z(0, 0, 512)],
            [lambda e: e.matmul(T.pp[0:8, 2048:2560], T.bt[:], T.far[:], True, True)])

    def odd():
        op("v", [z(0, 0, 512)], [("odd", 0, 512)],
           lambda e: e.tensor_scalar(T.odd[0:8, :], T.pp[0:8, 2048:2560], float(NEED), None, A.is_ge))

    def running():
        op("v", [("odd", 0, 512), ("c96", 0, 512)], [("pre", 16, 528)],
           lambda e: e.tensor_tensor_scan(T.pre[0:8, 16:528], T.odd[0:8, :], T.c96[0:8, :], 0.0, A.add, A.min))
        mms(z(2, 0, 256), [("lm", 0, 512), ("pre", 0, 528)],
            [(T.lm[0:8, 128 * k:128 * k + 128], T.pre[0:8, 16 - k // 2 + 256 * (k % 2):272 - k // 2 + 256 * (k % 2)])
             for k in range(4)])
        act(("ft", 0, 256), z(2, 0, 256), scale=-2.0 ** -12, bias=hcol)

    def middle(t, spare):
        spare = list(spare) + [skip] * 7
        lift("bl", 0, 1, 2, 3)
        if t == 0:
            places()
        else:
            act(("x5", 0, R), start(1), scale=1.25)
        weave(fold("bl", A.min, ("lof", 0, 512)), [skip] * 5 + spare[:2])
        if t == 0:
            plus(2, ("rf", 80, 320), ("rn", 0, 240))
        lift("bh", 0, 1)
        spread(t)
        lift("bh", 2, 3)
        act(("lt", 0, 512), ("lof", 0, 512), bias=("thf", 0, 1))
        prepare()
        if t == 0:
            moves()
        weave(fold("bh", A.max, ("pp", 0, 512)) + [count, odd, running],
              [skip] * 5 + spare[2:4] + [lambda: copy(("uu", 0, 240), ("pp", 512, 752))] + spare[4:6])

    def step(t, s, a, b):
        y, x, at = slot(t, s + 1, a, b), ("x5", 16 * a, 16 * b), 80 * s + (0 if t else 512)
        return [lambda: tt_gather(y, ("et", 0, V), ("lq1" if t else "wn", at + a, at + b), x, A.add),
                lambda qn="v": ts(x, y, 1.25, None, A.mult) if qn == "v" else act(x, y, scale=1.25)][:2 - s // 2]

    def flags(word, *parts):
        for qn, a, b in parts:
            gather(qn, ("wg", 48 * a, 48 * b), ("ft", 0, 256), ("uu", 3 * a, 3 * b))
        a, b = parts[0][1], parts[-1][2]
        extract(word, "wf", 48 * a, ("ni", ("p2", 3 * a, 3 * b)))

    def tests(word, a, b):
        six = (6 * a, 6 * b)
        return [lambda: op("v", [word, ("pw", 3 * a, 3 * b)], [("u6", *six)],
                           lambda e: e.tensor_tensor(T.u6[:, a:b, 1:4], ap(word), T.pw[:, 3 * a:3 * b], A.mult)),
                lambda: op("v", [("u6", *six)], [("e6", *six)],
                           lambda e: e.tensor_scalar(ap(("e6", *six)), T.u6[:, a:b, :], 1, None, A.bitwise_and))]

    def horner(to, lst, d0, a, b):
        return [lambda: scan((to, 6 * a, 6 * b), (d0, 6 * a, 6 * b), ("e6", 6 * a, 6 * b)),
                lambda: copy((lst, a, b), (to, 6 * a + 4, 6 * b, 6))]

    def pick(t, a, b, qn="v"):
        out, win = (("cio", V + 16 * a, V + 16 * b), ("xi", 64 * a, 64 * b)) if t else (start(1), ("xi", 0, 4 * R))
        if qn == "v":
            return op("v", [win, ("so", a, b)], [out],
                      lambda e: e.tensor_scalar(ap(out), ap(win).indirect(T.so[:, a:b]), 0.0, float(TOP), A.max, A.min))
        op("a", [win, ("so", a, b)], [out],
           lambda e: e.activation(ap(out), ap(win).indirect(T.so[:, a:b]), AF.Relu, bias=float(TOP), scale=-1.0))
        act(out, out, scale=-1.0, bias=float(TOP), func=AF.Relu)

    copy(("wq", 512, 592), ("rh", 0, 80))
    for b, at, c in (("xi", 4 * R, D), ("xn", XH + R, -1), ("xn", XB + R, D)):
        iota((b, at, at + 8), [[0, 8]], c)
    select(("mv", 0, 128), ("one", 0, 128), [[-32, 4], [-1, 16], [-16, 2]], 0)
    select(("eye", 0, 128), ("one", 0, 128), [[-1, 128]], 0)
    select(("bo", 0, 128), ("km", 0, 128), [[-2, 4], [0, 16], [-1, 2]], 0, rows=8)
    for k in range(4):
        act(("nv", 32 * k, 32 * k + 32), ("cio", 0, 32), scale=-16.0, bias=k255)
    offsets("cu0", "ci0", 0)
    rest("a", ("wq", 512, 552), 0, 40)
    rest("v", ("wq", 552, 592), 40, 80)
    offsets("cu0", "ci0", 1)
    see(0, "a", 0, 0, 1)
    see(0, "v", 0, 2, 3)
    seen(0)
    offsets("cu0", "ci0", 2, 3)
    see(0, "a", 1, 0, 1)
    see(0, "v", 1, 2, 3)
    seen(1)
    weave(lists(0, 0), [lambda: copy(("wq", 592, 832), ("rh", 80, 320))])
    ship(0, "s")
    fetch("s", "p", "xi", slice(3 * R, 4 * R), True)
    fetch("s", "p", "xn", slice(XH, XH + R), s="xc0")
    see(0, "a", 2, 0, 1, 2)
    see(0, "v", 2, 3)
    seen(2)
    see(0, "v", 3, 2)
    weave(lists(0, 1))
    ship(1, "s")
    see(0, "a", 3, 0, 1)
    see(0, "v", 3, 3)
    seen(3)
    ops("t", [("bo", 0, 128), ("ni", 0, 128)], [("pp", 0, 8)],
        [lambda e: e.matmul(T.pp[:, 0:8], T.bo[0:8, :], T.ni[0:8, 0:8], True, True)])
    weave(lists(0, 2))
    ship(2, "a")
    fetch("s", "o0", "of0", slice(0, 128))
    weave(lists(0, 3))
    ship(3, "s")
    fetch("s", "o1", "of0", slice(128, 256))
    dma("s", "get_t", [("ldt", 0, 8)], [("thi", 0, 1)], T.thi[:], T.ldt[:, mine, :])
    hand("s", "r", "own_", "wq", "wn", 512, 832)
    send("r")
    carving()
    strides()
    fetch("s", "o2", "of0", slice(256, 384))
    first(0, "lo", 0, es=(0, 1))
    first(0, "lo", 0, es=(1, 2), qn="v")
    first(0, "hi", 0)
    first(0, "lo", 1, 2)
    second(0, "lo", 0)
    fetch("s", "o3", "of0", slice(384, 512))
    first(0, "hi", 1)
    first(0, "lo", 3)
    first(0, "hi", 2, 3)
    second(0, "hi", 0)
    second(0, "lo", 1, 2)
    fetch("s", "r", "wn", slice(512, 832))
    second(0, "hi", 1, move=False)
    second(0, "lo", 3)
    abreast(0, "hi", 1)
    second(0, "hi", 2, 3)
    copy(("rf", 0, 320), ("wn", 512, 832))
    act(("bt", 0, 8), ("pp", 0, 8), scale=2.0 ** -24)
    for k in range(2):
        act(("thn", k, k + 1), ("thi", 0, 1))
    mms(z(3, 0, 2), [("mv", 0, 128), ("thn", 0, 2)], [(T.mv[:], T.thn[:])])
    act(("x5", 0, R), start(0), scale=1.25)
    l0, l1, l2 = (("li", 2 - s, 240, 3) for s in range(3))
    d0, d1, d2 = (("hv", 3 - s, 480, 6) for s in range(3))

    def places():
        act(("thf", 0, 2), z(3, 0, 2))
        act(l0, ("rf", 0, 80))
        act(("rn", 0, 240), ("rf", 0, 240), scale=-1.0)
        act(l1, ("rf", 80, 160))
        act(("hv", 4, 480, 6), ("rf", 0, 80))
        act(l2, ("rf", 160, 240))
        act(hcol, c16, scale=-1.0, bias=0.5, func=AF.Relu)
        act(c3r, c16, bias=3.0 * R)
        act(c5, c16, scale=3.0, bias=-3.0 * R)

    def moves():
        act(("pb", 0, 1), c16, scale=math.log(2.0), func=AF.Exp)
        act(d0, ("pp", 1024, 1104))
        act(("wf", 0, 144), ("cio", 0, 144), scale=0.0, bias=("pb", 0, 1))
        select(("wf", 0, 144), ("wf", 0, 144), [[-16, 9], [-1000, 16]], 16, how=A.is_ge)
        select(("wf", 0, 144), ("wf", 0, 144), [[16, 9], [0, 16]], -1, step=-1, how=A.is_ge)
        act(d1, ("pp", 1104, 1184))
        act(d2, ("pp", 1184, 1264))

    halves = ((0, 40), (40, 80))
    steps0 = [[step(0, s, a, b) for a, b in halves] for s in range(3)]
    middle(0, [skip, lambda: offsets("wq", "cw", 0), skip, skip, skip, lambda: offsets("wq", "cw", 1, 2, 3)])
    hand("s", "w", "own_", "wq", "wn", 0, 512)
    stage("s", "v", T.cand, slice(512, 1024))
    dma("s", "own_v", [], [("ci1", 0, 512)], T.ci1[mine], T.cand[mine, 512:1024])
    send("w")
    send("v")
    fetch("s", "w", "wn", slice(0, 512))
    fetch("s", "v", "ci1", slice(0, 512))

    flags(z(0, 0, 120), ("a", 0, 20), ("v", 20, 40))
    flags(z(1, 0, 120), ("a", 40, 72), ("v", 72, 80))
    origins()
    steps0[0][0][0]()
    weave(tests(z(0, 0, 120), 0, 40) + horner("hs", "lq1", "hv", 0, 40), [skip, skip, steps0[0][0][1]])
    rest("a", ("lq1", 0, 40), 0, 40)
    weave(tests(z(1, 0, 120), 40, 80) + horner("hs", "lq1", "hv", 40, 80))
    rest("a", ("lq1", 40, 60), 40, 60)
    rest("v", ("lq1", 60, 80), 60, 80)

    for p in range(3):
        see(1, "a", p, 0, 1, 2, 3)
        seen(p)
    weave(steps0[0][1], steps0[1][0][:1])
    weave(horner("hc", "so", "hx0", 0, 80), steps0[1][1], steps0[1][0][1:])
    weave(*steps0[2], lists(1, 0)[:1])
    weave(lists(1, 0)[1:], [lambda: pick(0, 0, 80)])
    dma("s", "xc1", [start(1)], [("xn", XH, XH + R)], T.xn[:, XH:XH + R], ap(start(1)))
    for a, b in zip(CUT, CUT[1:]):
        dma("s", "xq", [start(1)], [slot(1, 0, a, b)], ap(slot(1, 0, a, b)), T.xn[:, XB + 16 * a:XB + 16 * b])
    see(1, "a", 3, 0, 1, 2)
    weave(lists(1, 1), [lambda: see(1, "v", 3, 3), lambda: first(1, "lo", 0, qn="v")])
    seen(3)
    first(1, "lo", 1)
    weave(lists(1, 2), [lambda: second(1, "lo", 0)])
    first(1, "lo", 2)
    first(1, "hi", 0)
    weave(lists(1, 3), [lambda: second(1, "lo", 1)])
    first(1, "lo", 3)
    first(1, "hi", 1, 2, 3)
    second(1, "lo", 2)
    second(1, "hi", 0)
    second(1, "lo", 3)
    second(1, "hi", 1, 2, 3)
    act(l0, ("hs", 4, 480, 6))
    act(("hx1", 5, 480, 6), ("hc", 5, 480, 6), scale=-0.25)
    e0, e1, t1, t2 = ("e6", 3, 480, 6), ("e6", 2, 480, 6), ("t1", 0, 80), ("t2", 0, 80)
    weave([lambda: tt(t1, e1, d2, A.mult), lambda: tt(t1, t1, d1, A.add)],
          [lambda: tt(t2, e0, d2, A.mult), lambda: tt(l2, l2, t2, A.add)])
    later = [lambda: tt(t1, t1, e0, A.mult), lambda: tt(l1, l1, t1, A.add), skip, skip,
             lambda: (copy(("lq1", 160, 240), l2), copy(("lq1", 80, 160), l1))]

    def word(h):
        return z(h, 0, 3 * (CUT[h + 1] - CUT[h]))

    def last_flags(h):
        flags(word(h), ("a", CUT[h], CUT[h + 1]))

    def settle(h):
        return tests(word(h), CUT[h], CUT[h + 1]) + horner("hs", "so", "hx1", CUT[h], CUT[h + 1])

    def steps(s, h):
        return step(1, s, CUT[h], CUT[h + 1])

    def leave(h, qn="v"):
        a, b, c = CUT[h], CUT[h + 1], "y%d" % h
        pick(1, a, b, qn)
        stage("s", c, T.cio, slice(V + 16 * a, V + 16 * b), [("cio", V + 16 * a, V + 16 * b)])
        send(c)

    middle(1, later)
    last_flags(0)
    last_flags(1)
    flags(z(2, 0, 120), ("a", 40, 80))
    G = [[steps(s, h)[0] for h in range(PIECES)] for s in range(3)]
    M = [[steps(s, h)[1] for h in range(PIECES)] for s in range(2)]
    weave([G[0][0], M[0][0], G[1][0], M[1][0], G[2][0]], [G[0][1], M[0][1], G[1][1], M[1][1]])
    weave(settle(0), [G[2][1], G[0][2], G[0][3], M[0][2]])
    leave(0)
    weave(settle(1), [M[0][3], G[1][2], G[1][3]])
    M[1][2]("a")
    M[1][3]("a")
    leave(1, "a")
    weave(tests(z(2, 0, 120), 40, 80) + horner("hs", "so", "hx1", 40, 80), [skip, G[2][2], G[2][3]])
    act(("cn", 0, 80), ("hs", 5, 480, 6), scale=-1 / 320, bias=3.0, func=AF.Relu)
    act(("cn", 0, 80), ("cn", 0, 80), scale=-1.0, bias=3.0)
    dma("a", "stg_c", [("cn", 0, 80)], [("stc", 0, 8)], T.stc[:], T.cn[:])
    leave(2)
    leave(3)
    send("c")

    dma("s", "own_y0", [("cio", V, V + R)], [], T.yx[mine, :], T.cio[mine, V:V + R])
    dma("a", "own_c", [("cn", 0, 80)], [], T.yc[mine, :], T.cn[mine, :])
    for h in range(PIECES):
        fetch("s", "y%d" % h, "yx", slice(16 * CUT[h], 16 * CUT[h + 1]))
    fetch("a", "c", "yc", slice(0, 80))
    for s in total:
        need("g", s, total[s])
